import numpy as np, ml_dtypes
CORES = [16,18,20,22]
N = 4
BF = ml_dtypes.bfloat16
W, A, L, S, Q, C = 4096, 4, 3, 6, 80, 48
def place(x, wv, kv):
    u = np.sum(wv * x, axis=2) & (W - 1)
    return (((u * u) >> 5)[..., None] + kv[:, :, None, :] * u[..., None]) & (W - 1)
def search(X, q, wv, kv):
    n, m = q.shape[0], q.shape[3]
    pl = place(q, wv, kv); ok = np.ones(pl.shape, bool); line = [pl]; levels, dist = [], []
    for l in range(L):
        k = A ** (l + 1)
        occ = np.take_along_axis(X, pl.reshape(n, 8, 1, m * k), 3)
        d = np.sum(np.abs(occ.reshape(n, 8, 16, m, k) - q[..., None]), axis=2)
        if l == 0: hit = np.any(d == 0, axis=3)
        levels.append(pl); dist.append(np.where(ok, d, -1))
        if l < L - 1:
            good = ok & (occ[:, :, 0].reshape(n, 8, m, k) != 512)
            pl = place(occ, wv, kv).reshape(n, 8, m, k * A)
            line = [np.repeat(a, A, axis=3) for a in line]
            ok = np.repeat(good, A, axis=3)
            for a in line: ok = ok & (pl != a)
            line.append(pl)
    D = np.concatenate(dist, axis=3); v = D.shape[3] - 1 - np.argmax(D[..., ::-1], axis=3)
    path = np.full((n, 8, m, L), -1, np.int64); depth = np.zeros((n, 8, m), np.int64); base = 0
    for l in range(L):
        k = A ** (l + 1); here = (v >= base) & (v < base + k); j = np.clip(v - base, 0, k - 1)
        for h in range(l + 1):
            t = np.take_along_axis(levels[h], (j // A ** (l - h))[..., None], 3)[..., 0]
            path[..., h] = np.where(here, t, path[..., h])
        depth = np.where(here, l, depth); base += k
    return (q[:, :, 0] != 512) & ~hit, depth, path
def step(X, q, wv, kv):
    n, m = q.shape[0], q.shape[3]
    live, depth, path = search(X, q, wv, kv)
    meet = np.zeros((n, 8, m, m), bool)
    for a in range(L):
        for b in range(L):
            meet |= (path[..., a][..., :, None] == path[..., b][..., None, :]) & (path[..., a] >= 0)[..., None]
    go = live & ~np.any(meet & live[:, :, None, :] & np.tri(m, m, -1, dtype=bool), axis=3)
    old = [np.take_along_axis(X, np.maximum(path[..., l], 0)[:, :, None, :], 3) for l in range(L)]
    Y = X.copy(); val = q; vic = old[0]
    for l in range(L):
        r, g, i = np.nonzero(go & (depth >= l))
        Y[r, g, :, path[r, g, i, l]] = val[r, g, :, i]; val = old[l]
        vic = np.where((depth >= l)[:, :, None, :], old[l], vic)
    gone = go & (vic[:, :, 0] != 512); slot = np.add.accumulate(gone.astype(np.int64), axis=2) - 1
    out = np.full((n, 8, 16, C), 512, np.int32); r, g, i = np.nonzero(gone & (slot < C))
    out[r, g, :, slot[r, g, i]] = vic[r, g, :, i]
    return Y, out
def records(rng, k): return rng.integers(0, 256, (N, 8, 16, k)).astype(np.int32)
def hashes(rng): return rng.integers(1, 256, (N, 8, 16, 1)).astype(np.int32), 2 * rng.integers(0, 1024, (N, 8, A)) + 1
def fill(rng, rec, wv, kv, full, bare):
    pl = place(rec, wv, kv); k = rec.shape[3]; X = np.full((N, 8, 16, W), 512, np.int32)
    for r in range(N):
        for g in range(8):
            own = np.full(W, -1); free = np.arange(k)
            for a in range(A):
                p = pl[r, g, free, a]; e = own[p] < 0; own[p[e]] = free[e]; free = free[own[p] != free]
            if full[r, g]: own = np.where(own < 0, rng.integers(0, k, W), own)
            own = np.where(rng.random(W) < bare[r, g], -1, own)
            X[r, g] = np.where(own >= 0, rec[r, g][:, own], 512)
    return X
def ask(rng, X, fresh):
    c = rng.integers(0, W, (N, 8, 1, S * Q)); v = np.take_along_axis(X, c, 3).reshape(N, 8, 16, S, Q)
    q = np.where((rng.random((N, 8, 1, S, Q)) < 0.2) & (v[:, :, :1] != 512), v, fresh.reshape(N, 8, 16, S, Q))
    j = np.where(rng.random((N, 8, 1, S, Q)) < 0.06, rng.integers(0, Q, (N, 8, 1, S, Q)), np.arange(Q))
    return np.take_along_axis(q, j, 4)
def pack(X, q, wv, kv):
    return {"x0": X.reshape(N, 128, W).astype(np.float32).astype(BF), "qs": np.ascontiguousarray(q).reshape(N, 128, S * Q).astype(np.float32).astype(BF),
            "wt": wv.reshape(N, 128, 1).astype(np.float32).astype(BF), "kk": np.repeat(kv, 16, axis=1).astype(np.int32)}
def setup_inputs(rng):
    wv, kv = hashes(rng); full = rng.random((N, 8)) < 0.5; bare = rng.choice(np.array([0.0, 0.002, 0.005, 0.02, 0.1]), (N, 8))
    full[:, 0] = True; bare[:, 0] = 0.0; bare[:, 1] = 0.005; bare[:, 2] = 0.02
    X = fill(rng, records(rng, 2 * W), wv, kv, full, bare)
    return pack(X, ask(rng, X, records(rng, S * Q)), wv, kv)
def setup_inputs_room(rng):
    wv, kv = hashes(rng); X = fill(rng, records(rng, 2 * W), wv, kv, np.ones((N, 8), bool), np.zeros((N, 8)))
    q = ask(rng, X, records(rng, S * Q)); pool = records(rng, 2 * Q); live, depth, path = search(X, pool, wv, kv)
    home = np.any(place(X, wv, kv) == np.arange(W)[:, None], axis=3)
    for r in range(N):
        for g in range(8):
            n = int(rng.choice(np.array([0, 1, C - 1, C, C + 1, Q])))
            if r == 0: n = (C, C + 1, Q, C - 1, 1, 0, C, Q)[g]
            used, take = set(), []
            for i in rng.permutation(2 * Q):
                p = set(path[r, g, i].tolist()) - {-1}
                if len(take) < n and live[r, g, i] and not (p & used):
                    take.append(int(i)); used |= p
            stay = rng.choice(np.nonzero(home[r, g])[0], Q - len(take))
            q[r, g, :, 0] = np.concatenate([pool[r, g][:, np.array(take, np.int64)], X[r, g][:, stay]], axis=1)[:, rng.permutation(Q)]
    return pack(X, q, wv, kv)
def setup_inputs_alike(rng):
    wv, kv = hashes(rng); wv[:] = wv[:1].copy(); kv[:, 2] = kv[:, 2, :1]; kv[:, 3, 1:] = kv[:, 3, 1:2]; kv[:] = kv[:1].copy()
    rec = (255 * rng.integers(0, 2, (N, 8, 16, 2 * W))).astype(np.int32); fresh = (255 * rng.integers(0, 2, (N, 8, 16, S * Q))).astype(np.int32)
    few = rng.integers(0, 256, (16, 24)).astype(np.int32)
    for g in (1, 5):
        for r in range(N):
            rec[r, g] = few[:, rng.integers(0, 24, 2 * W)]
            fresh[r, g] = np.where(rng.random(S * Q) < 0.5, few[:, rng.integers(0, 24, S * Q)], rng.integers(0, 256, (16, S * Q)))
    rec[:, 6, :, ::4] = 0
    rec[:, 7] = rng.integers(0, 3, (N, 16, 2 * W))
    full = rng.random((N, 8)) < 0.7; full[:, 1] = True; bare = rng.choice(np.array([0.0, 0.005, 0.02]), (N, 8))
    X = fill(rng, rec, wv, kv, full, bare); q = ask(rng, X, fresh)
    q[:, 4, :, 1] = q[:, 4, :, 1, :1]; q[:, 6, :, 2, ::5] = 0; q[:, 6, :, 0, Q - 1] = 255
    return pack(X, q, wv, kv)
def setup_inputs_hollow(rng):
    wv, kv = hashes(rng); bare = rng.choice(np.array([0.3, 0.6, 0.9, 0.97, 1.0]), (N, 8)); bare[0, 0] = 1.0; bare[1, 1] = 0.6
    full = rng.random((N, 8)) < 0.5; bare[:, 6:] = 0.0; full[:, 7] = True
    X = fill(rng, records(rng, 2 * W), wv, kv, full, bare); q = ask(rng, X, records(rng, S * Q))
    q[:, :, :, 2] = q[:, :, :, 1][..., rng.permutation(Q)]
    return pack(X, q, wv, kv)
def setup_inputs_edges(rng):
    wv, kv = hashes(rng); wv[:, 0] = 255; kv[:, :2] = rng.choice(np.array([1, 2046, 2047]), (N, 2, A)); kv[:, :2, 0] = 2047
    wv[:, 6, 0] |= 1; kv[:, 6] = kv[:, 6, :1].copy()
    full = rng.random((N, 8)) < 0.5; full[:, 0] = True; full[:, 4] = False; full[::2, 5] = True; full[1::2, 5] = False; full[:, 6] = False
    bare = np.zeros((N, 8)); bare[:, 3] = 0.3; bare[:, 7] = 0.1
    rec, fresh = records(rng, 2 * W), records(rng, S * Q)
    for v in (rec, fresh):
        k = v.shape[3]; v[:, 0] = np.where(rng.random((N, 1, k)) < 0.5, rng.integers(200, 256, (N, 16, k)), v[:, 0])
        v[::2, 5] = v[::2, 5] >> 2
    X = fill(rng, rec, wv, kv, full, bare); q = ask(rng, X, fresh)
    q[:, 0, :, 0, 0] = 255
    q[:, 1:3, :, 0, :8] = records(rng, 8)[:, 1:3]
    t = q[:, :, :, 0, :8].copy(); pl = place(t, wv, kv)[..., 0]; i = rng.integers(0, 16, (N, 8, 1, 8))
    near = np.where(np.arange(16)[:, None] == i, t + np.where(t < 255, 1, -1), t)
    for r in range(N):
        for g in (1, 2):
            for j in range(7, -1, -1): X[r, g, :, pl[r, g, j]] = near[r, g, :, j]
    X[:, 3] = np.where(rng.random((N, 1, W)) < 0.02, 0, X[:, 3]); X[:, 3, :, 0] = 512
    q[:, 3, :, 0, 0] = 0; q[:, 3, :, 1, 0] = 255
    X[:, 7, :, 0] = records(rng, 1)[:, 7, :, 0]; q[:, 7, :, 0, 0] = 0; pe = place(X[..., :1], wv, kv)[:, 7, 0]
    for r in range(N): X[r, 7, :, pe[r]] = 512
    for r in range(N):
        g = 4 + r % 2; c = rng.choice(np.nonzero(X[r, g, 0] != 512)[0], Q); q[r, g, :, 0] = X[r, g][:, c]
    q[1::2, 4, :, 0, 0] = records(rng, 1)[1::2, 4, :, 0]; q[1::2, 4, :, 1] = q[1::2, 4, :, 0, :1]
    rr = np.arange(8) % N; m = 256; pool = rng.integers(128, 256, (1, 8, 16, m)).astype(np.int32)
    live, depth, path = search(X[rr, 5][None], pool, wv[rr, 5][None], kv[rr, 5][None])
    for r in range(1, N, 2):
        p = path[0, r]; same = np.sum((p[:, None, :, None] == p[None, :, None, :]) & (p >= 0)[:, None, :, None], axis=(2, 3))
        fit = (same == 1) & live[0, r][:, None] & (live[0, r] & (depth[0, r] == L - 1))[None, :]
        a, b = divmod(int(np.argmax(fit)), m); z = pool[0, r][:, b:b + 1]
        q[r, 5, :, 1] = z; q[r, 5, :, 1, 0] = pool[0, r, :, a]
        X[r - 1, 5] = np.where(rng.random(W) < 0.125, z, X[r - 1, 5])
    mine = place(rec, wv, kv)[:, 6, :, 0]
    for r in range(1, N, 2):
        e = r - 1; p = mine[e]; i = np.nonzero(np.any(X[e, 6][:, p] != rec[e, 6], axis=0))[0]
        i = i[np.unique(p[i], return_index=True)[1]]
        t = place(X[e, 6][:, p[i]][None, None], wv[r:r + 1, 6:7], kv[r:r + 1, 6:7])[0, 0, :, 0]
        j = rng.permutation(np.unique(t, return_index=True)[1]); last = j[X[r, 6, 0, t[j]] != 512][:1]
        j = j[j != last[0]][:Q - 1]; j = np.concatenate([j[:C - 1], last, j[C - 1:]])
        q[e, 6] = rec[e, 6][:, i[j]][:, None, :]
        z = X[r, 6, :, int(t[last[0]])].copy()
        X[r, 6, :, t[j[:C]]] = 512
        c = rng.choice(np.nonzero(X[r, 6, 0] != 512)[0], S * Q); q[r, 6] = X[r, 6][:, c].reshape(16, S, Q); q[r, 6, :, 1, 0] = z
    return pack(X, q, wv, kv)
def setup_inputs_spread(rng):
    def uneven(k):
        v = np.minimum((np.exp2(2 + 6 * rng.random((N, 8, 1, k))) * rng.random((N, 8, 16, k))).astype(np.int32), 255)
        return np.where(rng.random((N, 8, 16, k)) < 0.02, 255, v).astype(np.int32)
    wv = np.minimum(np.exp2(8 * rng.random((N, 8, 16, 1))).astype(np.int32), 255); kv = np.minimum(np.exp2(11 * rng.random((N, 8, A))).astype(np.int64), 2047)
    X = fill(rng, uneven(2 * W), wv, kv, rng.random((N, 8)) < 0.6, rng.choice(np.array([0.0, 0.003, 0.01]), (N, 8)))
    return pack(X, ask(rng, X, uneven(S * Q)), wv, kv)
def check_inputs(d):
    bad = []
    v = np.asarray(d["x0"]).astype(np.float32); e = v == 512
    if not np.all(e | ((v >= 0) & (v <= 255) & (np.floor(v) == v))): bad.append("range of x0")
    e = e.reshape(N, 8, 16, W)
    if np.any(np.any(e, axis=2) != np.all(e, axis=2)): bad.append("empty records of x0")
    for k, lo in (("qs", 0), ("wt", 1)):
        v = np.asarray(d[k]).astype(np.float32)
        if not np.all((v >= lo) & (v <= 255) & (np.floor(v) == v)): bad.append("range of " + k)
    k = np.asarray(d["kk"])
    if np.min(k) < 1 or np.max(k) > 2047: bad.append("range of kk")
    k = k.reshape(N, 8, 16, A)
    if np.any(k != k[:, :, :1]): bad.append("rows of kk")
    return bad
def reference(x0, qs, wt, kk):
    X = x0.astype(np.float32).astype(np.int32).reshape(N, 8, 16, W); q = qs.astype(np.float32).astype(np.int32).reshape(N, 8, 16, S, Q)
    wv = wt.astype(np.float32).astype(np.int32).reshape(N, 8, 16, 1); kv = kk.reshape(N, 8, 16, A)[:, :, 0].astype(np.int64)
    come = np.full((N, 8, 16, C), 512, np.int32)
    for s in range(S):
        X, out = step(X, np.concatenate([q[:, :, :, s], come], axis=3), wv, kv)
        come = np.roll(out, 1, axis=0)
    return {"y": X.reshape(N, 128, W).astype(np.float32).astype(BF)}

@@ -1,0 +1,530 @@
+from concourse.mybir import AluOpType as A, AxisListType, ActivationFunctionType as F
+
+S, C = 6, 48
+NH = {"D": 5, "A": 3}
+OFF = {"D": 0, "A": 5}
+QC = {"D": 4096, "A": 4256}
+DUMPX, XW = 4352, 4736
+BIG = 1 << 21
+THR = 4090.0 * 128
+CM = 12582912.0
+ZETA = {"D": (1, 3), "A": (1,)}
+LBA = {"D": (1, 3, 5, 7), "A": (1, 3)}
+DVC = {"D": (), "A": (1, 2)}
+SB, PS = "sbuf", "psum"
+CB = ("ID", "NID", "NEG", "BN", "BLK", "TRS", "TRL")
+CF = ("PERM", "SCL", "NIF")
+
+
+def _scratch():
+    b, f, i4, u2 = "bfloat16", "float32", "int32", "uint16"
+    d = {"X": ([XW], b), "QS": ([480], b), "QXD": ([6 * 1280], b), "QXA": ([768], b), "WT": ([1], b), "KI": ([4], i4), "KF": ([4], f),
+         "WL": ([2048], b), "OL": ([2048], b), "CB": ([7 * 128], b), "CF": ([3 * 128], f), "TRR": ([48], b), "HALF": ([240], f),
+         "MASK": ([240], f), "RST": ([240], f), "CR": ([240], f), "CG": ([128], f), "CP": ([128], f), "PI": ([4], i4), "PF": ([4], f),
+         "GM": ([8], f), "DUMP": ([24], f), "RT": ([8], f), "SD": ([16], f), "GP": ([16], b), "FE": ([384], b), "LB": ([3072], b),
+         "SND": ([256], b), "JK": ([2048], b), "RM": ([12], f), "ARR": ([5 * C], b), "r1D": ([24, 20], i4), "r1A": ([4, 12], i4),
+         "RG": ([512], b), "s16": ([8], u2)}
+    for h in "DA":
+        n = NH[h]
+        for l, m in ((1, 6 if h == "D" else 1), (2, 4), (3, 16)):
+            d["u%s%d" % (h, l)] = ([m, n], i4)
+            d["q%s%d" % (h, l)] = ([m, n], i4)
+            d["p%s%d" % (h, l)] = ([m, 4 * n], i4)
+            d["l%s%d" % (h, l)] = ([m * 4 * n], u2)
+        for nm, sh, ty in (("PL", [128 * n], i4), ("e21", [4, 4 * n], b), ("v1r", [4, 4 * n], b), ("v1", [4 * n], b), ("v2", [16 * n], b),
+                           ("v2r", [16, 4 * n], b), ("e32", [16, 4 * n], b), ("e31", [16, 4 * n], b), ("d1", [64 * n], b), ("b1", [64 * n], b),
+                           ("d2", [256 * n], b), ("b2", [256 * n], b), ("d3", [3 * 256 * n], b), ("cd", [84 * n], b), ("lv", [8 * n], f),
+                           ("MI", [n], i4), ("cc", [3 * n], i4), ("co", [3 * n], i4), ("hi", [3 * n], i4), ("o16", [3 * n], u2),
+                           ("gm", [48 * n], f), ("sc", [48 * n], f), ("yt", [48 * n], f), ("rl", [4 * n], u2), ("dp", [3 * n], f),
+                           ("nc", [3 * n], f), ("wm", [3 * n], f), ("w16", [3 * n], u2), ("res", [3 * n], f)):
+            d[nm + h] = (sh, ty)
+    o = {k: (SB, [128] + sh, ty) for k, (sh, ty) in d.items()}
+    for k in ("UD", "UA", "KD", "KA", "B4", "Z0", "Z1", "Z2"):
+        o[k] = (PS, [128, 512], f)
+    return o
+
+
+SCRATCH = _scratch()
+BANKS = [k for k in SCRATCH if SCRATCH[k][0] == PS]
+SEMAPHORES = ["cV", "cA", "cP", "cG"] + ["m%d" % i for i in range(50)] + ["arr%d" % i for i in range(1, S)] + ["snt%d" % i for i in range(1, S)]
+CYC, PCYC, WAKE = 0.00104, 0.0006, 0.1
+ORDER = {}
+
+
+def _dur(q, kind, n):
+    if q == "P":
+        return n * PCYC
+    if kind == "g":
+        return 0.06 + 1.5 * n * CYC
+    if kind == "s":
+        return 0.06 + 3.5 * n * CYC
+    return max(64, n) * CYC + (0.06 if q == "A" else 0.0)
+
+
+def rank_program(g, core, T, topo):
+    rank = T.rank_of(core)
+    if rank is None:
+        return
+    v, ac, pe = g.vector, g.scalar, g.tensor
+    mc = {nm: T.CB[:, 128 * i:128 * i + 128] for i, nm in enumerate(CB)}
+    for i, nm in enumerate(CF):
+        mc[nm] = T.CF[:, 128 * i:128 * i + 128]
+    ops = []
+
+    def rng(xs):
+        return [x if len(x) == 3 else (x[0], 0, 1 << 20) for x in xs]
+
+    def op(q, fn, rd, wr, dur, own=None):
+        ops.append((q, fn, rng(rd), rng(wr), dur, own))
+
+    def V(fn, rd, wr, n=64, kind="v"):
+        op("V", fn, rd, wr, _dur("V", kind, n))
+
+    def AC(fn, rd, wr, n=64, kind="v"):
+        op("A", fn, rd, wr, _dur("A", kind, n))
+
+    def P(fns, rd, wr, n):
+        def run():
+            i = None
+            for f in fns:
+                i = f()
+            return i
+        op("P", run, rd, wr, _dur("P", "p", n))
+
+    nsem = [0]
+
+    def DMA(q, fns, rd, wr, dur):
+        name = "m%d" % nsem[0]
+        nsem[0] += 1
+
+        def run():
+            for f in fns:
+                f().then_inc(T.sem[name], 16)
+        op(q, run, rd, wr, dur, (name, 16 * len(fns)))
+
+    def mm(out, l, r, a, b):
+        return lambda: pe.matmul(out, l, r, a, b)
+
+    def ts(o, i, s1, o1, s2=None, o2=None):
+        if o2 is None:
+            return lambda: v.tensor_scalar(o, i, s1, None, o1)
+        return lambda: v.tensor_scalar(o, i, s1, s2, o1, o2)
+
+    def tt(o, a, b, f):
+        return lambda: v.tensor_tensor(out=o, in0=a, in1=b, op=f)
+
+    def cp(o, i):
+        return lambda: v.tensor_copy(o, i)
+
+    def ms(o, c):
+        return lambda: v.memset(o, c)
+
+    def act(o, i, f, **k):
+        return lambda: ac.activation(o, i, f, **k)
+
+    def red(o, i):
+        return lambda: v.tensor_reduce(o, i, AxisListType.X, A.max)
+
+    def iota(o, pat, base, wr, n):
+        op("G", lambda: g.iota(o, pat, base, 0, allow_small_or_imprecise_dtypes=True), [], [wr], 0.13 + 2 * n * CYC)
+
+    def sd(o, i):
+        return lambda: g.sync.dma_start(o, i)
+
+    def W16(t, r):
+        return t[:, r * 128:r * 128 + 128]
+
+    DMA("S", [sd(T.QS[:, :], T.qs[:, :]), sd(T.WT[:, :], T.wt[:, :]), sd(T.KI[:, :], T.kk[:, :])], [], [("QS",), ("WT",), ("KI",)], 2.5)
+    DMA("AD", [lambda: ac.dma_start(T.X[:, 0:4096], T.x0[:, :])], [], [("X", 0, 4096), ("X0D",)], 6.0)
+    op("G", lambda: g.iota(T.PI[:, 0:1], [[0, 1]], 0, 1), [], [("PI", 0, 1)], 0.2)
+    iota(T.CG[:, :], [[1, 8], [0, 16]], 0, ("CG",), 128)
+    iota(T.CR[:, :], [[0, 15], [1, 16]], 0, ("CR",), 240)
+    iota(T.CP[:, :], [[1, 128]], 0, ("CP",), 128)
+    V(ts(T.PI[:, 1:2], T.PI[:, 0:1], 4, A.arith_shift_right), [("PI", 0, 1)], [("PI", 1, 2)])
+    V(ts(T.PI[:, 2:3], T.PI[:, 0:1], 15, A.bitwise_and), [("PI", 0, 1)], [("PI", 2, 3)])
+    V(cp(T.PF[:, 0:3], T.PI[:, 0:3]), [("PI", 0, 3)], [("PF",)])
+    pcol, gcol, rcol = T.PF[:, 0:1], T.PF[:, 1:2], T.PF[:, 2:3]
+    V(ts(mc["BLK"], T.CG[:, :], gcol, A.is_equal), [("CG",), ("PF",)], [("BLK",)], 128)
+    V(ms(T.WL[:, :], 0.0), [], [("WL",)], 1024)
+    V(ms(T.OL[:, :], 0.0), [], [("OL",)], 1024)
+    for nm, s1, k in (("WL", T.WT[:, 0:1], ("WT",)), ("OL", 128.0, ("BLK",))):
+        for r in range(16):
+            V(ts(T[nm][:, r * 128 + r:r * 128 + 128:16], T.CB[:, 512:640:16], s1, A.mult), [("BLK",), k] + ([(nm,)] if r == 0 else []), [(nm, r * 128, r * 128 + 128)])
+    V(cp(T.KF[:, :], T.KI[:, :]), [("KI",)], [("KF",)])
+    V(ts(mc["ID"], T.CP[:, :], pcol, A.is_equal), [("CP",), ("PF",)], [("ID",)], 128)
+    for nm, c, n in (("NEG", -float(BIG), 64), ("NID", -1.0, 64), ("BN", float(BIG), 64), ("NIF", -1.0, 128)):
+        V(ts(mc[nm], mc["ID"], c, A.mult), [("ID",)], [(nm,)], n)
+    V(ts(T.MASK[:, :], T.CR[:, :], rcol, A.is_equal), [("CR",), ("PF",)], [("MASK",)], 240)
+    V(ts(T.RST[:, :], T.CR[:, :], 0.0, A.is_gt), [("CR",)], [("RST",)], 240)
+    V(ts(mc["TRS"], T.CR[:, 0:128], rcol, A.is_gt), [("CR",), ("PF",)], [("TRS",)], 128)
+    V(tt(mc["TRS"], mc["TRS"], mc["BLK"], A.mult), [("TRS",), ("BLK",)], [("TRS",)], 256)
+    V(ts(T.TRR[:, :], T.CR[:, 0:48], pcol, A.is_ge, -64.0, A.mult), [("CR",), ("PF",)], [("TRR",)])
+    V(ts(T.HALF[:, :], T.CR[:, :], 0.0, A.mult), [("CR",)], [("HALF",)], 240)
+    V(ts(T.RM[:, 11:12], rcol, 0.0, A.is_equal, 0.5, A.mult), [("PF",)], [("RM", 11, 12)])
+    V(ts(T.HALF[:, :], T.HALF[:, :], T.RM[:, 11:12], A.add), [("HALF",), ("RM", 11, 12)], [("HALF",)], 240)
+    for f in range(16):
+        V(ms(T.CF[:, 128 + f:256:16], 2.0 ** -(f + 1) if f < 13 else 0.0), [], [("SCL", f, f + 1)])
+    V(tt(mc["SCL"], mc["SCL"], mc["BLK"], A.mult), [("SCL",), ("BLK",)], [("SCL",)], 256)
+    iota(T.CG[:, :], [[1, 16], [0, 8]], 0, ("CG",), 128)
+    iota(T.CP[:, :], [[1, 8], [8, 16]], 0, ("CP",), 128)
+    V(ts(mc["TRL"], T.CG[:, :], pcol, A.is_equal), [("CG",), ("PF",)], [("TRL",)], 128)
+    V(ts(mc["PERM"], T.CP[:, :], pcol, A.is_equal), [("CP",), ("PF",)], [("PERM",)], 128)
+    iota(T.GM[:, :], [[1, 8]], 0, ("GM",), 8)
+    V(ts(T.GM[:, :], T.GM[:, :], gcol, A.is_equal), [("GM",), ("PF",)], [("GM",)])
+    iota(T.DUMP[:, :], [[16, 24]], DUMPX, ("DUMP",), 24)
+    V(ts(T.DUMP[:, :], T.DUMP[:, :], rcol, A.add), [("DUMP",), ("PF",)], [("DUMP",)])
+    iota(T.RT[:, :], [[16, 8]], 0, ("RT",), 8)
+    V(ts(T.RT[:, :], T.RT[:, :], rcol, A.add), [("RT",), ("PF",)], [("RT",)])
+    V(ts(T.SD[:, 0:8], T.RT[:, :], 128.0, A.add), [("RT",)], [("SD", 0, 8)])
+    V(ms(T.GP[:, :], 0.0), [], [("GP",)])
+    V(ms(T.SND[:, :], 512.0), [], [("SND",)])
+    V(ms(T.X[:, 4096:XW], 0.0), [], [("X", 4096, XW)], 320)
+    for h in "DA":
+        n, o = NH[h], OFF[h]
+        for a, b, c in ((0, 4, 4), (4, 20, 16), (20, 84, 64)):
+            iota(T["cd" + h][:, a * n:b * n], [[1, b - a], [0, n]], c, ("cd" + h, a * n, b * n), (b - a) * n)
+        op("G", (lambda h=h, n=n: g.iota(T["hi" + h][:, :], [[1, n], [0, 3]], 0, 0)), [], [("hi" + h,)], 0.2)
+        V(ms(T["PL" + h][:, :], 0), [], [("PL" + h,)], 128 * n)
+        for c in range(2):
+            V(ts(T["PL" + h][:, c * n:c * n + n], T.RT[:, o:o + n], QC[h] - 16.0 * o + 16 * n * (1 - c), A.add), [("RT",)], [("PL" + h, c * n, c * n + n)])
+        k0 = 0 if h == "D" else n
+        V(ts(T["rl" + h][:, k0 + 2:k0 + 3 * n:3], T.RT[:, o:o + n], QC[h] - 16.0 * o, A.add), [("RT",)], [("rl" + h, 2, 3)])
+        V(ms(T["res" + h][:, :], 0.0), [], [("res" + h,)])
+
+    def chain(h, l, m, c0):
+        n, k = NH[h], "%s%d" % (h, l)
+        U, u, sq, p = T["U" + h], T["u" + k], T["q" + k], T["p" + k]
+        w = m * n
+        ru, rq, rp = ("u" + k,), ("q" + k,), ("p" + k,)
+        V(cp(u[:, :, :], U[:, c0:c0 + w]), [("U" + h, c0, c0 + w)], [ru], w)
+        V(ts(u[:, :, :], u[:, :, :], 4095, A.bitwise_and), [ru], [ru], w)
+        V(tt(sq[:, :, :], u[:, :, :], u[:, :, :], A.mult), [ru], [rq], 2 * w)
+        for a in range(4):
+            V(ts(p[:, :, a * n:a * n + n], u[:, :, :], T.KF[:, a:a + 1], A.mult), [ru, ("KF",)], [("p" + k, a, a + 1)], w)
+        V(ts(sq[:, :, :], sq[:, :, :], 5, A.arith_shift_right), [rq], [rq], w)
+        for a in range(4):
+            pa = p[:, :, a * n:a * n + n]
+            V(tt(pa, pa, sq[:, :, :], A.add), [rq, ("p" + k, a, a + 1)], [("p" + k, a, a + 1)], 2 * w)
+        V(ts(p[:, :, :], p[:, :, :], 4095, A.bitwise_and), [rp], [rp], 4 * w)
+        V(cp(T["l" + k][:, :], p[:, :, :]), [rp], [("l" + k,)], 4 * w)
+
+    def gath(h, l, lc0, oname, o0, QX, qn, q0, w):
+        V(tt(T[oname][:, o0:o0 + 16 * w], T.X[:, 0:4096].indirect(T["l%s%d" % (h, l)][:, lc0:lc0 + w]), QX[:, q0:q0 + 16 * w], A.subtract),
+          [("X", 0, 4096), ("l%s%d" % (h, l),), (qn, q0, q0 + 16 * w)], [(oname, o0, o0 + 16 * w)], 16 * w, "g")
+
+    def sums(o, L, b, b0, w, a, z):
+        return [mm(o, W16(T[L], r), b[:, b0 + r:b0 + 16 * w:16], a and r == 0, z and r == 15) for r in range(16)]
+
+    def keys(h, bname, b0, c0, w, pen, k0=None, code=True, lhs="NEG"):
+        k0 = c0 if k0 is None else k0
+        o = T["K" + h][:, k0:k0 + w]
+        f = sums(o, "OL", T[bname], b0, w, True, False)
+        if code:
+            f.append(mm(o, mc["ID"], T["cd" + h][:, c0:c0 + w], False, not pen))
+        for i, (e, _) in enumerate(pen):
+            f.append(mm(o, mc[lhs], e, False, i == len(pen) - 1))
+        P(f, [(bname, b0, b0 + 16 * w), ("OL",), ("ID",), (lhs,), ("cd" + h,)] + [x for _, x in pen], [("K" + h, k0, k0 + w)], len(f) * max(64, w))
+
+    zb, jb = [0], [0]
+
+    def bank():
+        zb[0] += 1
+        return "Z%d" % (zb[0] % 3)
+
+    def search(h, s):
+        n = NH[h]
+        QX, qn, q0 = (T.QXD, "QXD", s * 1280) if h == "D" else (T.QXA, "QXA", 0)
+        U, K, PL, lv = T["U" + h], T["K" + h], T["PL" + h], T["lv" + h]
+        un, ln, d3, dn, p2, p3 = "U" + h, "lv" + h, T["d3" + h], "d3" + h, "p%s2" % h, "p%s3" % h
+        if h == "A":
+            R, rn = T.ARR[:, s * C - C:s * C], "ARR%d" % s
+            AC(act(QX[:, 0:48], R, F.Copy), [(rn,)], [(qn, 0, 48)])
+            AC(act(QX[:, 48:96], R, F.Copy), [(rn,)], [(qn, 48, 96)])
+            w = 96
+            while w < 768:
+                AC(act(QX[:, w:2 * w], QX[:, 0:w], F.Copy), [(qn, 0, w)], [(qn, w, 2 * w)], w)
+                w *= 2
+            AC(act(T.X[:, QC[h]:QC[h] + 48], R, F.Copy), [(rn,)], [("X", QC[h], QC[h] + 48)])
+            P(sums(U[:, 0:n], "WL", T.ARR, s * C - C, n, True, True) + sums(U[:, n:2 * n], "OL", T.ARR, s * C - C, n, True, True),
+              [(rn,), ("WL",), ("OL",)], [(un, 0, 2 * n)], 32 * 64)
+            chain("A", 1, 1, 0)
+            V(ts(lv[:, 6 * n:7 * n], U[:, n:2 * n], THR, A.is_lt), [(un, n, 2 * n)], [(ln, 6 * n, 7 * n)])
+            p1, p1r, l0 = T.pA1[:, 0, :], ("pA1",), 0
+        else:
+            AC(act(T.X[:, QC[h]:QC[h] + 80], T.QS[:, s * 80:s * 80 + 80], F.Copy), [("QS",)], [("X", QC[h], QC[h] + 80)], 80)
+            p1, p1r, l0 = T.pD1[:, s, :], ("pD1",), s * 20
+        for l, w, c0, lc in ((1, 4 * n, 32, l0), (2, 16 * n, 64, 0)):
+            dd, c1 = "d%d%s" % (l, h), max(64, w) * 16
+            P(sums(U[:, c0:c0 + w], "WL", QX, q0, w, True, False), [(qn, q0, q0 + 16 * w), ("WL",)], [(un, c0, c0 + w)], c1)
+            gath(h, l, lc, dd, 0, QX, qn, q0, w)
+            P(sums(U[:, c0:c0 + w], "WL", T[dd], 0, w, False, True), [(dd,), ("WL",), (un, c0, c0 + w)], [(un, c0, c0 + w)], c1)
+            chain(h, l + 1, 4 ** l, c0)
+            AC(act(T["b%d%s" % (l, h)][:, :], T[dd][:, :], F.Abs), [(dd,)], [("b%d%s" % (l, h),)], 16 * w)
+        keys(h, "b1" + h, 0, 0, 4 * n, [])
+        k1 = ("K" + h, 0, 4 * n)
+        V(ts(T["v1" + h][:, :], K[:, 0:4 * n], THR, A.is_gt), [k1], [("v1" + h,)])
+        V(ts(lv[:, 0:4 * n], K[:, 0:4 * n], 128.0, A.is_ge), [k1], [(ln, 0, 4 * n)])
+        V(tt(lv[:, 4 * n:6 * n], lv[:, 0:2 * n], lv[:, 2 * n:4 * n], A.mult), [(ln, 0, 4 * n)], [(ln, 4 * n, 6 * n)])
+        V(tt(lv[:, 7 * n:8 * n], lv[:, 4 * n:5 * n], lv[:, 5 * n:6 * n], A.mult), [(ln, 4 * n, 6 * n)], [(ln, 7 * n, 8 * n)])
+        if h == "A":
+            V(tt(lv[:, 7 * n:8 * n], lv[:, 7 * n:8 * n], lv[:, 6 * n:7 * n], A.mult), [(ln, 6 * n, 8 * n)], [(ln, 7 * n, 8 * n)])
+        for a in range(4):
+            AC(act(T["v1r" + h][:, :, a * n:a * n + n], T["v1" + h][:, :], F.Copy), [("v1" + h,)], [("v1r" + h, a, a + 1)])
+        r1n = "r1A" if h == "A" else "r1D%d" % s
+        r1 = T.r1A[:, :, :] if h == "A" else T.r1D[:, 4 * s:4 * s + 4, :]
+        if h == "A":
+            for a in range(4):
+                V(cp(T.r1A[:, :, a * n:a * n + n], p1), [p1r], [("r1A", a, a + 1)])
+        up1, up2 = U[:, 288:288 + 16 * n], U[:, 192:192 + 16 * n]
+        V(cp(up1, r1), [(r1n,)], [(un, 288, 288 + 16 * n)], 16 * n)
+        V(tt(T["e21" + h][:, :, :], T[p2][:, :, :], up1, A.is_equal), [(p2,), (un, 288, 288 + 16 * n)], [("e21" + h,)], 16 * n)
+        pen = [(T["e21" + h][:, :, :], ("e21" + h,)), (T["v1r" + h][:, :, :], ("v1r" + h,))]
+        keys(h, "b2" + h, 0, 4 * n, 16 * n, pen)
+        keys(h, "b2" + h, 0, 4 * n, 16 * n, pen, 84 * n, False, "BN")
+        V(ts(T["v2" + h][:, :], K[:, 84 * n:100 * n], THR, A.is_gt), [("K" + h, 84 * n, 100 * n)], [("v2" + h,)], 16 * n)
+        for a in range(4):
+            AC(act(T["v2r" + h][:, :, a * n:a * n + n], T["v2" + h][:, :], F.Copy), [("v2" + h,)], [("v2r" + h, a, a + 1)], 16 * n)
+        V(cp(up2, T[p2][:, :, :]), [(p2,)], [(un, 192, 192 + 16 * n)], 16 * n)
+        for a in range(4):
+            blk = T[p3][:, :, a * n:a * n + n]
+            V(tt(T["e32" + h][:, :, a * n:a * n + n], blk, up2, A.is_equal), [(p3,), (un, 192, 192 + 16 * n)], [("e32" + h, a, a + 1)], 16 * n)
+            V(tt(T["e31" + h][:, :, a * n:a * n + n], blk, up1, A.is_equal), [(p3,), (un, 288, 288 + 16 * n)], [("e31" + h, a, a + 1)], 16 * n)
+        DMA("S", [sd(PL[:, 4 * n:8 * n], p1), sd(PL[:, 16 * n:32 * n], T[p2][:, :, :]), sd(PL[:, 64 * n:128 * n], T[p3][:, :, :])],
+            [p1r, (p2,), (p3,)], [("PL" + h, 4 * n, 8 * n), ("PL" + h, 16 * n, 32 * n), ("PL" + h, 64 * n, 128 * n)], 2.2)
+        W, l3 = 256 * n, "l%s3" % h
+        for c in range(4):
+            b0 = (c % 3) * W
+            if c in ZETA[h]:
+                AC(act(d3[:, b0:b0 + W], T.X[:, 0:4096].indirect(T[l3][:, c * 16 * n:c * 16 * n + 16 * n]), F.Copy), [("X", 0, 4096), (l3,)], [(dn, b0, b0 + W)], W, "g")
+                for a in range(0, W, 512):
+                    w = min(512, W - a)
+                    Zn = bank()
+                    Z, da = T[Zn][:, 0:w], d3[:, b0 + a:b0 + a + w]
+                    P([mm(Z, mc["ID"], da, True, False), mm(Z, mc["NID"], QX[:, q0 + a:q0 + a + w], False, True)],
+                      [(dn, b0 + a, b0 + a + w), (qn, q0 + a, q0 + a + w), ("ID",), ("NID",)], [(Zn, 0, w)], 2 * w)
+                    AC(act(da, Z, F.Abs), [(Zn, 0, w)], [(dn, b0 + a, b0 + a + w)], w)
+            else:
+                gath(h, 3, c * 16 * n, dn, b0, QX, qn, q0, 16 * n)
+                AC(act(d3[:, b0:b0 + W], d3[:, b0:b0 + W], F.Abs), [(dn, b0, b0 + W)], [(dn, b0, b0 + W)], W)
+            keys(h, dn, b0, (20 + 16 * c) * n, 16 * n, [(T[e + h][:, 4 * c:4 * c + 4, :], (e + h,)) for e in ("e32", "e31", "v2r")])
+
+    def tail(h, s):
+        n, o = NH[h], OFF[h]
+        w, f0 = 48 * n, 48 * o
+        K, lv, ln, cc, co, gm, sc, yt, rl, dp = [T[x + h] for x in ("K", "lv")] + ["lv" + h] + [T[x + h] for x in ("cc", "co", "gm", "sc", "yt", "rl", "dp")]
+        M, rM, live, rlv = lv[:, n:2 * n], (ln, n, 2 * n), lv[:, 7 * n:8 * n], (ln, 7 * n, 8 * n)
+        for i in range(n):
+            V(red(lv[:, n + i:n + i + 1], K[:, i:84 * n:n]), [("K" + h, 0, 84 * n)], [(ln, n + i, n + i + 1)], 84)
+        V(tt(T["MI" + h][:, :], M, live, A.mult), [rM, rlv], [("MI" + h,)])
+        for k, (sh, ma) in enumerate(((0, 127), (2, 31), (4, 7))):
+            V(ts(cc[:, k:3 * n:3], T["MI" + h][:, :], sh, A.arith_shift_right, ma, A.bitwise_and), [("MI" + h,)], [("cc" + h, k, k + 1)])
+        V(ts(co[:, :], cc[:, :], float(n), A.mult), [("cc" + h,)], [("co" + h,)])
+        V(tt(co[:, :], co[:, :], T["hi" + h][:, :], A.add), [("co" + h,), ("hi" + h,)], [("co" + h,)])
+        V(cp(T["o16" + h][:, :], co[:, :]), [("co" + h,)], [("o16" + h,)])
+        V(tt(gm[:, :], T["PL" + h][:, :].indirect(T["o16" + h][:, :]), T.MASK[:, 0:w], A.mult), [("PL" + h,), ("o16" + h,), ("MASK",)], [("gm" + h,)], w, "g")
+        P([mm(T.B4[:, 0:w], mc["SCL"], T.HALF[:, 0:w], True, False)], [("SCL",), ("HALF",)], [("B4", 0, w)], 4 * w)
+        P([mm(T.B4[:, 0:w], mc["SCL"], gm[:, :], False, True)], [("gm" + h,), ("SCL",), ("B4", 0, w)], [("B4", 0, w)], 4 * w)
+        V(lambda: v.tensor_tensor_scan(sc[:, :], T.RST[:, 0:w], gm[:, :], 0.0, A.mult, A.add), [("RST",), ("gm" + h,)], [("sc" + h,)], w)
+        k0, v0 = (0, 3 * n) if h == "D" else (n, 0)
+        V(cp(rl[:, k0:k0 + 3 * n:3], sc[:, 31:w:48]), [("sc" + h,)], [("rl" + h, 0, 1)])
+        V(cp(rl[:, k0 + 1:k0 + 3 * n:3], sc[:, 47:w:48]), [("sc" + h,)], [("rl" + h, 1, 2)])
+        V(cp(rl[:, v0:v0 + n], sc[:, 15:w:48]), [("sc" + h,)], [("rl" + h, 3, 4)])
+        xw = QC[h] + 32 * n
+        AC(act(T.RG[:, 64 * o:64 * o + 64 * n], T.X[:, 0:xw].indirect(rl[:, 0:4 * n]), F.Copy), [("X", 0, xw), ("rl" + h,)], [("RG", 64 * o, 64 * o + 64 * n)], 64 * n, "g")
+        ry, fe, rf = ("yt" + h,), T.FE[:, f0:f0 + w], ("FE", f0, f0 + w)
+        V(ts(yt[:, :], T.B4[:, 0:w], CM, A.add, CM, A.subtract), [("B4", 0, w)], [ry], w)
+        V(tt(yt[:, :], T.B4[:, 0:w], yt[:, :], A.subtract), [("B4", 0, w), ry], [ry], w)
+        V(ts(fe, yt[:, :], 0.0, A.is_gt, 0.5, A.subtract), [ry], [rf], w)
+        for gg in range(8):
+            dst, sg = T.LB[:, f0 * 8 + gg:(f0 + w) * 8:8], T.GM[:, gg:gg + 1]
+            if gg in LBA[h]:
+                AC(act(dst, fe, F.Copy, scale=sg), [rf, ("GM",)], [("LB" + h, gg, gg + 1)], w)
+            else:
+                V(ts(dst, fe, sg, A.mult), [rf, ("GM",)], [("LB" + h, gg, gg + 1)], w // 2)
+        dmp = T.DUMP[:, 3 * o:3 * o + 3 * n]
+        V(tt(dp[:, :], sc[:, 15:w:16], dmp, A.subtract), [("sc" + h,), ("DUMP",)], [("dp" + h,)])
+        V(ts(lv[:, 0:n], M, THR, A.is_lt), [rM], [(ln, 0, n)])
+        res = T["res" + h]
+        for i in range(n):
+            gi = o + i
+            z = 48 * (gi + 1)
+            per = 3 if 3 * z <= 512 else (2 if 2 * z <= 512 else 1)
+            for slot, kk in enumerate([list(range(3))[a:a + per] for a in range(0, 3, per)]):
+                Zn = bank()
+                Z, f, t = T[Zn], [], len(kk) * z
+                for j, k in enumerate(kk):
+                    L = W16(T.LB, gi * 3 + k)
+                    c = j * z
+                    if gi:
+                        f.append(mm(Z[:, c:c + z - 48], L, T.FE[:, 0:z - 48], True, True))
+                    f.append(mm(Z[:, c + z - 48:c + z], L, T.FE[:, z - 48:z], True, False))
+                    f.append(mm(Z[:, c + z - 48:c + z], mc["TRL"], T.TRR[:, :], False, True))
+                P(f, [("FE", 0, z), ("LB" + h,), ("TRL",), ("TRR",)], [(Zn, 0, t)], len(kk) * (max(64, z - 48) + 128))
+                x = slot * n + i
+                if slot in DVC[h]:
+                    V(red(T.RM[:, x:x + 1], Z[:, 0:t]), [(Zn, 0, t)], [("RM", x, x + 1)], t)
+                else:
+                    jb[0] = (jb[0] + 512) % 2048
+                    j0 = jb[0]
+                    AC(act(T.JK[:, j0:j0 + t], Z[:, 0:t], F.Relu, bias=-7.0, scale=2.0, accum_out=res[:, x:x + 1]), [(Zn, 0, t)],
+                       [("res" + h, x, x + 1), ("JK", j0, j0 + t)], t)
+        if DVC[h]:
+            x, y = DVC[h][0] * n, DVC[h][-1] * n + n
+            V(ts(res[:, x:y], T.RM[:, x:y], 3.75, A.is_gt), [("RM", x, y)], [("res" + h, x, y)])
+        ns = 2 if h == "D" else 3
+        c0 = 256 + 16 * (h == "A")
+        o4 = T.B4[:, c0:c0 + n]
+        P([mm(o4, mc["PERM"], res[:, i * n:i * n + n], i == 0, False) for i in range(ns)] + [mm(o4, mc["NIF"], live, False, True)],
+          [("res" + h,), ("PERM",), ("NIF",), rlv], [("B4", c0, c0 + n)], ns * 256 + 256)
+        nc, wm = T["nc" + h], T["wm" + h]
+        for k in range(3):
+            V(ts(nc[:, k:3 * n:3], o4, -1.0, A.is_equal), [("B4", c0, c0 + n)], [("nc" + h, k, k + 1)])
+        V(tt(wm[:, :], dp[:, :], nc[:, :], A.mult), [("dp" + h,), ("nc" + h,)], [("wm" + h,)])
+        V(tt(wm[:, :], wm[:, :], dmp, A.add), [("wm" + h,), ("DUMP",)], [("wm" + h,)])
+        V(cp(T["w16" + h][:, :], wm[:, :]), [("wm" + h,)], [("w16" + h,)])
+        if s == S - 1:
+            return
+        g0 = 8 + o
+        V(tt(T.GP[:, g0:g0 + n], nc[:, 0:3 * n:3], lv[:, 0:n], A.mult), [("nc" + h,), (ln, 0, n)], [("GP", g0, g0 + n)])
+        if h == "D" and s:
+            return
+        m = o + n
+        gone, rg, ds, p4 = T.GP[:, 8:8 + m], ("GP", 8, 8 + m), T.SD[:, 8:8 + m], T.B4[:, 288:288 + m]
+        f = [mm(p4, mc["TRS"], gone, True, False)] + [mm(p4, mc["BLK"], T.GP[:, 8 - x:8 - x + m], False, x == m - 1) for x in range(1, m)]
+        P(f, [("GP", 0, 8 + m), ("TRS",), ("BLK",)], [("B4", 288, 288 + m)], 64 * m)
+        V(tt(ds, p4, T.SD[:, 0:m], A.subtract), [("B4", 288, 288 + m), ("SD", 0, 8)], [("ds",)])
+        V(tt(ds, ds, gone, A.mult), [("ds",), rg], [("ds",)])
+        V(tt(ds, ds, T.SD[:, 0:m], A.add), [("ds",), ("SD", 0, 8)], [("ds",)])
+        V(cp(T.s16[:, 0:m], ds), [("ds",)], [("s16",)])
+
+    P(sums(T.UD[:, 0:30], "WL", T.QS, 0, 30, True, True), [("QS",), ("WL",)], [("UD", 0, 30)], 1024)
+    chain("D", 1, 6, 0)
+    for s in range(S):
+        b, w = s * 1280, 80
+        if s == 0:
+            V(cp(T.QXD[:, 0:80], T.QS[:, 0:80]), [("QS",)], [("QXD", 0, 80)])
+        else:
+            DMA("S", [sd(T.QXD[:, b:b + 80], T.QS[:, s * 80:s * 80 + 80])], [("QS",), ("X0D",)], [("QXD", b, b + 80)], 2.0)
+        while w < 1280:
+            if s == 0:
+                V(cp(T.QXD[:, w:2 * w], T.QXD[:, 0:w]), [("QXD", 0, w)], [("QXD", w, 2 * w)], w // 2)
+            else:
+                DMA("S", [sd(T.QXD[:, b + w:b + 2 * w], T.QXD[:, b:b + w])], [("QXD", b, b + w)], [("QXD", b + w, b + 2 * w)], 2.0)
+            w *= 2
+        for a in range(4):
+            V(cp(T.r1D[:, 4 * s:4 * s + 4, a * 5:a * 5 + 5], T.pD1[:, s, :]), [("pD1",)], [("r1D%d" % s, a, a + 1)])
+    nxt = T.cores[(rank + 1) % len(T.cores)]
+    rid, pid = topo.addr(nxt)[:2]
+    msk, neng = topo.mask(core, nxt), len(topo.engines(core, nxt))
+    for s in range(S):
+        halves = "DA" if s else "D"
+        if 0 < s < S - 1:
+            V(ms(T.SND[:, 0:C], 512.0), [("snt", s, s + 1)], [("SND",)])
+        for h in halves:
+            search(h, s)
+        for h in halves:
+            tail(h, s)
+        for h in halves:
+            n, r0 = NH[h], (0 if h == "D" else 368)
+            V((lambda h=h, n=n, r0=r0: v.tensor_copy(T.X[:, :].indirect(T["w16" + h][:, :]), T.RG[:, r0:r0 + 48 * n])),
+              [("w16" + h,), ("RG", r0, r0 + 48 * n)], [("X", 0, XW)], 48 * n, "s")
+        if s < S - 1:
+            n = 8 if s else 5
+            V((lambda n=n: v.tensor_copy(T.SND[:, :].indirect(T.s16[:, 0:n]), T.RG[:, 240:240 + 16 * n])), [("s16",), ("RG", 240, 240 + 16 * n)], [("SND",)], 16 * n, "s")
+            op("G", (lambda s=s: g.remote_dma(T.ARR[:, s * C:s * C + C], T.SND[:, 0:C], T.sem["arr%d" % (s + 1)], T.sem["snt%d" % (s + 1)], pid, rid, msk)),
+               [("SND",)], [], 0.5, ("none", 0))
+            op("N", None, [("SND",)], [("ARR%d" % (s + 1),)], 2.5, ("arr%d" % (s + 1), neng))
+            op("N", None, [("SND",)], [("snt", s + 1, s + 2)], 2.5, ("snt%d" % (s + 1), neng))
+    DMA("S", [sd(T.y[:, 0:2048], T.X[:, 0:2048])], [("X", 0, 2048)], [("y1",)], 4.0)
+    DMA("AD", [lambda: ac.dma_start(T.y[:, 2048:4096], T.X[:, 2048:4096])], [("X", 2048, 4096)], [("y2",)], 4.0)
+
+    eng = {"V": v, "A": ac, "P": pe, "G": g, "S": g.sync, "AD": ac}
+    phys = {"V": "V", "A": "A", "P": "P", "G": "G", "S": "S", "AD": "A", "N": "N"}
+    N = len(ops)
+    deps = [dict() for _ in range(N)]
+    hist = {}
+    for i, (q, fn, rd, wr, du, own) in enumerate(ops):
+        for isw, lst in ((0, rd), (1, wr)):
+            for nm, lo, hi in lst:
+                bank_ = nm in BANKS
+                for j, w, a, b in hist.get(nm, ()):
+                    over, same = lo < b and a < hi, ops[j][0] == q
+                    if j != i and ((over and (isw or w)) or (bank_ and not same)):
+                        deps[i][j] = deps[i].get(j, False) or bool(over or not same)
+        for isw, lst in ((0, rd), (1, wr)):
+            for nm, lo, hi in lst:
+                hh = hist.setdefault(nm, [])
+                if isw:
+                    hh[:] = [x for x in hh if x[0] == i or not (lo <= x[2] and x[3] <= hi)]
+                hh.append((i, isw, lo, hi))
+    if "o" not in ORDER:
+        succ = [[] for _ in range(N)]
+        for i in range(N):
+            for j in deps[i]:
+                succ[j].append(i)
+        pri, left, rt, fin = [0.0] * N, [len(d) for d in deps], [0.0] * N, [0.0] * N
+        for i in range(N - 1, -1, -1):
+            pri[i] = ops[i][4] + max([pri[k] + WAKE for k in succ[i]] + [0.0])
+        ready, free, order = {}, {}, []
+        for i in range(N):
+            if not left[i]:
+                ready.setdefault(phys[ops[i][0]], []).append(i)
+        while len(order) < N:
+            best = None
+            for q, lst in ready.items():
+                if lst:
+                    f = free.get(q, 0.0) if q != "N" else 0.0
+                    t0 = min(max(f, rt[i]) for i in lst)
+                    c = max((i for i in lst if max(f, rt[i]) <= t0 + 0.03), key=lambda i: (pri[i], -i))
+                    t = max(f, rt[c])
+                    if best is None or t < best[0]:
+                        best = (t, c, q)
+            t, c, q = best
+            ready[q].remove(c)
+            order.append(c)
+            free[q] = t + (ops[c][4] if ops[c][0] not in ("S", "AD") else 0.1)
+            fin[c] = t + ops[c][4]
+            for k in succ[c]:
+                left[k] -= 1
+                rt[k] = max(rt[k], fin[c] + WAKE * (deps[k][c] is True))
+                if not left[k]:
+                    ready.setdefault(phys[ops[k][0]], []).append(k)
+        ORDER["o"] = order
+    cnt = {"V": 0, "A": 0, "P": 0, "G": 0}
+    val, snap = [None] * N, [{} for _ in range(N)]
+    know = {q: {} for q in "VAPGS"}
+    for i in ORDER["o"]:
+        q, fn, rd, wr, du, own = ops[i]
+        p = phys[q]
+        if p == "N":
+            val[i] = own
+            continue
+        kn, want = know[p], {}
+        for j, need in deps[i].items():
+            if need or p != phys[ops[j][0]]:
+                sem, c = val[j]
+                if kn.get(sem, 0) < c:
+                    want[sem] = max(want.get(sem, (0, 0)), (c, j))
+        for sem in sorted(want, key=lambda k: -want[k][1]):
+            c, j = want[sem]
+            if kn.get(sem, 0) < c:
+                eng[q].wait_ge(T.sem[sem], c)
+                for k2, c2 in snap[j].items():
+                    kn[k2] = max(kn.get(k2, 0), c2)
+                kn[sem] = c
+        r = fn()
+        if own is None:
+            cnt[p] += 1
+            r.then_inc(T.sem["c" + p], 1)
+            val[i] = ("c" + p, cnt[p])
+        else:
+            val[i] = own
+        snap[i] = dict(kn)
+    for p in "VAPG":
+        g.wait_ge(T.sem["c" + p], cnt[p])
+    for i in range(N):
+        if ops[i][0] in ("S", "AD"):
+            g.wait_ge(T.sem[val[i][0]], val[i][1])
+    for s in range(1, S):
+        g.wait_ge(T.sem["snt%d" % s], neng)
+        g.wait_ge(T.sem["arr%d" % s], neng)

@@ -1,64 +1,62 @@
+import numpy as np
 from concourse.mybir import AluOpType as A, AxisListType, ActivationFunctionType as F
 
 S, C = 6, 48
 NH = {"D": 5, "A": 3}
 OFF = {"D": 0, "A": 5}
-QC = {"D": 4096, "A": 4256}
-DUMPX, XW = 4352, 4736
-BIG = 1 << 21
-THR = 4090.0 * 128
-CM = 12582912.0
-ZETA = {"D": (1, 3), "A": (1,)}
-LBA = {"D": (1, 3, 5, 7), "A": (1, 3)}
-DVC = {"D": (), "A": (1, 2)}
+STR = {"D": 8, "A": 4}
+QC, SPARE, DUMPX, XW = 4096, 4224, 4352, 4736
+B24, B22 = float(1 << 24), float(1 << 22)
+THR = 4090.0 * 1024
+CM = 1.5 * 2.0 ** 35
+SEG = {"D": ((0, 16, "V"), (16, 32, "A"), (32, 48, "V"), (48, 64, "A")), "A": ((0, 16, "A"), (16, 32, "V"), (32, 48, "A"), (48, 64, "V"))}
+KEY = {"D": ((0, 16), (16, 32), (32, 48), (48, 64)), "A": ((0, 32), (32, 64))}
 SB, PS = "sbuf", "psum"
-CB = ("ID", "NID", "NEG", "BN", "BLK", "TRS", "TRL")
-CF = ("PERM", "SCL", "NIF")
+CYC, PCYC, WAKE, AFIX = 0.00104, 0.00055, 0.1, 0.06
 
 
-def _scratch():
+def _shapes():
     b, f, i4, u2 = "bfloat16", "float32", "int32", "uint16"
-    d = {"X": ([XW], b), "QS": ([480], b), "QXD": ([6 * 1280], b), "QXA": ([768], b), "WT": ([1], b), "KI": ([4], i4), "KF": ([4], f),
-         "WL": ([2048], b), "OL": ([2048], b), "CB": ([7 * 128], b), "CF": ([3 * 128], f), "TRR": ([48], b), "HALF": ([240], f),
-         "MASK": ([240], f), "RST": ([240], f), "CR": ([240], f), "CG": ([128], f), "CP": ([128], f), "PI": ([4], i4), "PF": ([4], f),
-         "GM": ([8], f), "DUMP": ([24], f), "RT": ([8], f), "SD": ([16], f), "GP": ([16], b), "FE": ([384], b), "LB": ([3072], b),
-         "SND": ([256], b), "JK": ([2048], b), "RM": ([12], f), "ARR": ([5 * C], b), "r1D": ([24, 20], i4), "r1A": ([4, 12], i4),
-         "RG": ([512], b), "s16": ([8], u2)}
+    d = {"X": ([XW], b), "QS": ([480], b), "QX0": ([1280], b), "QXD": ([5, 1280], b), "QXA": ([768], b), "WT": ([1], b), "KI": ([4], i4),
+         "KF": ([4, 4], f), "WL": ([144], b), "OL": ([144], b), "CI": ([144], f), "CR": ([240], f), "MASK": ([240], f), "RST": ([240], f),
+         "PI": ([8], i4), "PF": ([8], f), "PEN": ([48], b), "C2K": ([32], b), "DUMP": ([24], f), "RT": ([8], f), "SD": ([8], f),
+         "GP": ([16], b), "SND": ([256], b), "JK": ([4, 144], b), "ARR": ([5, C], b), "SP": ([3, 128], u2), "EQ": ([3, 3, 3, 128], b),
+         "UQD": ([16, 30], f), "UQA": ([16, 3], f), "p1D": ([24, 5], i4), "l1D": ([120], u2), "l1A": ([12], u2)}
+    for k in ("ID", "NID", "NEG", "BIG", "BLK", "TRS"):
+        d[k] = ([128], b)
+    for k in ("IDF", "BLKF"):
+        d[k] = ([128], f)
     for h in "DA":
         n = NH[h]
-        for l, m in ((1, 6 if h == "D" else 1), (2, 4), (3, 16)):
-            d["u%s%d" % (h, l)] = ([m, n], i4)
-            d["q%s%d" % (h, l)] = ([m, n], i4)
-            d["p%s%d" % (h, l)] = ([m, 4 * n], i4)
-            d["l%s%d" % (h, l)] = ([m * 4 * n], u2)
-        for nm, sh, ty in (("PL", [128 * n], i4), ("e21", [4, 4 * n], b), ("v1r", [4, 4 * n], b), ("v1", [4 * n], b), ("v2", [16 * n], b),
-                           ("v2r", [16, 4 * n], b), ("e32", [16, 4 * n], b), ("e31", [16, 4 * n], b), ("d1", [64 * n], b), ("b1", [64 * n], b),
-                           ("d2", [256 * n], b), ("b2", [256 * n], b), ("d3", [3 * 256 * n], b), ("cd", [84 * n], b), ("lv", [8 * n], f),
-                           ("MI", [n], i4), ("cc", [3 * n], i4), ("co", [3 * n], i4), ("hi", [3 * n], i4), ("o16", [3 * n], u2),
-                           ("gm", [48 * n], f), ("sc", [48 * n], f), ("yt", [48 * n], f), ("rl", [4 * n], u2), ("dp", [3 * n], f),
-                           ("nc", [3 * n], f), ("wm", [3 * n], f), ("w16", [3 * n], u2), ("res", [3 * n], f)):
+        for nm, sh, ty in (("PL", [128, STR[h]], i4), ("PT", [128 * STR[h]], i4), ("cR", [16 * n], f), ("cv", [16 * n], f), ("cs", [16 * n], f), ("cz", [64, n], i4),
+                           ("l2", [16 * n], u2), ("l3", [64 * n], u2), ("r1", [16, n], i4), ("e21", [16 * n], b), ("v1", [4 * n], b),
+                           ("v1r", [16, n], b), ("v2", [16 * n], b), ("v2r", [64, n], b), ("e32", [64, n], b), ("e31", [64, n], b),
+                           ("d12", [320 * n], b), ("b12", [320 * n], b), ("d3", [1024 * n], b), ("cd", [84 * n], b), ("ht", [5 * n], b),
+                           ("M", [n], f), ("MI", [n], i4), ("ne", [n], f), ("cc", [3, n], i4), ("hi", [3 * n], i4), ("o16", [3 * n], u2),
+                           ("gm", [48 * n], f), ("sc", [48 * n], f), ("rl", [3 * n], u2), ("res", [n], f), ("wm", [3, n], f),
+                           ("w16", [3 * n], u2), ("ds", [n], f), ("s16", [n], u2), ("RG", [64 * n], b)):
             d[nm + h] = (sh, ty)
-    o = {k: (SB, [128] + sh, ty) for k, (sh, ty) in d.items()}
-    for k in ("UD", "UA", "KD", "KA", "B4", "Z0", "Z1", "Z2"):
-        o[k] = (PS, [128, 512], f)
-    return o
+    return d
 
 
-SCRATCH = _scratch()
-BANKS = [k for k in SCRATCH if SCRATCH[k][0] == PS]
-SEMAPHORES = ["cV", "cA", "cP", "cG"] + ["m%d" % i for i in range(50)] + ["arr%d" % i for i in range(1, S)] + ["snt%d" % i for i in range(1, S)]
-CYC, PCYC, WAKE = 0.00104, 0.0006, 0.1
+SHAPES = _shapes()
+BANKS = ("UD", "UA", "KD", "KA", "B4", "B5", "Z0", "Z1")
+SCRATCH = {k: (SB, [128] + sh, ty) for k, (sh, ty) in SHAPES.items()}
+for _k in BANKS:
+    SCRATCH[_k] = (PS, [128, 512], "float32")
+    SHAPES[_k] = ([512], "float32")
+SEMAPHORES = ["cV", "cA", "cP", "cG"] + ["m%d" % i for i in range(32)] + ["arr%d" % i for i in range(1, S)] + ["snt%d" % i for i in range(1, S)]
 ORDER = {}
+BITS = {}
 
 
-def _dur(q, kind, n):
-    if q == "P":
-        return n * PCYC
-    if kind == "g":
-        return 0.06 + 1.5 * n * CYC
-    if kind == "s":
-        return 0.06 + 3.5 * n * CYC
-    return max(64, n) * CYC + (0.06 if q == "A" else 0.0)
+def _bits(name, idx):
+    key = (name, repr(idx))
+    if key not in BITS:
+        m = np.zeros(SHAPES[name][0], bool)
+        m[idx] = True
+        BITS[key] = (int.from_bytes(np.packbits(m.ravel()).tobytes(), "big"), int(m.sum()))
+    return BITS[key]
 
 
 def rank_program(g, core, T, topo):
@@ -66,398 +64,359 @@ def rank_program(g, core, T, topo):
     if rank is None:
         return
     v, ac, pe = g.vector, g.scalar, g.tensor
-    mc = {nm: T.CB[:, 128 * i:128 * i + 128] for i, nm in enumerate(CB)}
-    for i, nm in enumerate(CF):
-        mc[nm] = T.CF[:, 128 * i:128 * i + 128]
     ops = []
+    sl = slice
 
-    def rng(xs):
-        return [x if len(x) == 3 else (x[0], 0, 1 << 20) for x in xs]
+    def R(name, *idx):
+        idx = tuple(sl(*x) if isinstance(x, tuple) else x for x in idx) or (sl(None),) * len(SHAPES[name][0])
+        b, n = _bits(name, idx)
+        return (T[name][(sl(None),) + idx], name, b, n)
+
+    def tok(name):
+        return (None, name, 1, 0)
 
     def op(q, fn, rd, wr, dur, own=None):
-        ops.append((q, fn, rng(rd), rng(wr), dur, own))
+        ops.append((q, fn, [(x[1], x[2]) for x in rd if isinstance(x, tuple)], [(x[1], x[2]) for x in wr], dur, own))
 
-    def V(fn, rd, wr, n=64, kind="v"):
-        op("V", fn, rd, wr, _dur("V", kind, n))
+    def two(*xs):
+        return all(SHAPES[x[1]][1] in ("bfloat16", "uint16") for x in xs)
 
-    def AC(fn, rd, wr, n=64, kind="v"):
-        op("A", fn, rd, wr, _dur("A", kind, n))
+    def val_(x):
+        return x[0] if isinstance(x, tuple) else x
 
-    def P(fns, rd, wr, n):
+    def ts(o, i, s1, o1, s2=None, o2=None):
+        a = (o[0], i[0], val_(s1), val_(s2), o1) + (() if o2 is None else (o2,))
+        op("V", lambda: v.tensor_scalar(*a), [i, s1, s2], [o], max(64, i[3] / (2 if two(o, i) else 1)) * CYC)
+
+    def tt(o, a, b, f):
+        c = 1 if a[1] in BANKS or b[1] in BANKS else 2
+        op("V", lambda: v.tensor_tensor(out=o[0], in0=a[0], in1=b[0], op=f), [a, b], [o], max(64, c * a[3]) * CYC)
+
+    def cp(o, i):
+        op("V", lambda: v.tensor_copy(o[0], i[0]), [i], [o], max(64, i[3] / (2 if two(o, i) else 1)) * CYC)
+
+    def ms(o, c):
+        op("V", lambda: v.memset(o[0], c), [], [o], max(64, o[3] / (2 if two(o) else 1)) * CYC)
+
+    def red(o, i):
+        op("V", lambda: v.tensor_reduce(o[0], i[0], AxisListType.X, A.max), [i], [o], max(64, i[3]) * CYC)
+
+    def act(o, i, f, **k):
+        a = {x: val_(y) for x, y in k.items()}
+        acc = [k["accum_out"]] if "accum_out" in k else []
+        op("A", lambda: ac.activation(o[0], i[0], f, **a), [i, k.get("bias"), k.get("scale")], [o] + acc, max(64, i[3]) * CYC + AFIX + 0.02 * len(acc))
+
+    def gat(o, win, off, q=None, f=A.subtract):
+        if q is None:
+            op("A", lambda: ac.activation(o[0], win[0].indirect(off[0]), F.Copy), [win, off], [o], 0.065 + 1.56 * o[3] * CYC)
+        else:
+            op("V", lambda: v.tensor_tensor(out=o[0], in0=win[0].indirect(off[0]), in1=q[0], op=f), [win, off, q], [o], 0.05 + 1.56 * o[3] * CYC)
+
+    def scat(win, off, i):
+        op("V", lambda: v.tensor_copy(win[0].indirect(off[0]), i[0]), [off, i], [win], 0.05 + 3.8 * i[3] * CYC)
+
+    def gcp(o, i):
+        op("G", lambda: g.affine_select(o[0], i[0], [[0, i[3]]], A.is_gt, 0.0, 1, 0), [i], [o], 0.17 + 2 * i[3] * CYC)
+
+    def iota(o, pat, base, cm=0):
+        op("G", lambda: g.iota(o[0], pat, base, cm, allow_small_or_imprecise_dtypes=True), [], [o], 0.13 + 2 * o[3] * CYC)
+
+    def P(o, terms, start=True, stop=True):
         def run():
-            i = None
-            for f in fns:
-                i = f()
+            for j, t in enumerate(terms):
+                i = pe.matmul((t[2] if len(t) > 2 else o)[0], t[0][0], t[1][0], start and j == 0, stop and j == len(terms) - 1)
             return i
-        op("P", run, rd, wr, _dur("P", "p", n))
+        d = sum(max(64, t[1][3]) * (1 if two(t[1]) else 4) for t in terms) * PCYC
+        op("P", run, [x for t in terms for x in t[:2]] + ([] if start else [o]), [o], d)
 
     nsem = [0]
 
-    def DMA(q, fns, rd, wr, dur):
+    def DMA(q, prs, rd, wr, dur):
         name = "m%d" % nsem[0]
         nsem[0] += 1
 
         def run():
-            for f in fns:
-                f().then_inc(T.sem[name], 16)
-        op(q, run, rd, wr, dur, (name, 16 * len(fns)))
+            for o, i in prs:
+                (g.sync if q == "S" else ac).dma_start(o, i).then_inc(T.sem[name], 16)
+        op(q, run, rd, wr, dur, (name, 16 * len(prs)))
 
-    def mm(out, l, r, a, b):
-        return lambda: pe.matmul(out, l, r, a, b)
+    def sums(L, b, b0, w):
+        return [(R(L, (15 - r, 143 - r)), R(b, (b0 + r, b0 + 16 * w, 16))) for r in range(16)]
 
-    def ts(o, i, s1, o1, s2=None, o2=None):
-        if o2 is None:
-            return lambda: v.tensor_scalar(o, i, s1, None, o1)
-        return lambda: v.tensor_scalar(o, i, s1, s2, o1, o2)
+    ID, NID, NEG, BIG, BLK, TRS, IDF, BLKF = [R(k) for k in ("ID", "NID", "NEG", "BIG", "BLK", "TRS", "IDF", "BLKF")]
+    XC = R("X", (0, 4096))
 
-    def tt(o, a, b, f):
-        return lambda: v.tensor_tensor(out=o, in0=a, in1=b, op=f)
-
-    def cp(o, i):
-        return lambda: v.tensor_copy(o, i)
-
-    def ms(o, c):
-        return lambda: v.memset(o, c)
-
-    def act(o, i, f, **k):
-        return lambda: ac.activation(o, i, f, **k)
-
-    def red(o, i):
-        return lambda: v.tensor_reduce(o, i, AxisListType.X, A.max)
-
-    def iota(o, pat, base, wr, n):
-        op("G", lambda: g.iota(o, pat, base, 0, allow_small_or_imprecise_dtypes=True), [], [wr], 0.13 + 2 * n * CYC)
-
-    def sd(o, i):
-        return lambda: g.sync.dma_start(o, i)
-
-    def W16(t, r):
-        return t[:, r * 128:r * 128 + 128]
-
-    DMA("S", [sd(T.QS[:, :], T.qs[:, :]), sd(T.WT[:, :], T.wt[:, :]), sd(T.KI[:, :], T.kk[:, :])], [], [("QS",), ("WT",), ("KI",)], 2.5)
-    DMA("AD", [lambda: ac.dma_start(T.X[:, 0:4096], T.x0[:, :])], [], [("X", 0, 4096), ("X0D",)], 6.0)
-    op("G", lambda: g.iota(T.PI[:, 0:1], [[0, 1]], 0, 1), [], [("PI", 0, 1)], 0.2)
-    iota(T.CG[:, :], [[1, 8], [0, 16]], 0, ("CG",), 128)
-    iota(T.CR[:, :], [[0, 15], [1, 16]], 0, ("CR",), 240)
-    iota(T.CP[:, :], [[1, 128]], 0, ("CP",), 128)
-    V(ts(T.PI[:, 1:2], T.PI[:, 0:1], 4, A.arith_shift_right), [("PI", 0, 1)], [("PI", 1, 2)])
-    V(ts(T.PI[:, 2:3], T.PI[:, 0:1], 15, A.bitwise_and), [("PI", 0, 1)], [("PI", 2, 3)])
-    V(cp(T.PF[:, 0:3], T.PI[:, 0:3]), [("PI", 0, 3)], [("PF",)])
-    pcol, gcol, rcol = T.PF[:, 0:1], T.PF[:, 1:2], T.PF[:, 2:3]
-    V(ts(mc["BLK"], T.CG[:, :], gcol, A.is_equal), [("CG",), ("PF",)], [("BLK",)], 128)
-    V(ms(T.WL[:, :], 0.0), [], [("WL",)], 1024)
-    V(ms(T.OL[:, :], 0.0), [], [("OL",)], 1024)
-    for nm, s1, k in (("WL", T.WT[:, 0:1], ("WT",)), ("OL", 128.0, ("BLK",))):
-        for r in range(16):
-            V(ts(T[nm][:, r * 128 + r:r * 128 + 128:16], T.CB[:, 512:640:16], s1, A.mult), [("BLK",), k] + ([(nm,)] if r == 0 else []), [(nm, r * 128, r * 128 + 128)])
-    V(cp(T.KF[:, :], T.KI[:, :]), [("KI",)], [("KF",)])
-    V(ts(mc["ID"], T.CP[:, :], pcol, A.is_equal), [("CP",), ("PF",)], [("ID",)], 128)
-    for nm, c, n in (("NEG", -float(BIG), 64), ("NID", -1.0, 64), ("BN", float(BIG), 64), ("NIF", -1.0, 128)):
-        V(ts(mc[nm], mc["ID"], c, A.mult), [("ID",)], [(nm,)], n)
-    V(ts(T.MASK[:, :], T.CR[:, :], rcol, A.is_equal), [("CR",), ("PF",)], [("MASK",)], 240)
-    V(ts(T.RST[:, :], T.CR[:, :], 0.0, A.is_gt), [("CR",)], [("RST",)], 240)
-    V(ts(mc["TRS"], T.CR[:, 0:128], rcol, A.is_gt), [("CR",), ("PF",)], [("TRS",)], 128)
-    V(tt(mc["TRS"], mc["TRS"], mc["BLK"], A.mult), [("TRS",), ("BLK",)], [("TRS",)], 256)
-    V(ts(T.TRR[:, :], T.CR[:, 0:48], pcol, A.is_ge, -64.0, A.mult), [("CR",), ("PF",)], [("TRR",)])
-    V(ts(T.HALF[:, :], T.CR[:, :], 0.0, A.mult), [("CR",)], [("HALF",)], 240)
-    V(ts(T.RM[:, 11:12], rcol, 0.0, A.is_equal, 0.5, A.mult), [("PF",)], [("RM", 11, 12)])
-    V(ts(T.HALF[:, :], T.HALF[:, :], T.RM[:, 11:12], A.add), [("HALF",), ("RM", 11, 12)], [("HALF",)], 240)
-    for f in range(16):
-        V(ms(T.CF[:, 128 + f:256:16], 2.0 ** -(f + 1) if f < 13 else 0.0), [], [("SCL", f, f + 1)])
-    V(tt(mc["SCL"], mc["SCL"], mc["BLK"], A.mult), [("SCL",), ("BLK",)], [("SCL",)], 256)
-    iota(T.CG[:, :], [[1, 16], [0, 8]], 0, ("CG",), 128)
-    iota(T.CP[:, :], [[1, 8], [8, 16]], 0, ("CP",), 128)
-    V(ts(mc["TRL"], T.CG[:, :], pcol, A.is_equal), [("CG",), ("PF",)], [("TRL",)], 128)
-    V(ts(mc["PERM"], T.CP[:, :], pcol, A.is_equal), [("CP",), ("PF",)], [("PERM",)], 128)
-    iota(T.GM[:, :], [[1, 8]], 0, ("GM",), 8)
-    V(ts(T.GM[:, :], T.GM[:, :], gcol, A.is_equal), [("GM",), ("PF",)], [("GM",)])
-    iota(T.DUMP[:, :], [[16, 24]], DUMPX, ("DUMP",), 24)
-    V(ts(T.DUMP[:, :], T.DUMP[:, :], rcol, A.add), [("DUMP",), ("PF",)], [("DUMP",)])
-    iota(T.RT[:, :], [[16, 8]], 0, ("RT",), 8)
-    V(ts(T.RT[:, :], T.RT[:, :], rcol, A.add), [("RT",), ("PF",)], [("RT",)])
-    V(ts(T.SD[:, 0:8], T.RT[:, :], 128.0, A.add), [("RT",)], [("SD", 0, 8)])
-    V(ms(T.GP[:, :], 0.0), [], [("GP",)])
-    V(ms(T.SND[:, :], 512.0), [], [("SND",)])
-    V(ms(T.X[:, 4096:XW], 0.0), [], [("X", 4096, XW)], 320)
+    DMA("S", [(T.QS[:, :], T.qs[:, :]), (T.WT[:, :], T.wt[:, :]), (T.KI[:, :], T.kk[:, :])], [], [R("QS"), R("WT"), R("KI")], 2.5)
+    DMA("AD", [(XC[0], T.x0[:, :])], [], [XC, tok("X0D")], 6.0)
+    iota(R("PI", (0, 1)), [[0, 1]], 0, 1)
+    iota(R("CI"), [[1, 144]], 0)
+    iota(R("CR"), [[0, 15], [1, 16]], 0)
+    ts(R("PI", (1, 2)), R("PI", (0, 1)), 112, A.bitwise_and)
+    ts(R("PI", (2, 3)), R("PI", (0, 1)), 15, A.bitwise_and)
+    cp(R("PF", (0, 3)), R("PI", (0, 3)))
+    pcol, gcol, rcol, g15, thr = [R("PF", (i, i + 1)) for i in range(5)]
+    ts(g15, gcol, 15.0, A.add)
+    cp(R("PF", (5, 6)), R("WT"))
+    ts(R("WL"), R("CI"), g15, A.is_equal, R("PF", (5, 6)), A.mult)
+    ts(R("OL"), R("CI"), g15, A.is_equal, 1024.0, A.mult)
+    ci = R("CI", (0, 128))
+    for k, c in ((NID, -1.0), (ID, 1.0), (IDF, 1.0), (NEG, -B24), (BIG, B22)):
+        ts(k, ci, pcol, A.is_equal, c, A.mult)
+    ms(R("C2K"), 2048.0)
+    ts(BLKF, ci, gcol, A.is_ge)
+    ts(BLK, ci, g15, A.is_le)
+    tt(BLK, BLK, BLKF, A.mult)
+    cp(BLKF, BLK)
+    ts(TRS, ci, pcol, A.is_gt)
+    tt(TRS, TRS, BLK, A.mult)
+    ts(R("MASK"), R("CR"), rcol, A.is_equal)
+    ts(R("RST"), R("CR"), 0.0, A.is_gt)
+    ts(R("PEN"), R("CR", (0, 48)), rcol, A.is_gt, -64.0, A.mult)
+    ts(R("JK", 0, (0, 48)), R("MASK", (0, 48)), -1.5, A.mult)
+    tt(R("PEN"), R("PEN"), R("JK", 0, (0, 48)), A.add)
+    P(R("B4", (0, 1)), [(BLK, R("WT"))])
+    ts(thr, R("B4", (0, 1)), 300.0, A.mult, -2048.0, A.add)
+    KK, KC = R("KF", 0), R("KF", 1)
+    ts(KK, R("KI"), 1920.5, A.is_gt, -4096.0, A.mult)
+    tt(KK, KK, R("KI"), A.add)
+    ts(KK, KK, 128.0, A.add)
+    ts(R("PI", (4, 8)), R("KI"), 1, A.bitwise_and)
+    ts(KC, R("PI", (4, 8)), 2048.0, A.mult, 3 * B22 - 131072.0, A.add)
+    iota(R("DUMP"), [[16, 24]], DUMPX)
+    ts(R("DUMP"), R("DUMP"), rcol, A.add)
+    iota(R("RT"), [[16, 8]], 0)
+    ts(R("RT"), R("RT"), rcol, A.add)
+    ts(R("SD"), R("RT"), 128.0 - B24, A.add)
+    ms(R("GP"), 0.0)
+    ms(R("SND"), 512.0)
+    ms(R("X", (4096, XW)), 0.0)
     for h in "DA":
         n, o = NH[h], OFF[h]
         for a, b, c in ((0, 4, 4), (4, 20, 16), (20, 84, 64)):
-            iota(T["cd" + h][:, a * n:b * n], [[1, b - a], [0, n]], c, ("cd" + h, a * n, b * n), (b - a) * n)
-        op("G", (lambda h=h, n=n: g.iota(T["hi" + h][:, :], [[1, n], [0, 3]], 0, 0)), [], [("hi" + h,)], 0.2)
-        V(ms(T["PL" + h][:, :], 0), [], [("PL" + h,)], 128 * n)
-        for c in range(2):
-            V(ts(T["PL" + h][:, c * n:c * n + n], T.RT[:, o:o + n], QC[h] - 16.0 * o + 16 * n * (1 - c), A.add), [("RT",)], [("PL" + h, c * n, c * n + n)])
-        k0 = 0 if h == "D" else n
-        V(ts(T["rl" + h][:, k0 + 2:k0 + 3 * n:3], T.RT[:, o:o + n], QC[h] - 16.0 * o, A.add), [("RT",)], [("rl" + h, 2, 3)])
-        V(ms(T["res" + h][:, :], 0.0), [], [("res" + h,)])
+            iota(R("cd" + h, (a * n, b * n)), [[STR[h], b - a], [0, n]], c * STR[h])
+        iota(R("hi" + h), [[0, 3], [1, n]], 0)
+        ms(R("PL" + h), 0)
+        ms(R("PT" + h, (32 * STR[h], 64 * STR[h])), 0)
+        for c, base in ((1, QC), (0, SPARE)):
+            ts(R("PL" + h, c, (0, n)), R("RT", (o, o + n)), float(base), A.add)
 
-    def chain(h, l, m, c0):
-        n, k = NH[h], "%s%d" % (h, l)
-        U, u, sq, p = T["U" + h], T["u" + k], T["q" + k], T["p" + k]
-        w = m * n
-        ru, rq, rp = ("u" + k,), ("q" + k,), ("p" + k,)
-        V(cp(u[:, :, :], U[:, c0:c0 + w]), [("U" + h, c0, c0 + w)], [ru], w)
-        V(ts(u[:, :, :], u[:, :, :], 4095, A.bitwise_and), [ru], [ru], w)
-        V(tt(sq[:, :, :], u[:, :, :], u[:, :, :], A.mult), [ru], [rq], 2 * w)
+    UP = {"D": {"U0": 0, "U1": 480, "U2": 0, "t": 80, "up1": 400, "pre": 500}, "A": {"U0": 0, "U1": 4, "U2": 16, "t": 64, "up1": 256, "pre": 352}}
+
+    def chain(h, m, U, p, l):
+        n = NH[h]
+        w, t0 = m * n, UP[h]["t"]
+        r_, v_, s_ = [R(x + h, (0, w)) for x in ("cR", "cv", "cs")]
+        ts(r_, U, CM, A.add, CM, A.subtract)
+        tt(v_, U, r_, A.subtract)
+        if w > 32:
+            act(s_, v_, F.Square)
+        else:
+            tt(s_, v_, v_, A.mult)
         for a in range(4):
-            V(ts(p[:, :, a * n:a * n + n], u[:, :, :], T.KF[:, a:a + 1], A.mult), [ru, ("KF",)], [("p" + k, a, a + 1)], w)
-        V(ts(sq[:, :, :], sq[:, :, :], 5, A.arith_shift_right), [rq], [rq], w)
+            act(R("U" + h, (t0 + a * w, t0 + a * w + w)), v_, F.Identity, scale=R("KF", 0, (a, a + 1)), bias=R("KF", 1, (a, a + 1)))
+        ts(s_, s_, 15.5, A.subtract, 2.0 ** -5, A.mult)
         for a in range(4):
-            pa = p[:, :, a * n:a * n + n]
-            V(tt(pa, pa, sq[:, :, :], A.add), [rq, ("p" + k, a, a + 1)], [("p" + k, a, a + 1)], 2 * w)
-        V(ts(p[:, :, :], p[:, :, :], 4095, A.bitwise_and), [rp], [rp], 4 * w)
-        V(cp(T["l" + k][:, :], p[:, :, :]), [rp], [("l" + k,)], 4 * w)
+            tt(R("cz" + h, (a, 4 * m, 4)), R("U" + h, (t0 + a * w, t0 + a * w + w)), s_, A.add)
+        ts(p, R("cz" + h, (0, 4 * m)), 4095, A.bitwise_and)
+        cp(l, p)
 
-    def gath(h, l, lc0, oname, o0, QX, qn, q0, w):
-        V(tt(T[oname][:, o0:o0 + 16 * w], T.X[:, 0:4096].indirect(T["l%s%d" % (h, l)][:, lc0:lc0 + w]), QX[:, q0:q0 + 16 * w], A.subtract),
-          [("X", 0, 4096), ("l%s%d" % (h, l),), (qn, q0, q0 + 16 * w)], [(oname, o0, o0 + 16 * w)], 16 * w, "g")
-
-    def sums(o, L, b, b0, w, a, z):
-        return [mm(o, W16(T[L], r), b[:, b0 + r:b0 + 16 * w:16], a and r == 0, z and r == 15) for r in range(16)]
-
-    def keys(h, bname, b0, c0, w, pen, k0=None, code=True, lhs="NEG"):
-        k0 = c0 if k0 is None else k0
-        o = T["K" + h][:, k0:k0 + w]
-        f = sums(o, "OL", T[bname], b0, w, True, False)
-        if code:
-            f.append(mm(o, mc["ID"], T["cd" + h][:, c0:c0 + w], False, not pen))
-        for i, (e, _) in enumerate(pen):
-            f.append(mm(o, mc[lhs], e, False, i == len(pen) - 1))
-        P(f, [(bname, b0, b0 + 16 * w), ("OL",), ("ID",), (lhs,), ("cd" + h,)] + [x for _, x in pen], [("K" + h, k0, k0 + w)], len(f) * max(64, w))
-
-    zb, jb = [0], [0]
-
-    def bank():
-        zb[0] += 1
-        return "Z%d" % (zb[0] % 3)
+    zb, jb, eb = [0], [0], [0]
 
     def search(h, s):
-        n = NH[h]
-        QX, qn, q0 = (T.QXD, "QXD", s * 1280) if h == "D" else (T.QXA, "QXA", 0)
-        U, K, PL, lv = T["U" + h], T["K" + h], T["PL" + h], T["lv" + h]
-        un, ln, d3, dn, p2, p3 = "U" + h, "lv" + h, T["d3" + h], "d3" + h, "p%s2" % h, "p%s3" % h
-        if h == "A":
-            R, rn = T.ARR[:, s * C - C:s * C], "ARR%d" % s
-            AC(act(QX[:, 0:48], R, F.Copy), [(rn,)], [(qn, 0, 48)])
-            AC(act(QX[:, 48:96], R, F.Copy), [(rn,)], [(qn, 48, 96)])
-            w = 96
-            while w < 768:
-                AC(act(QX[:, w:2 * w], QX[:, 0:w], F.Copy), [(qn, 0, w)], [(qn, w, 2 * w)], w)
-                w *= 2
-            AC(act(T.X[:, QC[h]:QC[h] + 48], R, F.Copy), [(rn,)], [("X", QC[h], QC[h] + 48)])
-            P(sums(U[:, 0:n], "WL", T.ARR, s * C - C, n, True, True) + sums(U[:, n:2 * n], "OL", T.ARR, s * C - C, n, True, True),
-              [(rn,), ("WL",), ("OL",)], [(un, 0, 2 * n)], 32 * 64)
-            chain("A", 1, 1, 0)
-            V(ts(lv[:, 6 * n:7 * n], U[:, n:2 * n], THR, A.is_lt), [(un, n, 2 * n)], [(ln, 6 * n, 7 * n)])
-            p1, p1r, l0 = T.pA1[:, 0, :], ("pA1",), 0
-        else:
-            AC(act(T.X[:, QC[h]:QC[h] + 80], T.QS[:, s * 80:s * 80 + 80], F.Copy), [("QS",)], [("X", QC[h], QC[h] + 80)], 80)
-            p1, p1r, l0 = T.pD1[:, s, :], ("pD1",), s * 20
-        for l, w, c0, lc in ((1, 4 * n, 32, l0), (2, 16 * n, 64, 0)):
-            dd, c1 = "d%d%s" % (l, h), max(64, w) * 16
-            P(sums(U[:, c0:c0 + w], "WL", QX, q0, w, True, False), [(qn, q0, q0 + 16 * w), ("WL",)], [(un, c0, c0 + w)], c1)
-            gath(h, l, lc, dd, 0, QX, qn, q0, w)
-            P(sums(U[:, c0:c0 + w], "WL", T[dd], 0, w, False, True), [(dd,), ("WL",), (un, c0, c0 + w)], [(un, c0, c0 + w)], c1)
-            chain(h, l + 1, 4 ** l, c0)
-            AC(act(T["b%d%s" % (l, h)][:, :], T[dd][:, :], F.Abs), [(dd,)], [("b%d%s" % (l, h),)], 16 * w)
-        keys(h, "b1" + h, 0, 0, 4 * n, [])
-        k1 = ("K" + h, 0, 4 * n)
-        V(ts(T["v1" + h][:, :], K[:, 0:4 * n], THR, A.is_gt), [k1], [("v1" + h,)])
-        V(ts(lv[:, 0:4 * n], K[:, 0:4 * n], 128.0, A.is_ge), [k1], [(ln, 0, 4 * n)])
-        V(tt(lv[:, 4 * n:6 * n], lv[:, 0:2 * n], lv[:, 2 * n:4 * n], A.mult), [(ln, 0, 4 * n)], [(ln, 4 * n, 6 * n)])
-        V(tt(lv[:, 7 * n:8 * n], lv[:, 4 * n:5 * n], lv[:, 5 * n:6 * n], A.mult), [(ln, 4 * n, 6 * n)], [(ln, 7 * n, 8 * n)])
-        if h == "A":
-            V(tt(lv[:, 7 * n:8 * n], lv[:, 7 * n:8 * n], lv[:, 6 * n:7 * n], A.mult), [(ln, 6 * n, 8 * n)], [(ln, 7 * n, 8 * n)])
-        for a in range(4):
-            AC(act(T["v1r" + h][:, :, a * n:a * n + n], T["v1" + h][:, :], F.Copy), [("v1" + h,)], [("v1r" + h, a, a + 1)])
-        r1n = "r1A" if h == "A" else "r1D%d" % s
-        r1 = T.r1A[:, :, :] if h == "A" else T.r1D[:, 4 * s:4 * s + 4, :]
-        if h == "A":
-            for a in range(4):
-                V(cp(T.r1A[:, :, a * n:a * n + n], p1), [p1r], [("r1A", a, a + 1)])
-        up1, up2 = U[:, 288:288 + 16 * n], U[:, 192:192 + 16 * n]
-        V(cp(up1, r1), [(r1n,)], [(un, 288, 288 + 16 * n)], 16 * n)
-        V(tt(T["e21" + h][:, :, :], T[p2][:, :, :], up1, A.is_equal), [(p2,), (un, 288, 288 + 16 * n)], [("e21" + h,)], 16 * n)
-        pen = [(T["e21" + h][:, :, :], ("e21" + h,)), (T["v1r" + h][:, :, :], ("v1r" + h,))]
-        keys(h, "b2" + h, 0, 4 * n, 16 * n, pen)
-        keys(h, "b2" + h, 0, 4 * n, 16 * n, pen, 84 * n, False, "BN")
-        V(ts(T["v2" + h][:, :], K[:, 84 * n:100 * n], THR, A.is_gt), [("K" + h, 84 * n, 100 * n)], [("v2" + h,)], 16 * n)
-        for a in range(4):
-            AC(act(T["v2r" + h][:, :, a * n:a * n + n], T["v2" + h][:, :], F.Copy), [("v2" + h,)], [("v2r" + h, a, a + 1)], 16 * n)
-        V(cp(up2, T[p2][:, :, :]), [(p2,)], [(un, 192, 192 + 16 * n)], 16 * n)
-        for a in range(4):
-            blk = T[p3][:, :, a * n:a * n + n]
-            V(tt(T["e32" + h][:, :, a * n:a * n + n], blk, up2, A.is_equal), [(p3,), (un, 192, 192 + 16 * n)], [("e32" + h, a, a + 1)], 16 * n)
-            V(tt(T["e31" + h][:, :, a * n:a * n + n], blk, up1, A.is_equal), [(p3,), (un, 288, 288 + 16 * n)], [("e31" + h, a, a + 1)], 16 * n)
-        DMA("S", [sd(PL[:, 4 * n:8 * n], p1), sd(PL[:, 16 * n:32 * n], T[p2][:, :, :]), sd(PL[:, 64 * n:128 * n], T[p3][:, :, :])],
-            [p1r, (p2,), (p3,)], [("PL" + h, 4 * n, 8 * n), ("PL" + h, 16 * n, 32 * n), ("PL" + h, 64 * n, 128 * n)], 2.2)
-        W, l3 = 256 * n, "l%s3" % h
-        for c in range(4):
-            b0 = (c % 3) * W
-            if c in ZETA[h]:
-                AC(act(d3[:, b0:b0 + W], T.X[:, 0:4096].indirect(T[l3][:, c * 16 * n:c * 16 * n + 16 * n]), F.Copy), [("X", 0, 4096), (l3,)], [(dn, b0, b0 + W)], W, "g")
-                for a in range(0, W, 512):
-                    w = min(512, W - a)
-                    Zn = bank()
-                    Z, da = T[Zn][:, 0:w], d3[:, b0 + a:b0 + a + w]
-                    P([mm(Z, mc["ID"], da, True, False), mm(Z, mc["NID"], QX[:, q0 + a:q0 + a + w], False, True)],
-                      [(dn, b0 + a, b0 + a + w), (qn, q0 + a, q0 + a + w), ("ID",), ("NID",)], [(Zn, 0, w)], 2 * w)
-                    AC(act(da, Z, F.Abs), [(Zn, 0, w)], [(dn, b0 + a, b0 + a + w)], w)
-            else:
-                gath(h, 3, c * 16 * n, dn, b0, QX, qn, q0, 16 * n)
-                AC(act(d3[:, b0:b0 + W], d3[:, b0:b0 + W], F.Abs), [(dn, b0, b0 + W)], [(dn, b0, b0 + W)], W)
-            keys(h, dn, b0, (20 + 16 * c) * n, 16 * n, [(T[e + h][:, 4 * c:4 * c + 4, :], (e + h,)) for e in ("e32", "e31", "v2r")])
+        n, o, up = NH[h], OFF[h], UP[h]
+        Un, Kn, PL = "U" + h, "K" + h, "PL" + h
 
-    def tail(h, s):
-        n, o = NH[h], OFF[h]
-        w, f0 = 48 * n, 48 * o
-        K, lv, ln, cc, co, gm, sc, yt, rl, dp = [T[x + h] for x in ("K", "lv")] + ["lv" + h] + [T[x + h] for x in ("cc", "co", "gm", "sc", "yt", "rl", "dp")]
-        M, rM, live, rlv = lv[:, n:2 * n], (ln, n, 2 * n), lv[:, 7 * n:8 * n], (ln, 7 * n, 8 * n)
+        def QX(a, b):
+            if h == "A":
+                return R("QXA", (a, b))
+            return R("QX0", (a, b)) if s == 0 else R("QXD", s - 1, (a, b))
+
+        def QXs(r, w):
+            return R("QXA", (r, 16 * w, 16))
+        p1, p2 = R(PL, (4, 8), (0, n)), R(PL, (16, 32), (0, n))
+        if h == "A":
+            q = R("ARR", s - 1)
+            gcp(QX(0, 48), q)
+            gcp(QX(48, 96), q)
+            for w in (96, 192, 384):
+                gcp(QX(w, 2 * w), QX(0, w))
+            U0 = R(Un, (0, n))
+            P(U0, [(NID, R("C2K", (0, n)))], True, False)
+            P(U0, [(R("WL", (15 - r, 143 - r)), R("ARR", s - 1, (r, C, 16))) for r in range(16)], False, True)
+            act(R("UQA", 0), U0, F.Copy)
+            chain(h, 1, U0, p1, R("l1A"))
+            ts(R("htA", (4 * n, 5 * n)), U0, thr, A.is_gt, -1.0, A.mult)
+            for w in (1, 2, 4, 8):
+                gcp(R("UQA", (w, 2 * w)), R("UQA", (0, w)))
+            l1, uq = R("l1A"), lambda m: R("UQA", (0, m))
+        else:
+            q = R("QS", (s * 80, s * 80 + 80))
+            gcp(p1, R("p1D", (4 * s, 4 * s + 4)))
+            l1, uq = R("l1D", (20 * s, 20 * s + 20)), lambda m: R("UQD", (0, m), (5 * s, 5 * s + 5))
+        gcp(R("X", (QC + 16 * o, QC + 16 * (o + n))), q)
+        gcp(R("RG" + h, (48 * n, 64 * n)), q)
+        for a in range(4):
+            gcp(R("r1" + h, (a, 16, 4)), p1)
+        up1 = R(Un, (up["up1"], up["up1"] + 16 * n))
+        up2 = R("KD", (432, 512)) if h == "D" else R(Un, (304, 352))
+        U1 = R(Un, (up["U1"], up["U1"] + 4 * n))
+        P(U1, [(IDF, uq(4))], True, False)
+        gat(R("d12" + h, (0, 64 * n)), XC, l1, QX(0, 64 * n))
+        P(U1, sums("WL", "d12" + h, 0, 4 * n), False, True)
+        chain(h, 4, U1, p2, R("l2" + h))
+        ts(R("v1" + h), U1, thr, A.is_gt)
+        for a in range(4):
+            gcp(R("v1r" + h, (a, 16, 4)), R("v1" + h))
+        gat(R("d12" + h, (64 * n, 320 * n)), XC, R("l2" + h), QX(0, 256 * n))
+        cp(up1, R("r1" + h))
+        tt(R("e21" + h), p2, up1, A.is_equal)
+        cp(up2, p2)
+        U2 = R(Un, (up["U2"], up["U2"] + 16 * n))
+        P(U2, [(IDF, uq(16)), (BIG, R("e21" + h)), (BIG, R("v1r" + h))], True, False)
+        P(U2, sums("WL", "d12" + h, 64 * n, 16 * n), False, True)
+        chain(h, 16, U2, R(PL, (64, 128), (0, n)), R("l3" + h))
+        for a, b in ((0, 32), (64, 128)):
+            i, d = R(PL, (a, b)), R("PT" + h, (a * STR[h], b * STR[h]))
+            DMA("S", [(d[0], i[0])], [i], [d], 2.5)
+        ts(R("v2" + h), U2, thr, A.is_gt)
+        for a in range(4):
+            gcp(R("v2r" + h, (a, 64, 4)), R("v2" + h))
+        for a in range(4):
+            blk = R(PL, (64 + a, 128, 4), (0, n))
+            tt(R("e32" + h, (a, 64, 4)), blk, up2, A.is_equal)
+            tt(R("e31" + h, (a, 64, 4)), blk, up1, A.is_equal)
+        act(R("b12" + h), R("d12" + h), F.Abs)
+        k2 = R(Kn, (5 * n, 21 * n))
+        P(R(Kn, (n, 21 * n)), sums("OL", "b12" + h, 0, 20 * n) + [(NEG, R("e21" + h), k2), (NEG, R("v1r" + h), k2), (ID, R("cd" + h, (0, 20 * n)))])
+        ts(R("ht" + h, (0, 4 * n)), R(Kn, (n, 5 * n)), 1024.0, A.is_lt, -1.0, A.mult)
+        P(R(Kn, (0, n)), [(NEG, R("ht" + h, (a * n, a * n + n))) for a in range(5 if h == "A" else 4)])
+        for c0, c1 in KEY[h]:
+            for a, b, e in SEG[h]:
+                if not c0 <= a < c1:
+                    continue
+                b0, W = 16 * n * a, 16 * n * (b - a)
+                d, l = R("d3" + h, (b0, b0 + W)), R("l3" + h, (a * n, b * n))
+                if e == "V":
+                    gat(d, XC, l, QX(0, W))
+                    act(d, d, F.Abs)
+                else:
+                    gat(d, XC, l)
+                    pc = 480 if h == "D" else 384
+                    for x in range(0, W, pc):
+                        w = min(pc, W - x)
+                        zb[0] ^= 1
+                        Z, da = R("Z%d" % zb[0], (0, w)), R("d3" + h, (b0 + x, b0 + x + w))
+                        P(Z, [(ID, da), (NID, QX(x, x + w))])
+                        act(da, Z, F.Abs)
+            P(R(Kn, ((21 + c0) * n, (21 + c1) * n)), [(ID, R("cd" + h, ((20 + c0) * n, (20 + c1) * n)))] +
+              [(NEG, R(e + h, (c0, c1))) for e in ("e32", "e31", "v2r")] + sums("OL", "d3" + h, 16 * n * c0, (c1 - c0) * n))
+
+    def tail(h, s, last):
+        n, o, st = NH[h], OFF[h], STR[h]
+        w = 48 * n
+        M, sc = R("M" + h), "sc" + h
         for i in range(n):
-            V(red(lv[:, n + i:n + i + 1], K[:, i:84 * n:n]), [("K" + h, 0, 84 * n)], [(ln, n + i, n + i + 1)], 84)
-        V(tt(T["MI" + h][:, :], M, live, A.mult), [rM, rlv], [("MI" + h,)])
-        for k, (sh, ma) in enumerate(((0, 127), (2, 31), (4, 7))):
-            V(ts(cc[:, k:3 * n:3], T["MI" + h][:, :], sh, A.arith_shift_right, ma, A.bitwise_and), [("MI" + h,)], [("cc" + h, k, k + 1)])
-        V(ts(co[:, :], cc[:, :], float(n), A.mult), [("cc" + h,)], [("co" + h,)])
-        V(tt(co[:, :], co[:, :], T["hi" + h][:, :], A.add), [("co" + h,), ("hi" + h,)], [("co" + h,)])
-        V(cp(T["o16" + h][:, :], co[:, :]), [("co" + h,)], [("o16" + h,)])
-        V(tt(gm[:, :], T["PL" + h][:, :].indirect(T["o16" + h][:, :]), T.MASK[:, 0:w], A.mult), [("PL" + h,), ("o16" + h,), ("MASK",)], [("gm" + h,)], w, "g")
-        P([mm(T.B4[:, 0:w], mc["SCL"], T.HALF[:, 0:w], True, False)], [("SCL",), ("HALF",)], [("B4", 0, w)], 4 * w)
-        P([mm(T.B4[:, 0:w], mc["SCL"], gm[:, :], False, True)], [("gm" + h,), ("SCL",), ("B4", 0, w)], [("B4", 0, w)], 4 * w)
-        V(lambda: v.tensor_tensor_scan(sc[:, :], T.RST[:, 0:w], gm[:, :], 0.0, A.mult, A.add), [("RST",), ("gm" + h,)], [("sc" + h,)], w)
-        k0, v0 = (0, 3 * n) if h == "D" else (n, 0)
-        V(cp(rl[:, k0:k0 + 3 * n:3], sc[:, 31:w:48]), [("sc" + h,)], [("rl" + h, 0, 1)])
-        V(cp(rl[:, k0 + 1:k0 + 3 * n:3], sc[:, 47:w:48]), [("sc" + h,)], [("rl" + h, 1, 2)])
-        V(cp(rl[:, v0:v0 + n], sc[:, 15:w:48]), [("sc" + h,)], [("rl" + h, 3, 4)])
-        xw = QC[h] + 32 * n
-        AC(act(T.RG[:, 64 * o:64 * o + 64 * n], T.X[:, 0:xw].indirect(rl[:, 0:4 * n]), F.Copy), [("X", 0, xw), ("rl" + h,)], [("RG", 64 * o, 64 * o + 64 * n)], 64 * n, "g")
-        ry, fe, rf = ("yt" + h,), T.FE[:, f0:f0 + w], ("FE", f0, f0 + w)
-        V(ts(yt[:, :], T.B4[:, 0:w], CM, A.add, CM, A.subtract), [("B4", 0, w)], [ry], w)
-        V(tt(yt[:, :], T.B4[:, 0:w], yt[:, :], A.subtract), [("B4", 0, w), ry], [ry], w)
-        V(ts(fe, yt[:, :], 0.0, A.is_gt, 0.5, A.subtract), [ry], [rf], w)
-        for gg in range(8):
-            dst, sg = T.LB[:, f0 * 8 + gg:(f0 + w) * 8:8], T.GM[:, gg:gg + 1]
-            if gg in LBA[h]:
-                AC(act(dst, fe, F.Copy, scale=sg), [rf, ("GM",)], [("LB" + h, gg, gg + 1)], w)
-            else:
-                V(ts(dst, fe, sg, A.mult), [rf, ("GM",)], [("LB" + h, gg, gg + 1)], w // 2)
-        dmp = T.DUMP[:, 3 * o:3 * o + 3 * n]
-        V(tt(dp[:, :], sc[:, 15:w:16], dmp, A.subtract), [("sc" + h,), ("DUMP",)], [("dp" + h,)])
-        V(ts(lv[:, 0:n], M, THR, A.is_lt), [rM], [(ln, 0, n)])
-        res = T["res" + h]
+            red(R("M" + h, (i, i + 1)), R("K" + h, (i, 85 * n, n)))
+        cp(R("MI" + h), M)
+        for k in range(3):
+            ts(R("cc" + h, k), R("MI" + h), 2 * k, A.arith_shift_right, ((128 >> 2 * k) - 1) * st, A.bitwise_and)
+        tt(R("cc" + h), R("cc" + h), R("hi" + h), A.add)
+        cp(R("o16" + h), R("cc" + h))
+        gat(R("gm" + h), R("PT" + h), R("o16" + h), R("MASK", (0, w)), A.mult)
+        sp = R("B4" if h == "D" else "B5", (0, w))
+        P(sp, [(BLKF, R("gm" + h))])
+        cp(R("SP", sl(None), (16 * o, 16 * (o + n))), sp)
+        a, b, c = R(sc), R("RST", (0, w)), R("gm" + h)
+        op("V", lambda: v.tensor_tensor_scan(a[0], b[0], c[0], 0.0, A.mult, A.add), [b, c], [a], w * CYC)
+        cp(R("rl" + h), R(sc, (15, w, 16)))
+        gat(R("RG" + h, (0, w)), R("X", (0, DUMPX)), R("rl" + h))
+        ts(R("ne" + h), M, THR, A.is_lt, 0.5, A.subtract)
         for i in range(n):
             gi = o + i
-            z = 48 * (gi + 1)
-            per = 3 if 3 * z <= 512 else (2 if 2 * z <= 512 else 1)
-            for slot, kk in enumerate([list(range(3))[a:a + per] for a in range(0, 3, per)]):
-                Zn = bank()
-                Z, f, t = T[Zn], [], len(kk) * z
-                for j, k in enumerate(kk):
-                    L = W16(T.LB, gi * 3 + k)
-                    c = j * z
-                    if gi:
-                        f.append(mm(Z[:, c:c + z - 48], L, T.FE[:, 0:z - 48], True, True))
-                    f.append(mm(Z[:, c + z - 48:c + z], L, T.FE[:, z - 48:z], True, False))
-                    f.append(mm(Z[:, c + z - 48:c + z], mc["TRL"], T.TRR[:, :], False, True))
-                P(f, [("FE", 0, z), ("LB" + h,), ("TRL",), ("TRR",)], [(Zn, 0, t)], len(kk) * (max(64, z - 48) + 128))
-                x = slot * n + i
-                if slot in DVC[h]:
-                    V(red(T.RM[:, x:x + 1], Z[:, 0:t]), [(Zn, 0, t)], [("RM", x, x + 1)], t)
-                else:
-                    jb[0] = (jb[0] + 512) % 2048
-                    j0 = jb[0]
-                    AC(act(T.JK[:, j0:j0 + t], Z[:, 0:t], F.Relu, bias=-7.0, scale=2.0, accum_out=res[:, x:x + 1]), [(Zn, 0, t)],
-                       [("res" + h, x, x + 1), ("JK", j0, j0 + t)], t)
-        if DVC[h]:
-            x, y = DVC[h][0] * n, DVC[h][-1] * n + n
-            V(ts(res[:, x:y], T.RM[:, x:y], 3.75, A.is_gt), [("RM", x, y)], [("res" + h, x, y)])
-        ns = 2 if h == "D" else 3
-        c0 = 256 + 16 * (h == "A")
-        o4 = T.B4[:, c0:c0 + n]
-        P([mm(o4, mc["PERM"], res[:, i * n:i * n + n], i == 0, False) for i in range(ns)] + [mm(o4, mc["NIF"], live, False, True)],
-          [("res" + h,), ("PERM",), ("NIF",), rlv], [("B4", c0, c0 + n)], ns * 256 + 256)
-        nc, wm = T["nc" + h], T["wm" + h]
+            e = eb[0] = (eb[0] + 1) % 3
+            for k in range(3):
+                ts(R("EQ", e, k, sl(None), (0, 16 * gi + 16)), R("SP", sl(None), (0, 16 * gi + 16)), R(sc, (16 * (k * n + i) + 15, 16 * (k * n + i) + 16)), A.is_equal)
+            Zn, z0 = ("B4", "B5")[gi % 2], 256
+            wo = 48 * min(gi, 2)
+            if gi:
+                P(R(Zn, (z0, z0 + wo)), [(BIG, R("EQ", e, k, sl(None), (16 * j, 16 * min(j + 2, gi))), R(Zn, (z0, z0 + 48 * (min(j + 2, gi) - j))))
+                                         for j in range(0, gi, 2) for k in range(3)])
+            P(R(Zn, (z0 + wo, z0 + wo + 48)), [(BIG, R("PEN"))] + [(BIG, R("EQ", e, k, sl(None), (16 * gi, 16 * gi + 16))) for k in range(3)])
+            Z = R(Zn, (z0, z0 + wo + 48))
+            jb[0] = (jb[0] + 1) % 4
+            act(R("JK", jb[0], (0, wo + 48)), Z, F.Relu, accum_out=R("res" + h, (i, i + 1)))
+        res = R("res" + h)
+        if s < S - 1:
+            gone, p4 = R("GP", (8 + o, 8 + o + n)), R("U" + h, (UP[h]["pre"], UP[h]["pre"] + n))
+            tt(gone, res, R("ne" + h), A.is_lt)
+            P(p4, [(TRS, gone), (NEG, gone)] + [(BLK, R("GP", (8 + o - x, 8 + o + n - x))) for x in range(1, o + n)])
+            tt(R("ds" + h), p4, R("SD", (o, o + n)), A.min)
+            ts(R("s16" + h), R("ds" + h), B24, A.add)
+            scat(R("SND"), R("s16" + h), R("RG" + h, (0, 16 * n)))
         for k in range(3):
-            V(ts(nc[:, k:3 * n:3], o4, -1.0, A.is_equal), [("B4", c0, c0 + n)], [("nc" + h, k, k + 1)])
-        V(tt(wm[:, :], dp[:, :], nc[:, :], A.mult), [("dp" + h,), ("nc" + h,)], [("wm" + h,)])
-        V(tt(wm[:, :], wm[:, :], dmp, A.add), [("wm" + h,), ("DUMP",)], [("wm" + h,)])
-        V(cp(T["w16" + h][:, :], wm[:, :]), [("wm" + h,)], [("w16" + h,)])
-        if s == S - 1:
-            return
-        g0 = 8 + o
-        V(tt(T.GP[:, g0:g0 + n], nc[:, 0:3 * n:3], lv[:, 0:n], A.mult), [("nc" + h,), (ln, 0, n)], [("GP", g0, g0 + n)])
-        if h == "D" and s:
-            return
-        m = o + n
-        gone, rg, ds, p4 = T.GP[:, 8:8 + m], ("GP", 8, 8 + m), T.SD[:, 8:8 + m], T.B4[:, 288:288 + m]
-        f = [mm(p4, mc["TRS"], gone, True, False)] + [mm(p4, mc["BLK"], T.GP[:, 8 - x:8 - x + m], False, x == m - 1) for x in range(1, m)]
-        P(f, [("GP", 0, 8 + m), ("TRS",), ("BLK",)], [("B4", 288, 288 + m)], 64 * m)
-        V(tt(ds, p4, T.SD[:, 0:m], A.subtract), [("B4", 288, 288 + m), ("SD", 0, 8)], [("ds",)])
-        V(tt(ds, ds, gone, A.mult), [("ds",), rg], [("ds",)])
-        V(tt(ds, ds, T.SD[:, 0:m], A.add), [("ds",), ("SD", 0, 8)], [("ds",)])
-        V(cp(T.s16[:, 0:m], ds), [("ds",)], [("s16",)])
+            tt(R("wm" + h, k), R(sc, (16 * k * n + 15, 16 * (k + 1) * n, 16)), res, A.add)
+        tt(R("wm" + h), R("wm" + h), R("DUMP", (3 * o, 3 * (o + n))), A.min)
+        cp(R("w16" + h), R("wm" + h))
 
-    P(sums(T.UD[:, 0:30], "WL", T.QS, 0, 30, True, True), [("QS",), ("WL",)], [("UD", 0, 30)], 1024)
-    chain("D", 1, 6, 0)
-    for s in range(S):
-        b, w = s * 1280, 80
-        if s == 0:
-            V(cp(T.QXD[:, 0:80], T.QS[:, 0:80]), [("QS",)], [("QXD", 0, 80)])
-        else:
-            DMA("S", [sd(T.QXD[:, b:b + 80], T.QS[:, s * 80:s * 80 + 80])], [("QS",), ("X0D",)], [("QXD", b, b + 80)], 2.0)
-        while w < 1280:
-            if s == 0:
-                V(cp(T.QXD[:, w:2 * w], T.QXD[:, 0:w]), [("QXD", 0, w)], [("QXD", w, 2 * w)], w // 2)
-            else:
-                DMA("S", [sd(T.QXD[:, b + w:b + 2 * w], T.QXD[:, b:b + w])], [("QXD", b, b + w)], [("QXD", b + w, b + 2 * w)], 2.0)
-            w *= 2
-        for a in range(4):
-            V(cp(T.r1D[:, 4 * s:4 * s + 4, a * 5:a * 5 + 5], T.pD1[:, s, :]), [("pD1",)], [("r1D%d" % s, a, a + 1)])
+    U0 = R("UD", (0, 30))
+    P(U0, [(NID, R("C2K", (0, 30)))] + sums("WL", "QS", 0, 30))
+    act(R("UQD", 0), U0, F.Copy)
+    chain("D", 6, U0, R("p1D"), R("l1D"))
+    for w in (1, 2, 4, 8):
+        gcp(R("UQD", (w, 2 * w)), R("UQD", (0, w)))
+    cp(R("QX0", (0, 80)), R("QS", (0, 80)))
+    for w in (80, 160, 320, 640):
+        cp(R("QX0", (w, 2 * w)), R("QX0", (0, w)))
+    DMA("S", [(T.QXD[:, :, 0:80], T.QS[:, 80:480])], [R("QS"), tok("X0D")], [R("QXD", sl(None), (0, 80))], 2.5)
+    for w in (80, 160, 320, 640):
+        DMA("S", [(T.QXD[:, :, w:2 * w], T.QXD[:, :, 0:w])], [R("QXD", sl(None), (0, w))], [R("QXD", sl(None), (w, 2 * w))], 2.5)
     nxt = T.cores[(rank + 1) % len(T.cores)]
     rid, pid = topo.addr(nxt)[:2]
     msk, neng = topo.mask(core, nxt), len(topo.engines(core, nxt))
+    snd = R("SND", (0, C))
     for s in range(S):
         halves = "DA" if s else "D"
         if 0 < s < S - 1:
-            V(ms(T.SND[:, 0:C], 512.0), [("snt", s, s + 1)], [("SND",)])
+            op("G", lambda: g.iota(snd[0], [[0, C]], 512, 0, allow_small_or_imprecise_dtypes=True), [tok("snt%d" % s)], [snd], 0.25)
         for h in halves:
             search(h, s)
         for h in halves:
-            tail(h, s)
-        for h in halves:
-            n, r0 = NH[h], (0 if h == "D" else 368)
-            V((lambda h=h, n=n, r0=r0: v.tensor_copy(T.X[:, :].indirect(T["w16" + h][:, :]), T.RG[:, r0:r0 + 48 * n])),
-              [("w16" + h,), ("RG", r0, r0 + 48 * n)], [("X", 0, XW)], 48 * n, "s")
+            tail(h, s, h == halves[-1])
         if s < S - 1:
-            n = 8 if s else 5
-            V((lambda n=n: v.tensor_copy(T.SND[:, :].indirect(T.s16[:, 0:n]), T.RG[:, 240:240 + 16 * n])), [("s16",), ("RG", 240, 240 + 16 * n)], [("SND",)], 16 * n, "s")
-            op("G", (lambda s=s: g.remote_dma(T.ARR[:, s * C:s * C + C], T.SND[:, 0:C], T.sem["arr%d" % (s + 1)], T.sem["snt%d" % (s + 1)], pid, rid, msk)),
-               [("SND",)], [], 0.5, ("none", 0))
-            op("N", None, [("SND",)], [("ARR%d" % (s + 1),)], 2.5, ("arr%d" % (s + 1), neng))
-            op("N", None, [("SND",)], [("snt", s + 1, s + 2)], 2.5, ("snt%d" % (s + 1), neng))
-    DMA("S", [sd(T.y[:, 0:2048], T.X[:, 0:2048])], [("X", 0, 2048)], [("y1",)], 4.0)
-    DMA("AD", [lambda: ac.dma_start(T.y[:, 2048:4096], T.X[:, 2048:4096])], [("X", 2048, 4096)], [("y2",)], 4.0)
+            op("G", (lambda s=s: g.remote_dma(T.ARR[:, s, :], snd[0], T.sem["arr%d" % (s + 1)], T.sem["snt%d" % (s + 1)], pid, rid, msk)),
+               [snd], [], 0.5, ("none", 0))
+            op("N", None, [snd], [R("ARR", s)], 2.5, ("arr%d" % (s + 1), neng))
+            op("N", None, [snd], [tok("snt%d" % (s + 1))], 2.5, ("snt%d" % (s + 1), neng))
+        for h in halves:
+            scat(R("X"), R("w16" + h), R("RG" + h, (16 * NH[h], 64 * NH[h])))
+    DMA("S", [(T.y[:, 0:2048], T.X[:, 0:2048])], [R("X", (0, 2048))], [tok("y1")], 4.0)
+    DMA("AD", [(T.y[:, 2048:4096], T.X[:, 2048:4096])], [R("X", (2048, 4096))], [tok("y2")], 4.0)
 
     eng = {"V": v, "A": ac, "P": pe, "G": g, "S": g.sync, "AD": ac}
     phys = {"V": "V", "A": "A", "P": "P", "G": "G", "S": "S", "AD": "A", "N": "N"}
     N = len(ops)
-    deps = [dict() for _ in range(N)]
-    hist = {}
-    for i, (q, fn, rd, wr, du, own) in enumerate(ops):
-        for isw, lst in ((0, rd), (1, wr)):
-            for nm, lo, hi in lst:
-                bank_ = nm in BANKS
-                for j, w, a, b in hist.get(nm, ()):
-                    over, same = lo < b and a < hi, ops[j][0] == q
-                    if j != i and ((over and (isw or w)) or (bank_ and not same)):
-                        deps[i][j] = deps[i].get(j, False) or bool(over or not same)
-        for isw, lst in ((0, rd), (1, wr)):
-            for nm, lo, hi in lst:
-                hh = hist.setdefault(nm, [])
-                if isw:
-                    hh[:] = [x for x in hh if x[0] == i or not (lo <= x[2] and x[3] <= hi)]
-                hh.append((i, isw, lo, hi))
     if "o" not in ORDER:
+        deps = [dict() for _ in range(N)]
+        hist, runs = {}, {}
+        for i, (q, fn, rd, wr, du, own) in enumerate(ops):
+            for isw, lst in ((0, rd), (1, wr)):
+                for nm, b in lst:
+                    for j, w, a in hist.get(nm, ()):
+                        if j != i and a & b and (isw or w):
+                            deps[i][j] = True
+                    if nm in BANKS:
+                        run = runs.setdefault(nm, [q, [], []])
+                        if run[0] != q:
+                            run[:] = [q, [], run[1]]
+                        run[1].append(i)
+                        for j in run[2]:
+                            deps[i][j] = True
+            for isw, lst in ((0, rd), (1, wr)):
+                for nm, b in lst:
+                    hh = hist.setdefault(nm, [])
+                    if isw:
+                        hh[:] = [x for x in hh if x[0] == i or x[2] & ~b]
+                    hh.append((i, isw, b))
         succ = [[] for _ in range(N)]
         for i in range(N):
             for j in deps[i]:
@@ -486,10 +445,11 @@ def rank_program(g, core, T, topo):
             fin[c] = t + ops[c][4]
             for k in succ[c]:
                 left[k] -= 1
-                rt[k] = max(rt[k], fin[c] + WAKE * (deps[k][c] is True))
+                rt[k] = max(rt[k], fin[c] + WAKE)
                 if not left[k]:
                     ready.setdefault(phys[ops[k][0]], []).append(k)
-        ORDER["o"] = order
+        ORDER["o"], ORDER["d"], ORDER["fin"], ORDER["ops"] = order, deps, fin, ops
+    deps = ORDER["d"]
     cnt = {"V": 0, "A": 0, "P": 0, "G": 0}
     val, snap = [None] * N, [{} for _ in range(N)]
     know = {q: {} for q in "VAPGS"}
@@ -500,11 +460,10 @@ def rank_program(g, core, T, topo):
             val[i] = own
             continue
         kn, want = know[p], {}
-        for j, need in deps[i].items():
-            if need or p != phys[ops[j][0]]:
-                sem, c = val[j]
-                if kn.get(sem, 0) < c:
-                    want[sem] = max(want.get(sem, (0, 0)), (c, j))
+        for j in deps[i]:
+            sem, c = val[j]
+            if kn.get(sem, 0) < c:
+                want[sem] = max(want.get(sem, (0, 0)), (c, j))
         for sem in sorted(want, key=lambda k: -want[k][1]):
             c, j = want[sem]
             if kn.get(sem, 0) < c:

@@ -9,18 +9,22 @@ QC, SPARE, DUMPX, XW = 4096, 4224, 4352, 4736
 B24, B22 = float(1 << 24), float(1 << 22)
 THR = 4090.0 * 1024
 CM = 1.5 * 2.0 ** 35
-SEG = {"D": ((0, 16, "V"), (16, 32, "A"), (32, 48, "V"), (48, 64, "A")), "A": ((0, 16, "A"), (16, 32, "V"), (32, 48, "A"), (48, 64, "V"))}
-KEY = {"D": ((0, 16), (16, 32), (32, 48), (48, 64)), "A": ((0, 32), (32, 64))}
+CFG = {"L2D": "V8 A8", "L2A": "V16", "L3D": "A8 V8 A8 V8 A8 V8 Y8 Y8", "L3A": "A10 V12 A10 V12 V10 V10",
+       "L2D0": "V8 A8", "L3D0": "A8 V8 A8 V8 A8 V8 Y8 Y8",
+       "KEYD": (16, 16, 16, 16), "KEYA": (22, 22, 20), "KEYD0": (16, 16, 16, 16), "ROUNDS": 2,
+       "FOLDD": ("B5", "B4", "B5", "B4", "B5"), "FOLDA": ("B4", "B5", "Z0"), "REDD": "AAAAA", "REDA": "AAV"}
 SB, PS = "sbuf", "psum"
-CYC, PCYC, WAKE, AFIX = 0.00104, 0.00055, 0.1, 0.06
+CYC, PCYC, WAKE, AFIX = 0.00095, 0.00045, 0.2, 0.06
+INORDER = "VAP"
 
 
 def _shapes():
     b, f, i4, u2 = "bfloat16", "float32", "int32", "uint16"
     d = {"X": ([XW], b), "QS": ([480], b), "QX0": ([1280], b), "QXD": ([5, 1280], b), "QXA": ([768], b), "WT": ([1], b), "KI": ([4], i4),
          "KF": ([4, 4], f), "WL": ([144], b), "OL": ([144], b), "CI": ([144], f), "CR": ([240], f), "MASK": ([240], f), "RST": ([240], f),
-         "PI": ([8], i4), "PF": ([8], f), "PEN": ([48], b), "C2K": ([32], b), "DUMP": ([24], f), "RT": ([8], f), "SD": ([8], f),
-         "GP": ([16], b), "SND": ([256], b), "JK": ([4, 144], b), "ARR": ([5, C], b), "SP": ([3, 128], u2), "EQ": ([3, 3, 3, 128], b),
+         "PI": ([8], i4), "PF": ([8], f), "PEN": ([144], b), "C2K": ([80], b), "DUMP": ([24], f), "RT": ([8], f), "SD": ([8], f),
+         "GPD": ([16], b), "GPA": ([8], b), "SND": ([256], b), "JK": ([4, 144], b), "ARR": ([5, C], b), "SP": ([3, 128], u2),
+         "EQD": ([5, 3, 3, 80], b), "EQA": ([3, 3, 3, 128], b), "r3D": ([1024 * 5], b), "r3A": ([1024 * 3], b), "OL2": ([144], b), "OLN": ([144], b),
          "UQD": ([16, 30], f), "UQA": ([16, 3], f), "p1D": ([24, 5], i4), "l1D": ([120], u2), "l1A": ([12], u2)}
     for k in ("ID", "NID", "NEG", "BIG", "BLK", "TRS"):
         d[k] = ([128], b)
@@ -28,13 +32,13 @@ def _shapes():
         d[k] = ([128], f)
     for h in "DA":
         n = NH[h]
-        for nm, sh, ty in (("PL", [128, STR[h]], i4), ("PT", [128 * STR[h]], i4), ("cR", [16 * n], f), ("cv", [16 * n], f), ("cs", [16 * n], f), ("cz", [64, n], i4),
-                           ("l2", [16 * n], u2), ("l3", [64 * n], u2), ("r1", [16, n], i4), ("e21", [16 * n], b), ("v1", [4 * n], b),
-                           ("v1r", [16, n], b), ("v2", [16 * n], b), ("v2r", [64, n], b), ("e32", [64, n], b), ("e31", [64, n], b),
-                           ("d12", [320 * n], b), ("b12", [320 * n], b), ("d3", [1024 * n], b), ("cd", [84 * n], b), ("ht", [5 * n], b),
-                           ("M", [n], f), ("MI", [n], i4), ("ne", [n], f), ("cc", [3, n], i4), ("hi", [3 * n], i4), ("o16", [3 * n], u2),
-                           ("gm", [48 * n], f), ("sc", [48 * n], f), ("rl", [3 * n], u2), ("res", [n], f), ("wm", [3, n], f),
-                           ("w16", [3 * n], u2), ("ds", [n], f), ("s16", [n], u2), ("RG", [64 * n], b)):
+        for nm, sh, ty in (("PL", [128, STR[h]], i4), ("PT", [128 * STR[h]], i4), ("cR", [16 * n], f), ("cv", [16 * n], f), ("cs", [16 * n], f),
+                           ("cz", [64, n], i4), ("l2", [16 * n], u2), ("l3", [64 * n], u2), ("r1", [16, n], i4), ("e21", [16 * n], b),
+                           ("v1", [4 * n], b), ("v1r", [16, n], b), ("v2", [16 * n], b), ("v2r", [64, n], b), ("e32", [64, n], b),
+                           ("e31", [64, n], b), ("d12", [320 * n], b), ("b12", [320 * n], b), ("d3", [1024 * n], b), ("cd", [85 * n], b),
+                           ("ht", [5 * n], b), ("M", [n], f), ("MI", [n], i4), ("ne", [n], f), ("cc", [3, n], i4), ("hi", [3 * n], i4),
+                           ("o16", [3 * n], u2), ("gm", [48 * n], f), ("sc", [48 * n], f), ("rl", [3 * n], u2), ("res", [n], f),
+                           ("wm", [3, n], f), ("w16", [3 * n], u2), ("ds", [n], f), ("s16", [n], u2), ("RG", [64 * n], b)):
             d[nm + h] = (sh, ty)
     return d
 
@@ -46,6 +50,7 @@ for _k in BANKS:
     SCRATCH[_k] = (PS, [128, 512], "float32")
     SHAPES[_k] = ([512], "float32")
 SEMAPHORES = ["cV", "cA", "cP", "cG"] + ["m%d" % i for i in range(32)] + ["arr%d" % i for i in range(1, S)] + ["snt%d" % i for i in range(1, S)]
+PHYS = {"V": "V", "A": "A", "P": "P", "G": "G", "S": "S", "AD": "A", "N": "N"}
 ORDER = {}
 BITS = {}
 
@@ -57,6 +62,95 @@ def _bits(name, idx):
         m[idx] = True
         BITS[key] = (int.from_bytes(np.packbits(m.ravel()).tobytes(), "big"), int(m.sum()))
     return BITS[key]
+
+
+def _pieces(text):
+    out, a = [], 0
+    for x in text.split():
+        out.append((a, a + int(x[1:]), x[0]))
+        a += int(x[1:])
+    return out
+
+
+def _place(ops, pre, suc, pri):
+    N = len(ops)
+    left, st, fin = [len(p) for p in pre], [0.0] * N, [0.0] * N
+    busy, ready = {}, [i for i in range(N) if not left[i]]
+    while ready:
+        c = max(ready, key=lambda i: (pri[i], -i))
+        ready.remove(c)
+        q, du = PHYS[ops[c][0]], ops[c][4]
+        occ = 0.1 if ops[c][0] in ("S", "AD") else du
+        t = max([fin[j] + WAKE * need for j, need in pre[c].items()] + [0.0])
+        banks = {nm for nm, b in ops[c][2] + ops[c][3] if nm in BANKS}
+        moved = q != "N"
+        while moved:
+            moved = False
+            for a, b, e in reversed(busy.get(q, ())):
+                if b < t - 6.0:
+                    break
+                if a < t + occ - 1e-9 and t < b - 1e-9:
+                    t, moved = b, True
+            for nm in banks:
+                for a, b, e in reversed(busy.get(nm, ())):
+                    if b < t - 6.0:
+                        break
+                    if e != q and a < t + du + WAKE - 1e-9 and t < b + WAKE - 1e-9:
+                        t, moved = b + WAKE, True
+        st[c], fin[c] = t, t + du
+        for nm, e in [(q, t + occ)] + [(nm, t + du) for nm in banks]:
+            lst = busy.setdefault(nm, [])
+            k = len(lst)
+            while k and lst[k - 1][0] > t:
+                k -= 1
+            lst.insert(k, (t, e, q))
+        for k in suc[c]:
+            left[k] -= 1
+            if not left[k]:
+                ready.append(k)
+    return st, fin
+
+
+def _schedule(ops):
+    N = len(ops)
+    deps, hist = [{} for _ in range(N)], {}
+    for i, (q, fn, rd, wr, du, own) in enumerate(ops):
+        for isw, lst in ((0, rd), (1, wr)):
+            for nm, b in lst:
+                for j, w, a in hist.get(nm, ()):
+                    if j != i and a & b and (isw or w):
+                        deps[i][j] = deps[i].get(j, False) or q != ops[j][0] or q not in INORDER or (w and q != "P")
+        for isw, lst in ((0, rd), (1, wr)):
+            for nm, b in lst:
+                hh = hist.setdefault(nm, [])
+                if isw:
+                    hh[:] = [x for x in hh if x[0] == i or x[2] & ~b]
+                hh.append((i, isw, b))
+    succ = [{} for _ in range(N)]
+    for i in range(N):
+        for j, need in deps[i].items():
+            succ[j][i] = need
+    pri = [0.0] * N
+    for i in range(N - 1, -1, -1):
+        pri[i] = ops[i][4] + max([pri[k] + WAKE * need for k, need in succ[i].items()] + [0.0])
+    best = None
+    for _ in range(CFG["ROUNDS"]):
+        st, fin = _place(ops, deps, succ, pri)
+        if best is None or max(fin) < max(best[1]):
+            best = (st, fin)
+        pri = _place(ops, succ, deps, fin)[1]
+    st = best[0]
+    order = sorted(range(N), key=lambda i: (st[i], i))
+    runs = {}
+    for i in order:
+        q = PHYS[ops[i][0]]
+        for nm in {nm for nm, b in ops[i][2] + ops[i][3] if nm in BANKS}:
+            run = runs.setdefault(nm, [q, [], []])
+            if run[0] != q:
+                run[:] = [q, [], run[1]]
+            run[1].append(i)
+            deps[i].update((j, True) for j in run[2])
+    return order, deps, best[1]
 
 
 def rank_program(g, core, T, topo):
@@ -108,9 +202,9 @@ def rank_program(g, core, T, topo):
 
     def gat(o, win, off, q=None, f=A.subtract):
         if q is None:
-            op("A", lambda: ac.activation(o[0], win[0].indirect(off[0]), F.Copy), [win, off], [o], 0.065 + 1.56 * o[3] * CYC)
+            op("A", lambda: ac.activation(o[0], win[0].indirect(off[0]), F.Copy), [win, off], [o] + ([tok("ordA")] if o[1][:2] == "d3" else []), 0.065 + 1.56 * o[3] * CYC)
         else:
-            op("V", lambda: v.tensor_tensor(out=o[0], in0=win[0].indirect(off[0]), in1=q[0], op=f), [win, off, q], [o], 0.05 + 1.56 * o[3] * CYC)
+            op("V", lambda: v.tensor_tensor(out=o[0], in0=win[0].indirect(off[0]), in1=q[0], op=f), [win, off, q], [o] + ([tok("ordV")] if o[1][:2] == "d3" else []), 0.05 + 1.56 * o[3] * CYC)
 
     def scat(win, off, i):
         op("V", lambda: v.tensor_copy(win[0].indirect(off[0]), i[0]), [off, i], [win], 0.05 + 3.8 * i[3] * CYC)
@@ -121,13 +215,13 @@ def rank_program(g, core, T, topo):
     def iota(o, pat, base, cm=0):
         op("G", lambda: g.iota(o[0], pat, base, cm, allow_small_or_imprecise_dtypes=True), [], [o], 0.13 + 2 * o[3] * CYC)
 
-    def P(o, terms, start=True, stop=True):
+    def P(o, terms, start=True, stop=True, free=False):
         def run():
             for j, t in enumerate(terms):
                 i = pe.matmul((t[2] if len(t) > 2 else o)[0], t[0][0], t[1][0], start and j == 0, stop and j == len(terms) - 1)
             return i
         d = sum(max(64, t[1][3]) * (1 if two(t[1]) else 4) for t in terms) * PCYC
-        op("P", run, [x for t in terms for x in t[:2]] + ([] if start else [o]), [o], d)
+        op("P", run, [x for t in terms for x in t[:2]] + ([tok("open" + o[1])] if free else []), [o] + ([] if free else [tok("open" + o[1])]), d)
 
     nsem = [0]
 
@@ -171,9 +265,11 @@ def rank_program(g, core, T, topo):
     tt(TRS, TRS, BLK, A.mult)
     ts(R("MASK"), R("CR"), rcol, A.is_equal)
     ts(R("RST"), R("CR"), 0.0, A.is_gt)
-    ts(R("PEN"), R("CR", (0, 48)), rcol, A.is_gt, -64.0, A.mult)
+    pen = R("PEN", (96, 144))
+    ms(R("PEN", (0, 96)), 0.0)
+    ts(pen, R("CR", (0, 48)), rcol, A.is_gt, -64.0, A.mult)
     ts(R("JK", 0, (0, 48)), R("MASK", (0, 48)), -1.5, A.mult)
-    tt(R("PEN"), R("PEN"), R("JK", 0, (0, 48)), A.add)
+    tt(pen, pen, R("JK", 0, (0, 48)), A.add)
     P(R("B4", (0, 1)), [(BLK, R("WT"))])
     ts(thr, R("B4", (0, 1)), 300.0, A.mult, -2048.0, A.add)
     KK, KC = R("KF", 0), R("KF", 1)
@@ -187,20 +283,24 @@ def rank_program(g, core, T, topo):
     iota(R("RT"), [[16, 8]], 0)
     ts(R("RT"), R("RT"), rcol, A.add)
     ts(R("SD"), R("RT"), 128.0 - B24, A.add)
-    ms(R("GP"), 0.0)
+    ms(R("GPD"), 0.0)
+    ms(R("GPA"), 0.0)
+    ts(R("OL2"), R("CI"), g15, A.is_equal, 2048.0, A.mult)
+    ts(R("OLN"), R("CI"), g15, A.is_equal, -1024.0, A.mult)
     ms(R("SND"), 512.0)
     ms(R("X", (4096, XW)), 0.0)
     for h in "DA":
         n, o = NH[h], OFF[h]
-        for a, b, c in ((0, 4, 4), (4, 20, 16), (20, 84, 64)):
+        for a, b, c in ((0, 4, 4), (4, 20, 16), (21, 85, 64)):
             iota(R("cd" + h, (a * n, b * n)), [[STR[h], b - a], [0, n]], c * STR[h])
+        ms(R("cd" + h, (20 * n, 21 * n)), 0.0)
         iota(R("hi" + h), [[0, 3], [1, n]], 0)
         ms(R("PL" + h), 0)
         ms(R("PT" + h, (32 * STR[h], 64 * STR[h])), 0)
         for c, base in ((1, QC), (0, SPARE)):
             ts(R("PL" + h, c, (0, n)), R("RT", (o, o + n)), float(base), A.add)
 
-    UP = {"D": {"U0": 0, "U1": 480, "U2": 0, "t": 80, "up1": 400, "pre": 500}, "A": {"U0": 0, "U1": 4, "U2": 16, "t": 64, "up1": 256, "pre": 352}}
+    UP = {"D": {"U1": 480, "U2": 0, "t": 80, "up1": 400, "pre": 500}, "A": {"U1": 4, "U2": 16, "t": 64, "up1": 256, "pre": 352}}
 
     def chain(h, m, U, p, l):
         n = NH[h]
@@ -225,14 +325,30 @@ def rank_program(g, core, T, topo):
     def search(h, s):
         n, o, up = NH[h], OFF[h], UP[h]
         Un, Kn, PL = "U" + h, "K" + h, "PL" + h
+        tag = h + ("0" if s == 0 else "")
 
         def QX(a, b):
             if h == "A":
                 return R("QXA", (a, b))
             return R("QX0", (a, b)) if s == 0 else R("QXD", s - 1, (a, b))
 
-        def QXs(r, w):
-            return R("QXA", (r, 16 * w, 16))
+        def dist(dn, bn, b0, W, l, e):
+            d = R(dn, (b0, b0 + W))
+            if e == "V":
+                gat(d, XC, l, QX(0, W))
+                act(R(bn, (b0, b0 + W)), d, F.Abs)
+                return
+            if e == "Y":
+                gat(d, XC, l, QX(0, W))
+                ts(R("r3" + h, (b0, b0 + W)), d, 0.0, A.max)
+                return
+            gat(d, XC, l)
+            pc = W // -(-W // 512)
+            for x in range(0, W, pc):
+                zb[0] ^= 1
+                Z = R("Z%d" % zb[0], (0, pc))
+                P(Z, [(ID, R(dn, (b0 + x, b0 + x + pc))), (NID, QX(x, x + pc))])
+                act(R(bn, (b0 + x, b0 + x + pc)), Z, F.Abs)
         p1, p2 = R(PL, (4, 8), (0, n)), R(PL, (16, 32), (0, n))
         if h == "A":
             q = R("ARR", s - 1)
@@ -261,18 +377,22 @@ def rank_program(g, core, T, topo):
         up2 = R("KD", (432, 512)) if h == "D" else R(Un, (304, 352))
         U1 = R(Un, (up["U1"], up["U1"] + 4 * n))
         P(U1, [(IDF, uq(4))], True, False)
-        gat(R("d12" + h, (0, 64 * n)), XC, l1, QX(0, 64 * n))
+        dist("d12" + h, "b12" + h, 0, 64 * n, l1, "V")
         P(U1, sums("WL", "d12" + h, 0, 4 * n), False, True)
         chain(h, 4, U1, p2, R("l2" + h))
         ts(R("v1" + h), U1, thr, A.is_gt)
         for a in range(4):
             gcp(R("v1r" + h, (a, 16, 4)), R("v1" + h))
-        gat(R("d12" + h, (64 * n, 320 * n)), XC, R("l2" + h), QX(0, 256 * n))
+        u2, first = up["U2"], []
+        for a, b, e in _pieces(CFG["L2" + tag]):
+            dist("d12" + h, "b12" + h, 64 * n + 16 * n * a, 16 * n * (b - a), R("l2" + h, (a * n, b * n)), e)
+            part = R(Un, (u2 + a * n, u2 + b * n))
+            first.append((IDF, uq(b - a), part) if e == "V" else (NID, R("C2K", (0, (b - a) * n)), part))
         cp(up1, R("r1" + h))
         tt(R("e21" + h), p2, up1, A.is_equal)
         cp(up2, p2)
-        U2 = R(Un, (up["U2"], up["U2"] + 16 * n))
-        P(U2, [(IDF, uq(16)), (BIG, R("e21" + h)), (BIG, R("v1r" + h))], True, False)
+        U2 = R(Un, (u2, u2 + 16 * n))
+        P(U2, [(BIG, R("e21" + h)), (BIG, R("v1r" + h))] + first, True, False)
         P(U2, sums("WL", "d12" + h, 64 * n, 16 * n), False, True)
         chain(h, 16, U2, R(PL, (64, 128), (0, n)), R("l3" + h))
         for a, b in ((0, 32), (64, 128)):
@@ -285,31 +405,26 @@ def rank_program(g, core, T, topo):
             blk = R(PL, (64 + a, 128, 4), (0, n))
             tt(R("e32" + h, (a, 64, 4)), blk, up2, A.is_equal)
             tt(R("e31" + h, (a, 64, 4)), blk, up1, A.is_equal)
-        act(R("b12" + h), R("d12" + h), F.Abs)
-        k2 = R(Kn, (5 * n, 21 * n))
-        P(R(Kn, (n, 21 * n)), sums("OL", "b12" + h, 0, 20 * n) + [(NEG, R("e21" + h), k2), (NEG, R("v1r" + h), k2), (ID, R("cd" + h, (0, 20 * n)))])
-        ts(R("ht" + h, (0, 4 * n)), R(Kn, (n, 5 * n)), 1024.0, A.is_lt, -1.0, A.mult)
-        P(R(Kn, (0, n)), [(NEG, R("ht" + h, (a * n, a * n + n))) for a in range(5 if h == "A" else 4)])
-        for c0, c1 in KEY[h]:
-            for a, b, e in SEG[h]:
-                if not c0 <= a < c1:
-                    continue
-                b0, W = 16 * n * a, 16 * n * (b - a)
-                d, l = R("d3" + h, (b0, b0 + W)), R("l3" + h, (a * n, b * n))
-                if e == "V":
-                    gat(d, XC, l, QX(0, W))
-                    act(d, d, F.Abs)
-                else:
-                    gat(d, XC, l)
-                    pc = 480 if h == "D" else 384
-                    for x in range(0, W, pc):
-                        w = min(pc, W - x)
-                        zb[0] ^= 1
-                        Z, da = R("Z%d" % zb[0], (0, w)), R("d3" + h, (b0 + x, b0 + x + w))
-                        P(Z, [(ID, da), (NID, QX(x, x + w))])
-                        act(da, Z, F.Abs)
-            P(R(Kn, ((21 + c0) * n, (21 + c1) * n)), [(ID, R("cd" + h, ((20 + c0) * n, (20 + c1) * n)))] +
-              [(NEG, R(e + h, (c0, c1))) for e in ("e32", "e31", "v2r")] + sums("OL", "d3" + h, 16 * n * c0, (c1 - c0) * n))
+        k2 = R(Kn, (4 * n, 20 * n))
+        P(R(Kn, (0, 20 * n)), [(ID, R("cd" + h, (0, 20 * n))), (NEG, R("e21" + h), k2), (NEG, R("v1r" + h), k2)] + sums("OL", "b12" + h, 0, 20 * n))
+        P(R(Kn, (20 * n, 85 * n)), [(ID, R("cd" + h, (20 * n, 85 * n)))], True, False)
+        ts(R("ht" + h, (0, 4 * n)), R(Kn, (0, 4 * n)), 1024.0, A.is_lt, -1.0, A.mult)
+        P(R(Kn, (20 * n, 21 * n)), [(NEG, R("ht" + h, (a * n, a * n + n))) for a in range(5 if h == "A" else 4)], False, False, True)
+        for j, e in enumerate(("e32", "e31", "v2r")):
+            k3 = R(Kn, (21 * n, 85 * n))
+            P(k3[:2] + (0, 0), [(NEG, R(e + h))], False, False, True)
+        for a, b, e in _pieces(CFG["L3" + tag]):
+            dist("d3" + h, "d3" + h, 16 * n * a, 16 * n * (b - a), R("l3" + h, (a * n, b * n)), e)
+        c0 = 0
+        kind = {a: e for a, b, e in _pieces(CFG["L3" + tag])}
+        for m in CFG["KEY" + tag]:
+            c1 = c0 + m
+            if kind[c0] == "Y":
+                t = sums("OLN", "d3" + h, 16 * n * c0, m * n) + sums("OL2", "r3" + h, 16 * n * c0, m * n)
+            else:
+                t = sums("OL", "d3" + h, 16 * n * c0, m * n)
+            P(R(Kn, ((21 + c0) * n, (21 + c1) * n)), t, False, c1 == 64, c1 < 64)
+            c0 = c1
 
     def tail(h, s, last):
         n, o, st = NH[h], OFF[h], STR[h]
@@ -320,10 +435,14 @@ def rank_program(g, core, T, topo):
         cp(R("MI" + h), M)
         for k in range(3):
             ts(R("cc" + h, k), R("MI" + h), 2 * k, A.arith_shift_right, ((128 >> 2 * k) - 1) * st, A.bitwise_and)
-        tt(R("cc" + h), R("cc" + h), R("hi" + h), A.add)
-        cp(R("o16" + h), R("cc" + h))
+        if last:
+            for i in range(n):
+                ts(R("o16" + h, (i, 3 * n, n)), R("cc" + h, sl(None), i), float(i), A.add)
+        else:
+            tt(R("cc" + h), R("cc" + h), R("hi" + h), A.add)
+            cp(R("o16" + h), R("cc" + h))
         gat(R("gm" + h), R("PT" + h), R("o16" + h), R("MASK", (0, w)), A.mult)
-        sp = R("B4" if h == "D" else "B5", (0, w))
+        sp = R("B4", (0, w)) if h == "D" else R("KA", (256, 256 + w))
         P(sp, [(BLKF, R("gm" + h))])
         cp(R("SP", sl(None), (16 * o, 16 * (o + n))), sp)
         a, b, c = R(sc), R("RST", (0, w)), R("gm" + h)
@@ -333,25 +452,37 @@ def rank_program(g, core, T, topo):
         ts(R("ne" + h), M, THR, A.is_lt, 0.5, A.subtract)
         for i in range(n):
             gi = o + i
-            e = eb[0] = (eb[0] + 1) % 3
-            for k in range(3):
-                ts(R("EQ", e, k, sl(None), (0, 16 * gi + 16)), R("SP", sl(None), (0, 16 * gi + 16)), R(sc, (16 * (k * n + i) + 15, 16 * (k * n + i) + 16)), A.is_equal)
-            Zn, z0 = ("B4", "B5")[gi % 2], 256
-            wo = 48 * min(gi, 2)
-            if gi:
-                P(R(Zn, (z0, z0 + wo)), [(BIG, R("EQ", e, k, sl(None), (16 * j, 16 * min(j + 2, gi))), R(Zn, (z0, z0 + 48 * (min(j + 2, gi) - j))))
-                                         for j in range(0, gi, 2) for k in range(3)])
-            P(R(Zn, (z0 + wo, z0 + wo + 48)), [(BIG, R("PEN"))] + [(BIG, R("EQ", e, k, sl(None), (16 * gi, 16 * gi + 16))) for k in range(3)])
-            Z = R(Zn, (z0, z0 + wo + 48))
-            jb[0] = (jb[0] + 1) % 4
-            act(R("JK", jb[0], (0, wo + 48)), Z, F.Relu, accum_out=R("res" + h, (i, i + 1)))
+            Zn, wo = CFG["FOLD" + h][i], 48 * min(gi, 2)
+            Z = R(Zn, (352 - wo, 400))
+            P(Z, [(BIG, R("PEN", (96 - wo, 144)))], True, False)
+            for b0, b1 in ((0, o), (o, gi + 1)) if o else ((0, gi + 1),):
+                for k in range(3):
+                    x = 16 * (k * n + i) + 15
+                    ts(R("EQ" + h, i, k, sl(None), (16 * b0, 16 * b1)), R("SP", sl(None), (16 * b0, 16 * b1)), R(sc, (x, x + 1)), A.is_equal)
+                    t = [(BIG, R("EQ" + h, i, k, sl(None), (16 * j, 16 * min(j + 2, b1, gi))), R(Zn, (352 - 48 * (min(j + 2, b1, gi) - j), 352)))
+                         for j in range(b0, min(b1, gi), 2)]
+                    if b1 > gi:
+                        t.append((BIG, R("EQ" + h, i, k, sl(None), (16 * gi, 16 * gi + 16)), R(Zn, (352, 400))))
+                    P(Z, t, False, b1 > gi and k == 2)
+            if CFG["RED" + h][i] == "V":
+                red(R("res" + h, (i, i + 1)), Z)
+            else:
+                jb[0] = (jb[0] + 1) % 4
+                act(R("JK", jb[0], (0, wo + 48)), Z, F.Relu, accum_out=R("res" + h, (i, i + 1)))
         res = R("res" + h)
         if s < S - 1:
-            gone, p4 = R("GP", (8 + o, 8 + o + n)), R("U" + h, (UP[h]["pre"], UP[h]["pre"] + n))
+            gone, p4 = R("GP" + h, (2 * n - 2, 3 * n - 2)), R("U" + h, (UP[h]["pre"], UP[h]["pre"] + n))
             tt(gone, res, R("ne" + h), A.is_lt)
-            P(p4, [(TRS, gone), (NEG, gone)] + [(BLK, R("GP", (8 + o - x, 8 + o + n - x))) for x in range(1, o + n)])
-            tt(R("ds" + h), p4, R("SD", (o, o + n)), A.min)
-            ts(R("s16" + h), R("ds" + h), B24, A.add)
+            if o:
+                P(p4, [(BLK, R("GPD", (x, x + n))) for x in range(6, 13)], True, False)
+            P(p4, [(TRS, gone), (NEG, gone)] + [(BLK, R("GP" + h, (2 * n - 2 - x, 3 * n - 2 - x))) for x in range(1, n)], not o, True)
+            if last:
+                for i in range(n):
+                    x = UP[h]["pre"] + i
+                    ts(R("s16" + h, (i, i + 1)), R("U" + h, (x, x + 1)), R("SD", (o + i, o + i + 1)), A.min, B24, A.add)
+            else:
+                tt(R("ds" + h), p4, R("SD", (o, o + n)), A.min)
+                ts(R("s16" + h), R("ds" + h), B24, A.add)
             scat(R("SND"), R("s16" + h), R("RG" + h, (0, 16 * n)))
         for k in range(3):
             tt(R("wm" + h, k), R(sc, (16 * k * n + 15, 16 * (k + 1) * n, 16)), res, A.add)
@@ -393,76 +524,24 @@ def rank_program(g, core, T, topo):
     DMA("AD", [(T.y[:, 2048:4096], T.X[:, 2048:4096])], [R("X", (2048, 4096))], [tok("y2")], 4.0)
 
     eng = {"V": v, "A": ac, "P": pe, "G": g, "S": g.sync, "AD": ac}
-    phys = {"V": "V", "A": "A", "P": "P", "G": "G", "S": "S", "AD": "A", "N": "N"}
     N = len(ops)
     if "o" not in ORDER:
-        deps = [dict() for _ in range(N)]
-        hist, runs = {}, {}
-        for i, (q, fn, rd, wr, du, own) in enumerate(ops):
-            for isw, lst in ((0, rd), (1, wr)):
-                for nm, b in lst:
-                    for j, w, a in hist.get(nm, ()):
-                        if j != i and a & b and (isw or w):
-                            deps[i][j] = True
-                    if nm in BANKS:
-                        run = runs.setdefault(nm, [q, [], []])
-                        if run[0] != q:
-                            run[:] = [q, [], run[1]]
-                        run[1].append(i)
-                        for j in run[2]:
-                            deps[i][j] = True
-            for isw, lst in ((0, rd), (1, wr)):
-                for nm, b in lst:
-                    hh = hist.setdefault(nm, [])
-                    if isw:
-                        hh[:] = [x for x in hh if x[0] == i or x[2] & ~b]
-                    hh.append((i, isw, b))
-        succ = [[] for _ in range(N)]
-        for i in range(N):
-            for j in deps[i]:
-                succ[j].append(i)
-        pri, left, rt, fin = [0.0] * N, [len(d) for d in deps], [0.0] * N, [0.0] * N
-        for i in range(N - 1, -1, -1):
-            pri[i] = ops[i][4] + max([pri[k] + WAKE for k in succ[i]] + [0.0])
-        ready, free, order = {}, {}, []
-        for i in range(N):
-            if not left[i]:
-                ready.setdefault(phys[ops[i][0]], []).append(i)
-        while len(order) < N:
-            best = None
-            for q, lst in ready.items():
-                if lst:
-                    f = free.get(q, 0.0) if q != "N" else 0.0
-                    t0 = min(max(f, rt[i]) for i in lst)
-                    c = max((i for i in lst if max(f, rt[i]) <= t0 + 0.03), key=lambda i: (pri[i], -i))
-                    t = max(f, rt[c])
-                    if best is None or t < best[0]:
-                        best = (t, c, q)
-            t, c, q = best
-            ready[q].remove(c)
-            order.append(c)
-            free[q] = t + (ops[c][4] if ops[c][0] not in ("S", "AD") else 0.1)
-            fin[c] = t + ops[c][4]
-            for k in succ[c]:
-                left[k] -= 1
-                rt[k] = max(rt[k], fin[c] + WAKE)
-                if not left[k]:
-                    ready.setdefault(phys[ops[k][0]], []).append(k)
-        ORDER["o"], ORDER["d"], ORDER["fin"], ORDER["ops"] = order, deps, fin, ops
+        ORDER["o"], ORDER["d"], ORDER["fin"] = _schedule(ops)
+        ORDER["ops"] = ops
     deps = ORDER["d"]
     cnt = {"V": 0, "A": 0, "P": 0, "G": 0}
     val, snap = [None] * N, [{} for _ in range(N)]
     know = {q: {} for q in "VAPGS"}
     for i in ORDER["o"]:
         q, fn, rd, wr, du, own = ops[i]
-        p = phys[q]
+        p = PHYS[q]
         if p == "N":
             val[i] = own
             continue
         kn, want = know[p], {}
-        for j in deps[i]:
+        for j, need in deps[i].items():
             sem, c = val[j]
-            if kn.get(sem, 0) < c:
+            if need and kn.get(sem, 0) < c:
                 want[sem] = max(want.get(sem, (0, 0)), (c, j))
         for sem in sorted(want, key=lambda k: -want[k][1]):
             c, j = want[sem]

@@ -2,54 +2,57 @@ import numpy as np
 from concourse.mybir import AluOpType as A, AxisListType, ActivationFunctionType as F
 
 S, C = 6, 48
-NH = {"D": 5, "A": 3}
-OFF = {"D": 0, "A": 5}
-STR = {"D": 8, "A": 4}
+NM = 5
+STR = 8
 QC, SPARE, DUMPX, XW = 4096, 4224, 4352, 4736
 B24, B22 = float(1 << 24), float(1 << 22)
 THR = 4090.0 * 1024
 CM = 1.5 * 2.0 ** 35
-CFG = {"L2D": "V8 A8", "L2A": "V16", "L3D": "A8 V8 A8 V8 A8 V8 Y8 Y8", "L3A": "A10 V12 A10 V12 V10 V10",
-       "L2D0": "V8 A8", "L3D0": "A8 V8 A8 V8 A8 V8 Y8 Y8",
-       "KEYD": (16, 16, 16, 16), "KEYA": (22, 22, 20), "KEYD0": (16, 16, 16, 16), "ROUNDS": 2,
-       "FOLDD": ("B5", "B4", "B5", "B4", "B5"), "FOLDA": ("B4", "B5", "Z0"), "REDD": "AAAAA", "REDA": "AAV"}
+CFG = {"ND": 5, "ND0": 4, "L2D": "V8 A8", "L2A": "V8 A8", "L3D": "A8 V8 A8 V8 V8 A8 V8 V8", "L3A": "A10 V12 A10 V6 V6 V6 V6 V8",
+       "L2D0": "V8 A8", "L3D0": "A10 V12 A10 V12 V10 V10", "L2A0": "V8 A8", "L3A0": "V16 A16 V16 V16", "KEYA0": (64,),
+       "KEYD": (24, 24, 16), "KEYA": (22, 22, 20), "KEYD0": (22, 22, 20), "ROUNDS": 2, "SQ": 20, "S2": 999, "ONE": 12, "L1D": "A4", "L1A": "A4",
+       "AMIN": 64, "CUTD": (0, 16, 40, 64), "CUTA": (0, 64), "LGD": 1, "LGA": 0, "TUNE": 230, "PAD": 0, "SPLIT": 3, "FL": 1, "UP": 0,
+       "ACP": ("w16D", "o16D", "rlD", "l1D"), "ANDU": 0, "W1": 0, "LIFT": {}, "TV": 12, "SEED": 0, "NK": 2, "SD": 1.5,
+       "FINE": 0, "SF": 1, "FOLDD": ("B5", "B4", "B5", "B4", "B5"), "FOLDA": ("B4", "B5", "Z0", "Z1", "B4"), "REDD": "AAAAA", "REDA": "AAV"}
 SB, PS = "sbuf", "psum"
-CYC, PCYC, WAKE, AFIX = 0.00095, 0.00045, 0.2, 0.06
+CYC, PCYC, WAKE, AFIX, VFIX = 0.00095, 0.00053, 0.2, 0.005, 0.005
+RANGE = ((0.14, 1.0, 1.0, 1.0, 1.0, 0, 0, 3.5, 194), (0.14, 0.92, 0.92, 0.82, 1.3, 0, 0, 2.4, 172), (0.06, 1.1, 1.08, 0.86, 1.4, 0, 0, 2.5, 198),
+         (0.26, 0.9, 1.03, 0.9, 1.0, 0, 0, 3.0, 202), (0.25, 0.88, 0.92, 0.78, 1.1, 0, 0, 5.0, 197), (0.08, 1.25, 0.95, 1.28, 1.4, 0, 0, 2.5, 249))
 INORDER = "VAP"
+HEAD = ("cRA", "cvA", "csA", "ctA", "czA", "PLA", "l1A", "l2A", "l3A", "d12A", "UA", "QXA", "UQA", "e21A", "v1A", "v1rA", "r1A")
 
 
 def _shapes():
     b, f, i4, u2 = "bfloat16", "float32", "int32", "uint16"
-    d = {"X": ([XW], b), "QS": ([480], b), "QX0": ([1280], b), "QXD": ([5, 1280], b), "QXA": ([768], b), "WT": ([1], b), "KI": ([4], i4),
-         "KF": ([4, 4], f), "WL": ([144], b), "OL": ([144], b), "CI": ([144], f), "CR": ([240], f), "MASK": ([240], f), "RST": ([240], f),
-         "PI": ([8], i4), "PF": ([8], f), "PEN": ([144], b), "C2K": ([80], b), "DUMP": ([24], f), "RT": ([8], f), "SD": ([8], f),
-         "GPD": ([16], b), "GPA": ([8], b), "SND": ([256], b), "JK": ([4, 144], b), "ARR": ([5, C], b), "SP": ([3, 128], u2),
-         "EQD": ([5, 3, 3, 80], b), "EQA": ([3, 3, 3, 128], b), "r3D": ([1024 * 5], b), "r3A": ([1024 * 3], b), "OL2": ([144], b), "OLN": ([144], b),
-         "UQD": ([16, 30], f), "UQA": ([16, 3], f), "p1D": ([24, 5], i4), "l1D": ([120], u2), "l1A": ([12], u2)}
-    for k in ("ID", "NID", "NEG", "BIG", "BLK", "TRS"):
-        d[k] = ([128], b)
-    for k in ("IDF", "BLKF"):
-        d[k] = ([128], f)
+    n = NM
+    d = {"X": ([XW], b), "QS": ([480], b), "QX0": ([1280], b), "QXD": ([5, 1280], b), "QXA": ([1280], b), "WT": ([1], b), "KI": ([4], i4),
+         "KF": ([4, 4], f), "ST": ([4, 144], b), "MB": ([7, 128], b), "MF": ([2, 128], f), "CI": ([144], f), "CR": ([240], f), "MASK": ([240], f),
+         "RST": ([240], f), "PI": ([8], i4), "PF": ([8], f), "PEN": ([144], b), "C2K": ([80], b), "DUMP": ([24], f), "RT": ([8], f), "SD": ([8], f),
+         "GPD": ([24], b), "GPA": ([16], b), "SND": ([256], b), "JK": ([4, 144], b), "ARR": ([5, C], b), "SP": ([3, 128], u2),
+         "EQD": ([5, 3, 3, 80], b), "EQA": ([5, 3, 3, 128], b), "UQD": ([16, 30], f), "UQA": ([16, n], f), "p1D": ([24, 5], i4),
+         "l1D": ([120], u2), "l1A": ([4 * n], u2), "cd": ([85, n], b), "hi": ([3, n], i4)}
     for h in "DA":
-        n = NH[h]
-        for nm, sh, ty in (("PL", [128, STR[h]], i4), ("PT", [128 * STR[h]], i4), ("cR", [16 * n], f), ("cv", [16 * n], f), ("cs", [16 * n], f),
-                           ("cz", [64, n], i4), ("l2", [16 * n], u2), ("l3", [64 * n], u2), ("r1", [16, n], i4), ("e21", [16 * n], b),
-                           ("v1", [4 * n], b), ("v1r", [16, n], b), ("v2", [16 * n], b), ("v2r", [64, n], b), ("e32", [64, n], b),
-                           ("e31", [64, n], b), ("d12", [320 * n], b), ("b12", [320 * n], b), ("d3", [1024 * n], b), ("cd", [85 * n], b),
-                           ("ht", [5 * n], b), ("M", [n], f), ("MI", [n], i4), ("ne", [n], f), ("cc", [3, n], i4), ("hi", [3 * n], i4),
-                           ("o16", [3 * n], u2), ("gm", [48 * n], f), ("sc", [48 * n], f), ("rl", [3 * n], u2), ("res", [n], f),
-                           ("wm", [3, n], f), ("w16", [3 * n], u2), ("ds", [n], f), ("s16", [n], u2), ("RG", [64 * n], b)):
+        for nm, sh, ty in (("PL", [128, STR], i4), ("PT", [128 * STR], i4), ("cR", [16 * n], f), ("cv", [16 * n], f), ("cs", [16 * n], f),
+                           ("cz", [64, n], i4), ("ct", [2, 16, n], f), ("l2", [16 * n], u2), ("l3", [64 * n], u2), ("r1", [16, n], f),
+                           ("r2", [16 * n], f), ("e21", [16 * n], b), ("v1", [4 * n], b), ("v1r", [16, n], b), ("v2", [16 * n], b),
+                           ("v2r", [64, n], b), ("e32", [64, n], b), ("e31", [64, n], b), ("d12", [320 * n], b), ("b12", [320 * n], b),
+                           ("d3", [1024 * n], b), ("r3", [1024 * n], b), ("ht", [5 * n], b), ("MI", [n], i4), ("ne", [n], f),
+                           ("cc", [3, n], i4), ("o16", [3 * n + 1], u2), ("gm", [48 * n], f), ("sc", [48 * n], f), ("rl", [3 * n + 1], u2),
+                           ("res", [n], f), ("wm", [3, n], f), ("w16", [3 * n + 1], u2), ("ds", [n], f), ("s16", [n + 1], u2), ("RG", [64 * n], b)):
             d[nm + h] = (sh, ty)
     return d
 
 
 SHAPES = _shapes()
+PART = {k: (buf, i) for buf, ks in (("ST", ("WL", "OL", "OL2", "OLN")), ("MB", ("ID", "NID", "NEG", "BIG", "BLK", "TRS", "POS")), ("MF", ("IDF", "BLKF")))
+        for i, k in enumerate(ks)}
 BANKS = ("UD", "UA", "KD", "KA", "B4", "B5", "Z0", "Z1")
+APART = BANKS + ("either",)
 SCRATCH = {k: (SB, [128] + sh, ty) for k, (sh, ty) in SHAPES.items()}
 for _k in BANKS:
     SCRATCH[_k] = (PS, [128, 512], "float32")
     SHAPES[_k] = ([512], "float32")
-SEMAPHORES = ["cV", "cA", "cP", "cG"] + ["m%d" % i for i in range(32)] + ["arr%d" % i for i in range(1, S)] + ["snt%d" % i for i in range(1, S)]
+SEMAPHORES = ["cV", "cA", "cP", "cG"] + ["m%d" % i for i in range(34)] + ["arr%d" % i for i in range(1, S)] + ["snt%d" % i for i in range(1, S)]
 PHYS = {"V": "V", "A": "A", "P": "P", "G": "G", "S": "S", "AD": "A", "N": "N"}
 ORDER = {}
 BITS = {}
@@ -82,7 +85,7 @@ def _place(ops, pre, suc, pri):
         q, du = PHYS[ops[c][0]], ops[c][4]
         occ = 0.1 if ops[c][0] in ("S", "AD") else du
         t = max([fin[j] + WAKE * need for j, need in pre[c].items()] + [0.0])
-        banks = {nm for nm, b in ops[c][2] + ops[c][3] if nm in BANKS}
+        banks = {nm for nm, b in ops[c][2] + ops[c][3] if nm in APART}
         moved = q != "N"
         while moved:
             moved = False
@@ -111,15 +114,15 @@ def _place(ops, pre, suc, pri):
     return st, fin
 
 
-def _schedule(ops):
+def _schedule(ops, kind):
     N = len(ops)
     deps, hist = [{} for _ in range(N)], {}
-    for i, (q, fn, rd, wr, du, own) in enumerate(ops):
+    for i, (q, fn, rd, wr, du, own, cat) in enumerate(ops):
         for isw, lst in ((0, rd), (1, wr)):
             for nm, b in lst:
                 for j, w, a in hist.get(nm, ()):
                     if j != i and a & b and (isw or w):
-                        deps[i][j] = deps[i].get(j, False) or q != ops[j][0] or q not in INORDER or (w and q != "P")
+                        deps[i][j] = deps[i].get(j, False) or q != ops[j][0] or q not in INORDER or (w and q != "P" and nm in SHAPES)
         for isw, lst in ((0, rd), (1, wr)):
             for nm, b in lst:
                 hh = hist.setdefault(nm, [])
@@ -133,24 +136,60 @@ def _schedule(ops):
     pri = [0.0] * N
     for i in range(N - 1, -1, -1):
         pri[i] = ops[i][4] + max([pri[k] + WAKE * need for k, need in succ[i].items()] + [0.0])
-    best = None
+    pri = [pri[i] + CFG["LIFT"].get(kind[i][2], 0.0) for i in range(N)]
+    best, pri0, now = None, pri, 1e9
     for _ in range(CFG["ROUNDS"]):
         st, fin = _place(ops, deps, succ, pri)
         if best is None or max(fin) < max(best[1]):
-            best = (st, fin)
+            best, pri0 = (st, fin), pri
         pri = _place(ops, succ, deps, fin)[1]
-    st = best[0]
-    order = sorted(range(N), key=lambda i: (st[i], i))
-    runs = {}
-    for i in order:
-        q = PHYS[ops[i][0]]
-        for nm in {nm for nm, b in ops[i][2] + ops[i][3] if nm in BANKS}:
-            run = runs.setdefault(nm, [q, [], []])
-            if run[0] != q:
-                run[:] = [q, [], run[1]]
-            run[1].append(i)
-            deps[i].update((j, True) for j in run[2])
-    return order, deps, best[1]
+    durs = [[_under(m, o) for o in ops] for m in RANGE]
+    apart = [{nm for nm, b in o[2] + o[3] if nm in APART} for o in ops]
+
+    def settle(st):
+        order, runs, more = sorted(range(N), key=lambda i: (st[i], i)), {}, [()] * N
+        for i in order:
+            q = PHYS[ops[i][0]]
+            for nm in apart[i]:
+                run = runs.setdefault(nm, [q, [], []])
+                if run[0] != q:
+                    run[:] = [q, [], run[1]]
+                run[1].append(i)
+                more[i] = more[i] + tuple(run[2])
+        ends = []
+        for m, du in zip(RANGE, durs):
+            fin, free, wk = [0.0] * N, {}, m[0]
+            for i in order:
+                q = PHYS[ops[i][0]]
+                t = max([fin[j] + wk * need for j, need in deps[i].items()] + [fin[j] + wk for j in more[i]] + [free.get(q, 0.0) if q != "N" else 0.0])
+                fin[i] = t + du[i]
+                free[q] = t + (0.1 if ops[i][0] in ("S", "AD") else du[i])
+            ends.append(max(fin))
+        rel = [100.0 * e / m[8] for e, m in zip(ends, RANGE)]
+        return (sum(rel) / len(rel) + max(rel)) / 2, order, more, ends
+
+    kinds, rng = sorted(set(kind)), np.random.default_rng(CFG["SEED"])
+    lift, now = {k: 0.0 for k in kinds}, settle(best[0]) + (best[1],)
+    for _ in range(CFG["TUNE"]):
+        trial = dict(lift)
+        for k in rng.choice(len(kinds), CFG["NK"]):
+            trial[kinds[k]] += float(rng.normal(0.0, CFG["SD"]))
+        st, fin = _place(ops, deps, succ, [pri0[i] + trial[kind[i]] for i in range(N)])
+        if max(fin) < 1.03 * max(now[4]):
+            new = settle(st) + (fin,)
+            if new[0] <= now[0]:
+                now, lift = new, trial
+    for i in range(N):
+        deps[i].update((j, True) for j in now[2][i])
+    ORDER["mean"], ORDER["ends"] = now[0], now[3]
+    return now[1], deps, now[4]
+
+
+def _under(m, o):
+    f, du, cat = m[1], o[4], o[6]
+    if cat in "gs":
+        return 0.06 + (du - 0.06) * f * m[3 + (cat == "s")]
+    return {"V": du * f, "A": du * f + m[6], "P": du * f * m[2], "G": du * f + m[5], "N": m[7]}.get(cat, du)
 
 
 def rank_program(g, core, T, topo):
@@ -160,8 +199,11 @@ def rank_program(g, core, T, topo):
     v, ac, pe = g.vector, g.scalar, g.tensor
     ops = []
     sl = slice
+    kind, seen, phase = [], {}, [""]
 
     def R(name, *idx):
+        if name in PART:
+            name, idx = PART[name][0], (PART[name][1],) + idx
         idx = tuple(sl(*x) if isinstance(x, tuple) else x for x in idx) or (sl(None),) * len(SHAPES[name][0])
         b, n = _bits(name, idx)
         return (T[name][(sl(None),) + idx], name, b, n)
@@ -169,8 +211,12 @@ def rank_program(g, core, T, topo):
     def tok(name):
         return (None, name, 1, 0)
 
-    def op(q, fn, rd, wr, dur, own=None):
-        ops.append((q, fn, [(x[1], x[2]) for x in rd if isinstance(x, tuple)], [(x[1], x[2]) for x in wr], dur, own))
+    def op(q, fn, rd, wr, dur, own=None, cat=None):
+        dur += VFIX * (q == "V" and cat is None)
+        k = (q, wr[0][1] if wr else "", phase[0])
+        seen[k] = seen.get(k, 0) + 1
+        kind.append(k + ((seen[k],) if CFG["FINE"] else ()))
+        ops.append((q, fn, [(x[1], x[2]) for x in rd if isinstance(x, tuple)], [(x[1], x[2]) for x in wr], dur, own, cat or q))
 
     def two(*xs):
         return all(SHAPES[x[1]][1] in ("bfloat16", "uint16") for x in xs)
@@ -187,6 +233,8 @@ def rank_program(g, core, T, topo):
         op("V", lambda: v.tensor_tensor(out=o[0], in0=a[0], in1=b[0], op=f), [a, b], [o], max(64, c * a[3]) * CYC)
 
     def cp(o, i):
+        if o[1] in CFG["ACP"]:
+            return gcp(o, i)
         op("V", lambda: v.tensor_copy(o[0], i[0]), [i], [o], max(64, i[3] / (2 if two(o, i) else 1)) * CYC)
 
     def ms(o, c):
@@ -198,19 +246,19 @@ def rank_program(g, core, T, topo):
     def act(o, i, f, **k):
         a = {x: val_(y) for x, y in k.items()}
         acc = [k["accum_out"]] if "accum_out" in k else []
-        op("A", lambda: ac.activation(o[0], i[0], f, **a), [i, k.get("bias"), k.get("scale")], [o] + acc, max(64, i[3]) * CYC + AFIX + 0.02 * len(acc))
+        op("A", lambda: ac.activation(o[0], i[0], f, **a), [i, k.get("bias"), k.get("scale")], [o] + acc, max(CFG["AMIN"], i[3]) * CYC + AFIX + 0.02 * len(acc))
 
     def gat(o, win, off, q=None, f=A.subtract):
         if q is None:
-            op("A", lambda: ac.activation(o[0], win[0].indirect(off[0]), F.Copy), [win, off], [o] + ([tok("ordA")] if o[1][:2] == "d3" else []), 0.065 + 1.56 * o[3] * CYC)
+            op("A", lambda: ac.activation(o[0], win[0].indirect(off[0]), F.Copy), [win, off], [o] + ([tok("ordA")] if o[1][:2] == "d3" else []), 0.065 + 1.56 * o[3] * CYC, None, "g")
         else:
-            op("V", lambda: v.tensor_tensor(out=o[0], in0=win[0].indirect(off[0]), in1=q[0], op=f), [win, off, q], [o] + ([tok("ordV")] if o[1][:2] == "d3" else []), 0.05 + 1.56 * o[3] * CYC)
+            op("V", lambda: v.tensor_tensor(out=o[0], in0=win[0].indirect(off[0]), in1=q[0], op=f), [win, off, q], [o] + ([tok("ordV")] if o[1][:2] == "d3" else []), 0.05 + 1.56 * o[3] * CYC, None, "g")
 
-    def scat(win, off, i):
-        op("V", lambda: v.tensor_copy(win[0].indirect(off[0]), i[0]), [off, i], [win], 0.05 + 3.8 * i[3] * CYC)
+    def scat(win, off, i, after=None):
+        op("V", lambda: v.tensor_copy(win[0].indirect(off[0]), i[0]), [off, i], [win] + ([(None, after, int(after != "either"), 0)] if after else []), 0.05 + 3.8 * i[3] * CYC, None, "s")
 
-    def gcp(o, i):
-        op("G", lambda: g.affine_select(o[0], i[0], [[0, i[3]]], A.is_gt, 0.0, 1, 0), [i], [o], 0.17 + 2 * i[3] * CYC)
+    def gcp(o, i, also=[]):
+        op("G", lambda: g.affine_select(o[0], i[0], [[0, i[3]]], A.is_gt, 0.0, 1, 0), [i], [o] + also, 0.2 + 2 * i[3] * CYC)
 
     def iota(o, pat, base, cm=0):
         op("G", lambda: g.iota(o[0], pat, base, cm, allow_small_or_imprecise_dtypes=True), [], [o], 0.13 + 2 * o[3] * CYC)
@@ -238,10 +286,10 @@ def rank_program(g, core, T, topo):
         return [(R(L, (15 - r, 143 - r)), R(b, (b0 + r, b0 + 16 * w, 16))) for r in range(16)]
 
     ID, NID, NEG, BIG, BLK, TRS, IDF, BLKF = [R(k) for k in ("ID", "NID", "NEG", "BIG", "BLK", "TRS", "IDF", "BLKF")]
-    XC = R("X", (0, 4096))
+    XC, POS = R("X", (0, 4096)), R("POS")
 
     DMA("S", [(T.QS[:, :], T.qs[:, :]), (T.WT[:, :], T.wt[:, :]), (T.KI[:, :], T.kk[:, :])], [], [R("QS"), R("WT"), R("KI")], 2.5)
-    DMA("AD", [(XC[0], T.x0[:, :])], [], [XC, tok("X0D")], 6.0)
+    DMA("AD", [(XC[0], T.x0[:, :])], [], [XC, tok("X0D")], 4.8)
     iota(R("PI", (0, 1)), [[0, 1]], 0, 1)
     iota(R("CI"), [[1, 144]], 0)
     iota(R("CR"), [[0, 15], [1, 16]], 0)
@@ -254,7 +302,7 @@ def rank_program(g, core, T, topo):
     ts(R("WL"), R("CI"), g15, A.is_equal, R("PF", (5, 6)), A.mult)
     ts(R("OL"), R("CI"), g15, A.is_equal, 1024.0, A.mult)
     ci = R("CI", (0, 128))
-    for k, c in ((NID, -1.0), (ID, 1.0), (IDF, 1.0), (NEG, -B24), (BIG, B22)):
+    for k, c in ((NID, -1.0), (ID, 1.0), (IDF, 1.0), (NEG, -B24), (BIG, B22), (POS, B24)):
         ts(k, ci, pcol, A.is_equal, c, A.mult)
     ms(R("C2K"), 2048.0)
     ts(BLKF, ci, gcol, A.is_ge)
@@ -271,7 +319,19 @@ def rank_program(g, core, T, topo):
     ts(R("JK", 0, (0, 48)), R("MASK", (0, 48)), -1.5, A.mult)
     tt(pen, pen, R("JK", 0, (0, 48)), A.add)
     P(R("B4", (0, 1)), [(BLK, R("WT"))])
-    ts(thr, R("B4", (0, 1)), 300.0, A.mult, -2048.0, A.add)
+    rs, rb = R("PF", (6, 7)), R("PF", (7, 8))
+    if CFG["FL"]:
+        ts(thr, R("B4", (0, 1)), 200.0, A.mult)
+        op("V", lambda: v.reciprocal(rs[0], thr[0]), [thr], [rs], 0.2)
+        ts(rb, rs, 2048.0, A.mult, -1.5, A.add)
+    else:
+        ts(rb, R("B4", (0, 1)), 300.0, A.mult, -2048.0, A.add)
+
+    def empty(o, U):
+        if CFG["FL"]:
+            act(o, U, F.Relu, scale=rs, bias=rb)
+        else:
+            ts(o, U, rb, A.is_gt)
     KK, KC = R("KF", 0), R("KF", 1)
     ts(KK, R("KI"), 1920.5, A.is_gt, -4096.0, A.mult)
     tt(KK, KK, R("KI"), A.add)
@@ -283,49 +343,84 @@ def rank_program(g, core, T, topo):
     iota(R("RT"), [[16, 8]], 0)
     ts(R("RT"), R("RT"), rcol, A.add)
     ts(R("SD"), R("RT"), 128.0 - B24, A.add)
-    ms(R("GPD"), 0.0)
     ms(R("GPA"), 0.0)
-    ts(R("OL2"), R("CI"), g15, A.is_equal, 2048.0, A.mult)
-    ts(R("OLN"), R("CI"), g15, A.is_equal, -1024.0, A.mult)
+    if CFG["PAD"]:
+        ms(R("r3A", (0, 320)), 0.0)
+    if any("Y" in CFG[k] for k in ("L3D", "L3A", "L3D0", "L3A0")):
+        ts(R("OL2"), R("CI"), g15, A.is_equal, 2048.0, A.mult)
+        ts(R("OLN"), R("CI"), g15, A.is_equal, -1024.0, A.mult)
     ms(R("SND"), 512.0)
     ms(R("X", (4096, XW)), 0.0)
+    for a, b, c in ((0, 4, 4), (4, 20, 16), (21, 85, 64)):
+        iota(R("cd", (a, b)), [[STR, b - a], [0, NM]], c * STR)
+    ms(R("cd", 20), 0.0)
+    iota(R("hi"), [[0, 3], [1, NM]], 0)
+    for a, b in ((0, 32), (64, 128)):
+        ms(R("PLD", (a, b)), 0)
+        iota(R("PLA", (a, b)), [[0, (b - a) * STR]], 0)
     for h in "DA":
-        n, o = NH[h], OFF[h]
-        for a, b, c in ((0, 4, 4), (4, 20, 16), (21, 85, 64)):
-            iota(R("cd" + h, (a * n, b * n)), [[STR[h], b - a], [0, n]], c * STR[h])
-        ms(R("cd" + h, (20 * n, 21 * n)), 0.0)
-        iota(R("hi" + h), [[0, 3], [1, n]], 0)
-        ms(R("PL" + h), 0)
-        ms(R("PT" + h, (32 * STR[h], 64 * STR[h])), 0)
-        for c, base in ((1, QC), (0, SPARE)):
-            ts(R("PL" + h, c, (0, n)), R("RT", (o, o + n)), float(base), A.add)
+        iota(R("PT" + h, (32 * STR, 64 * STR)), [[0, 32 * STR]], 0)
 
-    UP = {"D": {"U1": 480, "U2": 0, "t": 80, "up1": 400, "pre": 500}, "A": {"U1": 4, "U2": 16, "t": 64, "up1": 256, "pre": 352}}
+    up = {"U2": 0, "t": 80, "up1": 400, "U1": 480, "pre": 500, "U0": 506}
 
-    def chain(h, m, U, p, l):
-        n = NH[h]
-        w, t0 = m * n, UP[h]["t"]
+    def chain(h, n, m, U, p, l, pl=None):
+        w, t0 = m * n, up["t"]
         r_, v_, s_ = [R(x + h, (0, w)) for x in ("cR", "cv", "cs")]
+        z = R("cz" + h, (0, 4 * m), (0, n))
         ts(r_, U, CM, A.add, CM, A.subtract)
         tt(v_, U, r_, A.subtract)
-        if w > 32:
+        if w > CFG["SQ"]:
             act(s_, v_, F.Square)
         else:
             tt(s_, v_, v_, A.mult)
-        for a in range(4):
-            act(R("U" + h, (t0 + a * w, t0 + a * w + w)), v_, F.Identity, scale=R("KF", 0, (a, a + 1)), bias=R("KF", 1, (a, a + 1)))
-        ts(s_, s_, 15.5, A.subtract, 2.0 ** -5, A.mult)
-        for a in range(4):
-            tt(R("cz" + h, (a, 4 * m, 4)), R("U" + h, (t0 + a * w, t0 + a * w + w)), s_, A.add)
-        ts(p, R("cz" + h, (0, 4 * m)), 4095, A.bitwise_and)
-        cp(l, p)
+        if w <= CFG["TV"]:
+            ts(s_, s_, 15.0, A.subtract, 2.0 ** -5, A.mult)
+            for a in range(4):
+                ts(R("ct" + h, 0, (a, 4 * m, 4), (0, n)), v_, R("KF", 0, (a, a + 1)), A.mult, R("KF", 1, (a, a + 1)), A.add)
+            for a in range(4):
+                tt(R("cz" + h, (a, 4 * m, 4), (0, n)), R("ct" + h, 0, (a, 4 * m, 4), (0, n)), s_, A.add)
+        elif w <= CFG["ONE"]:
+            for a in range(4):
+                act(R("ct" + h, 0, (a, 4 * m, 4), (0, n)), v_, F.Identity, scale=R("KF", 0, (a, a + 1)), bias=R("KF", 1, (a, a + 1)))
+            for a in range(4):
+                act(R("ct" + h, 1, (a, 4 * m, 4), (0, n)), s_, F.Identity, scale=2.0 ** -5, bias=-0.46875)
+            tt(z, R("ct" + h, 0, (0, 4 * m), (0, n)), R("ct" + h, 1, (0, 4 * m), (0, n)), A.add)
+        else:
+            for a in range(4):
+                act(R("U" + h, (t0 + a * w, t0 + a * w + w)), v_, F.Identity, scale=R("KF", 0, (a, a + 1)), bias=R("KF", 1, (a, a + 1)))
+            if w > CFG["S2"]:
+                act(s_, s_, F.Identity, scale=2.0 ** -5, bias=-0.46875)
+            else:
+                ts(s_, s_, 15.0, A.subtract, 2.0 ** -5, A.mult)
+            for a in range(4):
+                tt(R("cz" + h, (a, 4 * m, 4), (0, n)), R("U" + h, (t0 + a * w, t0 + a * w + w)), s_, A.add)
+        if m != 16:
+            if CFG["ANDU"] and not pl:
+                ts(l, z, 4095, A.bitwise_and)
+            ts(p, z, 4095, A.bitwise_and)
+            if pl or not CFG["ANDU"]:
+                cp(l, pl or p)
+            return
+        cut = CFG["CUT" + h]
+        for a, b in zip(cut, cut[1:]):
+            pp, ll = R("PL" + h, (64 + a, 64 + b), (0, n)), R("l3" + h, (a * n, b * n))
+            if CFG["ANDU"]:
+                ts(ll, R("cz" + h, (a, b), (0, n)), 4095, A.bitwise_and)
+            ts(pp, R("cz" + h, (a, b), (0, n)), 4095, A.bitwise_and)
+            if not CFG["ANDU"]:
+                (gcp if CFG["LG" + h] and a else cp)(ll, pp)
 
-    zb, jb, eb = [0], [0], [0]
+    zb, jb, where = [0], [0], {}
 
-    def search(h, s):
-        n, o, up = NH[h], OFF[h], UP[h]
+    def search(h, s, o, n):
         Un, Kn, PL = "U" + h, "K" + h, "PL" + h
         tag = h + ("0" if s == 0 else "")
+        ns = (0, n)
+        phase[0] = "head" + h
+        if where.get(h) != o:
+            where[h] = o
+            for c, base in ((1, QC), (0, SPARE)):
+                ts(R(PL, c, (0, min(NM, 8 - o))), R("RT", (o, min(o + NM, 8))), float(base), A.add)
 
         def QX(a, b):
             if h == "A":
@@ -346,116 +441,144 @@ def rank_program(g, core, T, topo):
             pc = W // -(-W // 512)
             for x in range(0, W, pc):
                 zb[0] ^= 1
-                Z = R("Z%d" % zb[0], (0, pc))
+                Z = R(("B4", "B5")[zb[0]] if dn == "d12A" else "Z%d" % zb[0], (0, pc))
                 P(Z, [(ID, R(dn, (b0 + x, b0 + x + pc))), (NID, QX(x, x + pc))])
                 act(R(bn, (b0 + x, b0 + x + pc)), Z, F.Abs)
-        p1, p2 = R(PL, (4, 8), (0, n)), R(PL, (16, 32), (0, n))
+        p1, p2 = R(PL, (4, 8), ns), R(PL, (16, 32), ns)
+        nd = min(n, 5 - o)
+        na = n - nd
+        if nd:
+            gcp(R(PL, (4, 8), (0, nd)), R("p1D", (4 * s, 4 * s + 4), (o, o + nd)))
         if h == "A":
-            q = R("ARR", s - 1)
-            gcp(QX(0, 48), q)
-            gcp(QX(48, 96), q)
-            for w in (96, 192, 384):
+            q, l1, uq = QX(0, 16 * n), R("l1A", (0, 4 * n)), lambda m: R("UQA", (0, m), ns)
+            if nd:
+                for c in range(2):
+                    gcp(QX(16 * n * c, 16 * (n * c + nd)), R("QS", (80 * s + 16 * o, 80 * s + 80)))
+                gcp(R("UQA", 0, (0, nd)), R("UQD", 0, (5 * s + o, 5 * s + 5)))
+            if na:
+                for c in range(2):
+                    gcp(QX(16 * (n * c + nd), 16 * n * (c + 1)), R("ARR", s - 1))
+                U0 = R(Un, (up["U0"], up["U0"] + na))
+                P(U0, [(NID, R("C2K", (0, na)))], True, False)
+                P(U0, [(R("WL", (15 - r, 143 - r)), R("ARR", s - 1, (r, C, 16))) for r in range(16)], False, True)
+                act(R("UQA", 0, (nd, n)), U0, F.Copy)
+                chain(h, na, 1, U0, R(PL, (4, 8), (nd, n)), l1, p1 if nd else None)
+                empty(R("htA", (4 * n, 4 * n + na)), U0)
+            else:
+                cp(l1, p1)
+            for w in (32 * n, 64 * n, 128 * n):
                 gcp(QX(w, 2 * w), QX(0, w))
-            U0 = R(Un, (0, n))
-            P(U0, [(NID, R("C2K", (0, n)))], True, False)
-            P(U0, [(R("WL", (15 - r, 143 - r)), R("ARR", s - 1, (r, C, 16))) for r in range(16)], False, True)
-            act(R("UQA", 0), U0, F.Copy)
-            chain(h, 1, U0, p1, R("l1A"))
-            ts(R("htA", (4 * n, 5 * n)), U0, thr, A.is_gt, -1.0, A.mult)
             for w in (1, 2, 4, 8):
-                gcp(R("UQA", (w, 2 * w)), R("UQA", (0, w)))
-            l1, uq = R("l1A"), lambda m: R("UQA", (0, m))
+                gcp(R("UQA", (w, 2 * w), ns), R("UQA", (0, w), ns))
         else:
-            q = R("QS", (s * 80, s * 80 + 80))
-            gcp(p1, R("p1D", (4 * s, 4 * s + 4)))
-            l1, uq = R("l1D", (20 * s, 20 * s + 20)), lambda m: R("UQD", (0, m), (5 * s, 5 * s + 5))
-        gcp(R("X", (QC + 16 * o, QC + 16 * (o + n))), q)
+            q = R("QS", (s * 80, s * 80 + 16 * n))
+            l1, uq = R("l1D", (20 * s, 20 * s + 4 * n)), lambda m: R("UQD", (0, m), (5 * s, 5 * s + n))
+        gcp(R("X", (QC + 16 * o, QC + 16 * (o + n))), q, [tok("own")])
         gcp(R("RG" + h, (48 * n, 64 * n)), q)
         for a in range(4):
-            gcp(R("r1" + h, (a, 16, 4)), p1)
-        up1 = R(Un, (up["up1"], up["up1"] + 16 * n))
-        up2 = R("KD", (432, 512)) if h == "D" else R(Un, (304, 352))
+            gcp(R("r1" + h, (a, 16, 4), ns), p1)
+        up1, up2 = R(Un, (up["up1"], up["up1"] + 16 * n)), R(Kn, (432, 432 + 16 * n))
+        e21, v1, v2, v1r = R("e21" + h, (0, 16 * n)), R("v1" + h, (0, 4 * n)), R("v2" + h, (0, 16 * n)), R("v1r" + h, sl(None), ns)
         U1 = R(Un, (up["U1"], up["U1"] + 4 * n))
-        P(U1, [(IDF, uq(4))], True, False)
-        dist("d12" + h, "b12" + h, 0, 64 * n, l1, "V")
+        first = []
+        for a, b, e in _pieces(CFG["L1" + h]):
+            lo = 20 * s if h == "D" else 0
+            dist("d12" + h, "b12" + h, 16 * n * a, 16 * n * (b - a), R("l1" + h, (lo + a * n, lo + b * n)), e)
+            part = R(Un, (up["U1"] + a * n, up["U1"] + b * n))
+            first.append((IDF, uq(b - a), part) if e == "V" else (NID, R("C2K", (0, (b - a) * n)), part))
+        P(U1, ([(BIG, R("PEN", (0, 4 * n)))] if len(first) > 1 else []) + first, True, False)
         P(U1, sums("WL", "d12" + h, 0, 4 * n), False, True)
-        chain(h, 4, U1, p2, R("l2" + h))
-        ts(R("v1" + h), U1, thr, A.is_gt)
+        chain(h, n, 4, U1, p2, R("l2" + h, (0, 16 * n)))
+        empty(v1, U1)
         for a in range(4):
-            gcp(R("v1r" + h, (a, 16, 4)), R("v1" + h))
+            gcp(R("v1r" + h, (a, 16, 4), ns), v1)
         u2, first = up["U2"], []
         for a, b, e in _pieces(CFG["L2" + tag]):
             dist("d12" + h, "b12" + h, 64 * n + 16 * n * a, 16 * n * (b - a), R("l2" + h, (a * n, b * n)), e)
             part = R(Un, (u2 + a * n, u2 + b * n))
             first.append((IDF, uq(b - a), part) if e == "V" else (NID, R("C2K", (0, (b - a) * n)), part))
-        cp(up1, R("r1" + h))
-        tt(R("e21" + h), p2, up1, A.is_equal)
-        cp(up2, p2)
+        if CFG["UP"]:
+            act(up1, R("r1" + h, sl(None), ns), F.Copy)
+            gcp(R("r2" + h, (0, 16 * n)), p2)
+            act(up2, R("r2" + h, (0, 16 * n)), F.Copy)
+        else:
+            cp(up1, R("r1" + h, sl(None), ns))
+            cp(up2, p2)
+        tt(e21, p2, up1, A.is_equal)
         U2 = R(Un, (u2, u2 + 16 * n))
-        P(U2, [(BIG, R("e21" + h)), (BIG, R("v1r" + h))] + first, True, False)
+        P(U2, [(BIG, e21), (BIG, v1r)] + first, True, False)
         P(U2, sums("WL", "d12" + h, 64 * n, 16 * n), False, True)
-        chain(h, 16, U2, R(PL, (64, 128), (0, n)), R("l3" + h))
+        chain(h, n, 16, U2, None, None)
+        phase[0] = "keys" + h
         for a, b in ((0, 32), (64, 128)):
-            i, d = R(PL, (a, b)), R("PT" + h, (a * STR[h], b * STR[h]))
+            i, d = R(PL, (a, b)), R("PT" + h, (a * STR, b * STR))
             DMA("S", [(d[0], i[0])], [i], [d], 2.5)
-        ts(R("v2" + h), U2, thr, A.is_gt)
+        empty(v2, U2)
         for a in range(4):
-            gcp(R("v2r" + h, (a, 64, 4)), R("v2" + h))
+            gcp(R("v2r" + h, (a, 64, 4), ns), v2)
         for a in range(4):
-            blk = R(PL, (64 + a, 128, 4), (0, n))
-            tt(R("e32" + h, (a, 64, 4)), blk, up2, A.is_equal)
-            tt(R("e31" + h, (a, 64, 4)), blk, up1, A.is_equal)
+            blk = R(PL, (64 + a, 128, 4), ns)
+            tt(R("e32" + h, (a, 64, 4), ns), blk, up2, A.is_equal)
+            tt(R("e31" + h, (a, 64, 4), ns), blk, up1, A.is_equal)
         k2 = R(Kn, (4 * n, 20 * n))
-        P(R(Kn, (0, 20 * n)), [(ID, R("cd" + h, (0, 20 * n))), (NEG, R("e21" + h), k2), (NEG, R("v1r" + h), k2)] + sums("OL", "b12" + h, 0, 20 * n))
-        P(R(Kn, (20 * n, 85 * n)), [(ID, R("cd" + h, (20 * n, 85 * n)))], True, False)
-        ts(R("ht" + h, (0, 4 * n)), R(Kn, (0, 4 * n)), 1024.0, A.is_lt, -1.0, A.mult)
-        P(R(Kn, (20 * n, 21 * n)), [(NEG, R("ht" + h, (a * n, a * n + n))) for a in range(5 if h == "A" else 4)], False, False, True)
-        for j, e in enumerate(("e32", "e31", "v2r")):
-            k3 = R(Kn, (21 * n, 85 * n))
-            P(k3[:2] + (0, 0), [(NEG, R(e + h))], False, False, True)
+        P(R(Kn, (0, 20 * n)), [(ID, R("cd", (0, 20), ns)), (NEG, e21, k2), (NEG, v1r, k2)] + sums("OL", "b12" + h, 0, 20 * n))
+        P(R(Kn, (20 * n, 85 * n)), [(ID, R("cd", (20, 85), ns))], True, False)
+        if CFG["FL"]:
+            act(R("ht" + h, (0, 4 * n)), R(Kn, (0, 4 * n)), F.Relu, scale=-2.0 ** -9, bias=2.0)
+        else:
+            ts(R("ht" + h, (0, 4 * n)), R(Kn, (0, 4 * n)), 1024.0, A.is_lt)
+        P(R(Kn, (20 * n, 21 * n)), [(POS, R("ht" + h, (a * n, a * n + n))) for a in range(4)] +
+          ([(POS, R("htA", (4 * n, 4 * n + na)), R(Kn, (20 * n + nd, 21 * n)))] if na else []), False, False, True)
+        for e in ("e32", "e31", "v2r"):
+            P(R(Kn, (21 * n, 85 * n))[:2] + (0, 0), [(NEG, R(e + h, sl(None), ns))], False, False, True)
+        for _ in range(CFG["PAD"]):
+            P(R(Kn, (21 * n, 85 * n))[:2] + (0, 0), [(ID, R("r3A", (0, 64 * n)))] * 4, False, False, True)
         for a, b, e in _pieces(CFG["L3" + tag]):
             dist("d3" + h, "d3" + h, 16 * n * a, 16 * n * (b - a), R("l3" + h, (a * n, b * n)), e)
         c0 = 0
-        kind = {a: e for a, b, e in _pieces(CFG["L3" + tag])}
+        who = {a: e for a, b, e in _pieces(CFG["L3" + tag])}
         for m in CFG["KEY" + tag]:
             c1 = c0 + m
-            if kind[c0] == "Y":
+            if who[c0] == "Y":
                 t = sums("OLN", "d3" + h, 16 * n * c0, m * n) + sums("OL2", "r3" + h, 16 * n * c0, m * n)
             else:
                 t = sums("OL", "d3" + h, 16 * n * c0, m * n)
             P(R(Kn, ((21 + c0) * n, (21 + c1) * n)), t, False, c1 == 64, c1 < 64)
             c0 = c1
 
-    def tail(h, s, last):
-        n, o, st = NH[h], OFF[h], STR[h]
-        w = 48 * n
-        M, sc = R("M" + h), "sc" + h
+    def tail(h, s, o, n, last):
+        w, ns = 48 * n, (0, n)
+        phase[0] = "tail" + h
+        MI, sc, cc, gm, o16 = R("MI" + h, ns), "sc" + h, "cc" + h, R("gm" + h, (0, w)), R("o16" + h, (0, 3 * n))
         for i in range(n):
-            red(R("M" + h, (i, i + 1)), R("K" + h, (i, 85 * n, n)))
-        cp(R("MI" + h), M)
+            red(R("MI" + h, (i, i + 1)), R("K" + h, (i, 85 * n, n)))
         for k in range(3):
-            ts(R("cc" + h, k), R("MI" + h), 2 * k, A.arith_shift_right, ((128 >> 2 * k) - 1) * st, A.bitwise_and)
-        if last:
+            ts(R(cc, k, ns), MI, 2 * k, A.arith_shift_right, ((128 >> 2 * k) - 1) * STR, A.bitwise_and)
+        if last or n < NM:
             for i in range(n):
-                ts(R("o16" + h, (i, 3 * n, n)), R("cc" + h, sl(None), i), float(i), A.add)
+                ts(R("o16" + h, (i, 3 * n, n)), R(cc, sl(None), i), float(i), A.add)
         else:
-            tt(R("cc" + h), R("cc" + h), R("hi" + h), A.add)
-            cp(R("o16" + h), R("cc" + h))
-        gat(R("gm" + h), R("PT" + h), R("o16" + h), R("MASK", (0, w)), A.mult)
-        sp = R("B4", (0, w)) if h == "D" else R("KA", (256, 256 + w))
-        P(sp, [(BLKF, R("gm" + h))])
+            tt(R(cc, sl(None), ns), R(cc, sl(None), ns), R("hi", sl(None), ns), A.add)
+            cp(o16, R(cc, sl(None), ns))
+        gat(gm, R("PT" + h), o16, R("MASK", (0, w)), A.mult)
+        sp = R("B4" if h == "D" else "KA", (0, w))
+        P(sp, [(BLKF, gm)])
         cp(R("SP", sl(None), (16 * o, 16 * (o + n))), sp)
-        a, b, c = R(sc), R("RST", (0, w)), R("gm" + h)
-        op("V", lambda: v.tensor_tensor_scan(a[0], b[0], c[0], 0.0, A.mult, A.add), [b, c], [a], w * CYC)
-        cp(R("rl" + h), R(sc, (15, w, 16)))
-        gat(R("RG" + h, (0, w)), R("X", (0, DUMPX)), R("rl" + h))
-        ts(R("ne" + h), M, THR, A.is_lt, 0.5, A.subtract)
+        a, b = R(sc, (0, w)), R("RST", (0, w))
+        op("V", lambda: v.tensor_tensor_scan(a[0], b[0], gm[0], 0.0, A.mult, A.add), [b, gm], [a], w * CYC)
+        rg, win, rl = R("RG" + h, (0, w)), R("X", (0, DUMPX)), R("rl" + h, (0, 3 * n))
+        cp(rl, R(sc, (15, w, 16)))
+        if o:
+            op("A", lambda: ac.activation(rg[0], win[0].indirect(rl[0]), F.Copy), [tok("own"), tok("last"), rl, (None, "either", 0, 0)], [rg], 0.065 + 1.56 * w * CYC, None, "g")
+        else:
+            gat(rg, win, rl)
+        ts(R("ne" + h, ns), MI, THR, A.is_lt, 0.5, A.subtract)
         for i in range(n):
             gi = o + i
             Zn, wo = CFG["FOLD" + h][i], 48 * min(gi, 2)
             Z = R(Zn, (352 - wo, 400))
             P(Z, [(BIG, R("PEN", (96 - wo, 144)))], True, False)
-            for b0, b1 in ((0, o), (o, gi + 1)) if o else ((0, gi + 1),):
+            for b0, b1 in ((0, o), (o, gi + 1)) if o and i < CFG["SPLIT"] else ((0, gi + 1),):
                 for k in range(3):
                     x = 16 * (k * n + i) + 15
                     ts(R("EQ" + h, i, k, sl(None), (16 * b0, 16 * b1)), R("SP", sl(None), (16 * b0, 16 * b1)), R(sc, (x, x + 1)), A.is_equal)
@@ -464,76 +587,87 @@ def rank_program(g, core, T, topo):
                     if b1 > gi:
                         t.append((BIG, R("EQ" + h, i, k, sl(None), (16 * gi, 16 * gi + 16)), R(Zn, (352, 400))))
                     P(Z, t, False, b1 > gi and k == 2)
-            if CFG["RED" + h][i] == "V":
+            if CFG["RED" + h][i] == "V" and gi:
                 red(R("res" + h, (i, i + 1)), Z)
             else:
                 jb[0] = (jb[0] + 1) % 4
                 act(R("JK", jb[0], (0, wo + 48)), Z, F.Relu, accum_out=R("res" + h, (i, i + 1)))
-        res = R("res" + h)
+        res = R("res" + h, ns)
         if s < S - 1:
-            gone, p4 = R("GP" + h, (2 * n - 2, 3 * n - 2)), R("U" + h, (UP[h]["pre"], UP[h]["pre"] + n))
-            tt(gone, res, R("ne" + h), A.is_lt)
+            gone, p4 = R("GP" + h, (8, 8 + n)), R("U" + h, (up["pre"], up["pre"] + n))
+            if h == "D" and s < 2:
+                ms(R("GPD"), 0.0)
+            tt(gone, res, R("ne" + h, ns), A.is_lt)
             if o:
-                P(p4, [(BLK, R("GPD", (x, x + n))) for x in range(6, 13)], True, False)
-            P(p4, [(TRS, gone), (NEG, gone)] + [(BLK, R("GP" + h, (2 * n - 2 - x, 3 * n - 2 - x))) for x in range(1, n)], not o, True)
+                P(p4, [(BLK, R("GPD", (x, x + n))) for x in range(9 - n, 8 + o)], True, False)
+            P(p4, [(TRS, gone), (NEG, gone)] + [(BLK, R("GP" + h, (8 - x, 8 + n - x))) for x in range(1, n)], not o, True)
             if last:
                 for i in range(n):
-                    x = UP[h]["pre"] + i
+                    x = up["pre"] + i
                     ts(R("s16" + h, (i, i + 1)), R("U" + h, (x, x + 1)), R("SD", (o + i, o + i + 1)), A.min, B24, A.add)
             else:
-                tt(R("ds" + h), p4, R("SD", (o, o + n)), A.min)
-                ts(R("s16" + h), R("ds" + h), B24, A.add)
-            scat(R("SND"), R("s16" + h), R("RG" + h, (0, 16 * n)))
+                tt(R("ds" + h, ns), p4, R("SD", (o, o + n)), A.min)
+                ts(R("s16" + h, ns), R("ds" + h, ns), B24, A.add)
+            scat(R("SND"), R("s16" + h, ns), R("RG" + h, (0, 16 * n)), "last" if last and CFG["SF"] else None)
+        if last and CFG["W1"]:
+            for x in range(3 * n):
+                ts(R("w16" + h, (x, x + 1)), R(sc, (16 * x + 15, 16 * x + 16)), R("res" + h, (x % n, x % n + 1)), A.add, R("DUMP", (3 * o + x, 3 * o + x + 1)), A.min)
+            return
         for k in range(3):
-            tt(R("wm" + h, k), R(sc, (16 * k * n + 15, 16 * (k + 1) * n, 16)), res, A.add)
-        tt(R("wm" + h), R("wm" + h), R("DUMP", (3 * o, 3 * (o + n))), A.min)
-        cp(R("w16" + h), R("wm" + h))
+            tt(R("wm" + h, k, ns), R(sc, (16 * k * n + 15, 16 * (k + 1) * n, 16)), res, A.add)
+        wm = R("wm" + h, sl(None), ns)
+        tt(wm, wm, R("DUMP", (3 * o, 3 * (o + n))), A.min)
+        cp(R("w16" + h, (0, 3 * n)), wm)
 
+    n0, nd = CFG["ND0"], CFG["ND"]
     U0 = R("UD", (0, 30))
     P(U0, [(NID, R("C2K", (0, 30)))] + sums("WL", "QS", 0, 30))
     act(R("UQD", 0), U0, F.Copy)
-    chain("D", 6, U0, R("p1D"), R("l1D"))
+    chain("D", 5, 6, U0, R("p1D"), R("l1D", (0, 4 * n0)), R("p1D", (0, 4), (0, n0)))
+    for s in range(1, S):
+        cp(R("l1D", (20 * s, 20 * s + 4 * nd)), R("p1D", (4 * s, 4 * s + 4), (0, nd)))
     for w in (1, 2, 4, 8):
         gcp(R("UQD", (w, 2 * w)), R("UQD", (0, w)))
-    cp(R("QX0", (0, 80)), R("QS", (0, 80)))
-    for w in (80, 160, 320, 640):
+    cp(R("QX0", (0, 16 * n0)), R("QS", (0, 16 * n0)))
+    for w in (16 * n0, 32 * n0, 64 * n0, 128 * n0):
         cp(R("QX0", (w, 2 * w)), R("QX0", (0, w)))
-    DMA("S", [(T.QXD[:, :, 0:80], T.QS[:, 80:480])], [R("QS"), tok("X0D")], [R("QXD", sl(None), (0, 80))], 2.5)
-    for w in (80, 160, 320, 640):
+    DMA("S", [(T.QXD[:, s - 1, 0:16 * nd], T.QS[:, 80 * s:80 * s + 16 * nd]) for s in range(1, S)], [R("QS"), tok("X0D")], [R("QXD", sl(None), (0, 16 * nd))], 2.5)
+    for w in (16 * nd, 32 * nd, 64 * nd, 128 * nd):
         DMA("S", [(T.QXD[:, :, w:2 * w], T.QXD[:, :, 0:w])], [R("QXD", sl(None), (0, w))], [R("QXD", sl(None), (w, 2 * w))], 2.5)
     nxt = T.cores[(rank + 1) % len(T.cores)]
     rid, pid = topo.addr(nxt)[:2]
     msk, neng = topo.mask(core, nxt), len(topo.engines(core, nxt))
     snd = R("SND", (0, C))
     for s in range(S):
-        halves = "DA" if s else "D"
+        halves = [("D", 0, nd), ("A", nd, 8 - nd)] if s else [("D", 0, n0), ("A", n0, 5 - n0)][:1 + (n0 < 5)]
+        seen.clear()
         if 0 < s < S - 1:
             op("G", lambda: g.iota(snd[0], [[0, C]], 512, 0, allow_small_or_imprecise_dtypes=True), [tok("snt%d" % s)], [snd], 0.25)
-        for h in halves:
-            search(h, s)
-        for h in halves:
-            tail(h, s, h == halves[-1])
-        if s < S - 1:
-            op("G", (lambda s=s: g.remote_dma(T.ARR[:, s, :], snd[0], T.sem["arr%d" % (s + 1)], T.sem["snt%d" % (s + 1)], pid, rid, msk)),
-               [snd], [], 0.5, ("none", 0))
-            op("N", None, [snd], [R("ARR", s)], 2.5, ("arr%d" % (s + 1), neng))
-            op("N", None, [snd], [tok("snt%d" % (s + 1))], 2.5, ("snt%d" % (s + 1), neng))
-        for h in halves:
-            scat(R("X"), R("w16" + h), R("RG" + h, (16 * NH[h], 64 * NH[h])))
+        for h, o, n in halves:
+            search(h, s, o, n)
+        for h, o, n in halves:
+            last = h == halves[-1][0]
+            tail(h, s, o, n, last)
+            if last and s < S - 1:
+                op("G", (lambda s=s: g.remote_dma(T.ARR[:, s, :], snd[0], T.sem["arr%d" % (s + 1)], T.sem["snt%d" % (s + 1)], pid, rid, msk)),
+                   [snd], [], 0.5, ("none", 0))
+                op("N", None, [snd], [R("ARR", s)], 3.5, ("arr%d" % (s + 1), neng))
+                op("N", None, [snd], [tok("snt%d" % (s + 1))], 2.5, ("snt%d" % (s + 1), neng))
+            scat(R("X"), R("w16" + h, (0, 3 * n)), R("RG" + h, (16 * n, 64 * n)), "last" if last else "either")
     DMA("S", [(T.y[:, 0:2048], T.X[:, 0:2048])], [R("X", (0, 2048))], [tok("y1")], 4.0)
     DMA("AD", [(T.y[:, 2048:4096], T.X[:, 2048:4096])], [R("X", (2048, 4096))], [tok("y2")], 4.0)
 
     eng = {"V": v, "A": ac, "P": pe, "G": g, "S": g.sync, "AD": ac}
     N = len(ops)
     if "o" not in ORDER:
-        ORDER["o"], ORDER["d"], ORDER["fin"] = _schedule(ops)
+        ORDER["o"], ORDER["d"], ORDER["fin"] = _schedule(ops, kind)
         ORDER["ops"] = ops
     deps = ORDER["d"]
     cnt = {"V": 0, "A": 0, "P": 0, "G": 0}
     val, snap = [None] * N, [{} for _ in range(N)]
     know = {q: {} for q in "VAPGS"}
     for i in ORDER["o"]:
-        q, fn, rd, wr, du, own = ops[i]
+        q, fn, rd, wr, du, own, cat = ops[i]
         p = PHYS[q]
         if p == "N":
             val[i] = own

import numpy as np
from concourse.mybir import AluOpType as A, AxisListType, ActivationFunctionType as F

S, C = 6, 48
NM = 5
STR = 8
QC, SPARE, DUMPX, XW = 4096, 4224, 4352, 4736
B24, B22 = float(1 << 24), float(1 << 22)
THR = 4090.0 * 1024
CM = 1.5 * 2.0 ** 35
CFG = {"ND": 5, "ND0": 4, "L2D": "V8 A8", "L2A": "V8 A8", "L3D": "A8 V8 A8 V8 V8 A8 V8 V8", "L3A": "A10 V12 A10 V6 V6 V6 V6 V8",
       "L2D0": "V8 A8", "L3D0": "A10 V12 A10 V12 V10 V10", "L2A0": "V8 A8", "L3A0": "V16 A16 V16 V16", "KEYA0": (64,),
       "KEYD": (24, 24, 16), "KEYA": (22, 22, 20), "KEYD0": (22, 22, 20), "ROUNDS": 2, "SQ": 20, "S2": 999, "ONE": 12, "L1D": "A4", "L1A": "A4",
       "AMIN": 64, "CUTD": (0, 16, 40, 64), "CUTA": (0, 64), "LGD": 1, "LGA": 0, "TUNE": 230, "PAD": 0, "SPLIT": 3, "FL": 1, "UP": 0,
       "ACP": ("w16D", "o16D", "rlD", "l1D"), "ANDU": 0, "W1": 0, "LIFT": {}, "TV": 12, "SEED": 0, "NK": 2, "SD": 1.5,
       "FINE": 0, "SF": 1, "FOLDD": ("B5", "B4", "B5", "B4", "B5"), "FOLDA": ("B4", "B5", "Z0", "Z1", "B4"), "REDD": "AAAAA", "REDA": "AAV"}
SB, PS = "sbuf", "psum"
CYC, PCYC, WAKE, AFIX, VFIX = 0.00095, 0.00053, 0.2, 0.005, 0.005
RANGE = ((0.14, 1.0, 1.0, 1.0, 1.0, 0, 0, 3.5, 194), (0.14, 0.92, 0.92, 0.82, 1.3, 0, 0, 2.4, 172), (0.06, 1.1, 1.08, 0.86, 1.4, 0, 0, 2.5, 198),
         (0.26, 0.9, 1.03, 0.9, 1.0, 0, 0, 3.0, 202), (0.25, 0.88, 0.92, 0.78, 1.1, 0, 0, 5.0, 197), (0.08, 1.25, 0.95, 1.28, 1.4, 0, 0, 2.5, 249))
INORDER = "VAP"
HEAD = ("cRA", "cvA", "csA", "ctA", "czA", "PLA", "l1A", "l2A", "l3A", "d12A", "UA", "QXA", "UQA", "e21A", "v1A", "v1rA", "r1A")


def _shapes():
    b, f, i4, u2 = "bfloat16", "float32", "int32", "uint16"
    n = NM
    d = {"X": ([XW], b), "QS": ([480], b), "QX0": ([1280], b), "QXD": ([5, 1280], b), "QXA": ([1280], b), "WT": ([1], b), "KI": ([4], i4),
         "KF": ([4, 4], f), "ST": ([4, 144], b), "MB": ([7, 128], b), "MF": ([2, 128], f), "CI": ([144], f), "CR": ([240], f), "MASK": ([240], f),
         "RST": ([240], f), "PI": ([8], i4), "PF": ([8], f), "PEN": ([144], b), "C2K": ([80], b), "DUMP": ([24], f), "RT": ([8], f), "SD": ([8], f),
         "GPD": ([24], b), "GPA": ([16], b), "SND": ([256], b), "JK": ([4, 144], b), "ARR": ([5, C], b), "SP": ([3, 128], u2),
         "EQD": ([5, 3, 3, 80], b), "EQA": ([5, 3, 3, 128], b), "UQD": ([16, 30], f), "UQA": ([16, n], f), "p1D": ([24, 5], i4),
         "l1D": ([120], u2), "l1A": ([4 * n], u2), "cd": ([85, n], b), "hi": ([3, n], i4)}
    for h in "DA":
        for nm, sh, ty in (("PL", [128, STR], i4), ("PT", [128 * STR], i4), ("cR", [16 * n], f), ("cv", [16 * n], f), ("cs", [16 * n], f),
                           ("cz", [64, n], i4), ("ct", [2, 16, n], f), ("l2", [16 * n], u2), ("l3", [64 * n], u2), ("r1", [16, n], f),
                           ("r2", [16 * n], f), ("e21", [16 * n], b), ("v1", [4 * n], b), ("v1r", [16, n], b), ("v2", [16 * n], b),
                           ("v2r", [64, n], b), ("e32", [64, n], b), ("e31", [64, n], b), ("d12", [320 * n], b), ("b12", [320 * n], b),
                           ("d3", [1024 * n], b), ("r3", [1024 * n], b), ("ht", [5 * n], b), ("MI", [n], i4), ("ne", [n], f),
                           ("cc", [3, n], i4), ("o16", [3 * n + 1], u2), ("gm", [48 * n], f), ("sc", [48 * n], f), ("rl", [3 * n + 1], u2),
                           ("res", [n], f), ("wm", [3, n], f), ("w16", [3 * n + 1], u2), ("ds", [n], f), ("s16", [n + 1], u2), ("RG", [64 * n], b)):
            d[nm + h] = (sh, ty)
    return d


SHAPES = _shapes()
PART = {k: (buf, i) for buf, ks in (("ST", ("WL", "OL", "OL2", "OLN")), ("MB", ("ID", "NID", "NEG", "BIG", "BLK", "TRS", "POS")), ("MF", ("IDF", "BLKF")))
        for i, k in enumerate(ks)}
BANKS = ("UD", "UA", "KD", "KA", "B4", "B5", "Z0", "Z1")
APART = BANKS + ("either",)
SCRATCH = {k: (SB, [128] + sh, ty) for k, (sh, ty) in SHAPES.items()}
for _k in BANKS:
    SCRATCH[_k] = (PS, [128, 512], "float32")
    SHAPES[_k] = ([512], "float32")
SEMAPHORES = ["cV", "cA", "cP", "cG"] + ["m%d" % i for i in range(34)] + ["arr%d" % i for i in range(1, S)] + ["snt%d" % i for i in range(1, S)]
PHYS = {"V": "V", "A": "A", "P": "P", "G": "G", "S": "S", "AD": "A", "N": "N"}
ORDER = {}
BITS = {}


def _bits(name, idx):
    key = (name, repr(idx))
    if key not in BITS:
        m = np.zeros(SHAPES[name][0], bool)
        m[idx] = True
        BITS[key] = (int.from_bytes(np.packbits(m.ravel()).tobytes(), "big"), int(m.sum()))
    return BITS[key]


def _pieces(text):
    out, a = [], 0
    for x in text.split():
        out.append((a, a + int(x[1:]), x[0]))
        a += int(x[1:])
    return out


def _place(ops, pre, suc, pri):
    N = len(ops)
    left, st, fin = [len(p) for p in pre], [0.0] * N, [0.0] * N
    busy, ready = {}, [i for i in range(N) if not left[i]]
    while ready:
        c = max(ready, key=lambda i: (pri[i], -i))
        ready.remove(c)
        q, du = PHYS[ops[c][0]], ops[c][4]
        occ = 0.1 if ops[c][0] in ("S", "AD") else du
        t = max([fin[j] + WAKE * need for j, need in pre[c].items()] + [0.0])
        banks = {nm for nm, b in ops[c][2] + ops[c][3] if nm in APART}
        moved = q != "N"
        while moved:
            moved = False
            for a, b, e in reversed(busy.get(q, ())):
                if b < t - 6.0:
                    break
                if a < t + occ - 1e-9 and t < b - 1e-9:
                    t, moved = b, True
            for nm in banks:
                for a, b, e in reversed(busy.get(nm, ())):
                    if b < t - 6.0:
                        break
                    if e != q and a < t + du + WAKE - 1e-9 and t < b + WAKE - 1e-9:
                        t, moved = b + WAKE, True
        st[c], fin[c] = t, t + du
        for nm, e in [(q, t + occ)] + [(nm, t + du) for nm in banks]:
            lst = busy.setdefault(nm, [])
            k = len(lst)
            while k and lst[k - 1][0] > t:
                k -= 1
            lst.insert(k, (t, e, q))
        for k in suc[c]:
            left[k] -= 1
            if not left[k]:
                ready.append(k)
    return st, fin


def _schedule(ops, kind):
    N = len(ops)
    deps, hist = [{} for _ in range(N)], {}
    for i, (q, fn, rd, wr, du, own, cat) in enumerate(ops):
        for isw, lst in ((0, rd), (1, wr)):
            for nm, b in lst:
                for j, w, a in hist.get(nm, ()):
                    if j != i and a & b and (isw or w):
                        deps[i][j] = deps[i].get(j, False) or q != ops[j][0] or q not in INORDER or (w and q != "P" and nm in SHAPES)
        for isw, lst in ((0, rd), (1, wr)):
            for nm, b in lst:
                hh = hist.setdefault(nm, [])
                if isw:
                    hh[:] = [x for x in hh if x[0] == i or x[2] & ~b]
                hh.append((i, isw, b))
    succ = [{} for _ in range(N)]
    for i in range(N):
        for j, need in deps[i].items():
            succ[j][i] = need
    pri = [0.0] * N
    for i in range(N - 1, -1, -1):
        pri[i] = ops[i][4] + max([pri[k] + WAKE * need for k, need in succ[i].items()] + [0.0])
    pri = [pri[i] + CFG["LIFT"].get(kind[i][2], 0.0) for i in range(N)]
    best, pri0, now = None, pri, 1e9
    for _ in range(CFG["ROUNDS"]):
        st, fin = _place(ops, deps, succ, pri)
        if best is None or max(fin) < max(best[1]):
            best, pri0 = (st, fin), pri
        pri = _place(ops, succ, deps, fin)[1]
    durs = [[_under(m, o) for o in ops] for m in RANGE]
    apart = [{nm for nm, b in o[2] + o[3] if nm in APART} for o in ops]

    def settle(st):
        order, runs, more = sorted(range(N), key=lambda i: (st[i], i)), {}, [()] * N
        for i in order:
            q = PHYS[ops[i][0]]
            for nm in apart[i]:
                run = runs.setdefault(nm, [q, [], []])
                if run[0] != q:
                    run[:] = [q, [], run[1]]
                run[1].append(i)
                more[i] = more[i] + tuple(run[2])
        ends = []
        for m, du in zip(RANGE, durs):
            fin, free, wk = [0.0] * N, {}, m[0]
            for i in order:
                q = PHYS[ops[i][0]]
                t = max([fin[j] + wk * need for j, need in deps[i].items()] + [fin[j] + wk for j in more[i]] + [free.get(q, 0.0) if q != "N" else 0.0])
                fin[i] = t + du[i]
                free[q] = t + (0.1 if ops[i][0] in ("S", "AD") else du[i])
            ends.append(max(fin))
        rel = [100.0 * e / m[8] for e, m in zip(ends, RANGE)]
        return (sum(rel) / len(rel) + max(rel)) / 2, order, more, ends

    kinds, rng = sorted(set(kind)), np.random.default_rng(CFG["SEED"])
    lift, now = {k: 0.0 for k in kinds}, settle(best[0]) + (best[1],)
    for _ in range(CFG["TUNE"]):
        trial = dict(lift)
        for k in rng.choice(len(kinds), CFG["NK"]):
            trial[kinds[k]] += float(rng.normal(0.0, CFG["SD"]))
        st, fin = _place(ops, deps, succ, [pri0[i] + trial[kind[i]] for i in range(N)])
        if max(fin) < 1.03 * max(now[4]):
            new = settle(st) + (fin,)
            if new[0] <= now[0]:
                now, lift = new, trial
    for i in range(N):
        deps[i].update((j, True) for j in now[2][i])
    ORDER["mean"], ORDER["ends"] = now[0], now[3]
    return now[1], deps, now[4]


def _under(m, o):
    f, du, cat = m[1], o[4], o[6]
    if cat in "gs":
        return 0.06 + (du - 0.06) * f * m[3 + (cat == "s")]
    return {"V": du * f, "A": du * f + m[6], "P": du * f * m[2], "G": du * f + m[5], "N": m[7]}.get(cat, du)


def rank_program(g, core, T, topo):
    rank = T.rank_of(core)
    if rank is None:
        return
    v, ac, pe = g.vector, g.scalar, g.tensor
    ops = []
    sl = slice
    kind, seen, phase = [], {}, [""]

    def R(name, *idx):
        if name in PART:
            name, idx = PART[name][0], (PART[name][1],) + idx
        idx = tuple(sl(*x) if isinstance(x, tuple) else x for x in idx) or (sl(None),) * len(SHAPES[name][0])
        b, n = _bits(name, idx)
        return (T[name][(sl(None),) + idx], name, b, n)

    def tok(name):
        return (None, name, 1, 0)

    def op(q, fn, rd, wr, dur, own=None, cat=None):
        dur += VFIX * (q == "V" and cat is None)
        k = (q, wr[0][1] if wr else "", phase[0])
        seen[k] = seen.get(k, 0) + 1
        kind.append(k + ((seen[k],) if CFG["FINE"] else ()))
        ops.append((q, fn, [(x[1], x[2]) for x in rd if isinstance(x, tuple)], [(x[1], x[2]) for x in wr], dur, own, cat or q))

    def two(*xs):
        return all(SHAPES[x[1]][1] in ("bfloat16", "uint16") for x in xs)

    def val_(x):
        return x[0] if isinstance(x, tuple) else x

    def ts(o, i, s1, o1, s2=None, o2=None):
        a = (o[0], i[0], val_(s1), val_(s2), o1) + (() if o2 is None else (o2,))
        op("V", lambda: v.tensor_scalar(*a), [i, s1, s2], [o], max(64, i[3] / (2 if two(o, i) else 1)) * CYC)

    def tt(o, a, b, f):
        c = 1 if a[1] in BANKS or b[1] in BANKS else 2
        op("V", lambda: v.tensor_tensor(out=o[0], in0=a[0], in1=b[0], op=f), [a, b], [o], max(64, c * a[3]) * CYC)

    def cp(o, i):
        if o[1] in CFG["ACP"]:
            return gcp(o, i)
        op("V", lambda: v.tensor_copy(o[0], i[0]), [i], [o], max(64, i[3] / (2 if two(o, i) else 1)) * CYC)

    def ms(o, c):
        op("V", lambda: v.memset(o[0], c), [], [o], max(64, o[3] / (2 if two(o) else 1)) * CYC)

    def red(o, i):
        op("V", lambda: v.tensor_reduce(o[0], i[0], AxisListType.X, A.max), [i], [o], max(64, i[3]) * CYC)

    def act(o, i, f, **k):
        a = {x: val_(y) for x, y in k.items()}
        acc = [k["accum_out"]] if "accum_out" in k else []
        op("A", lambda: ac.activation(o[0], i[0], f, **a), [i, k.get("bias"), k.get("scale")], [o] + acc, max(CFG["AMIN"], i[3]) * CYC + AFIX + 0.02 * len(acc))

    def gat(o, win, off, q=None, f=A.subtract):
        if q is None:
            op("A", lambda: ac.activation(o[0], win[0].indirect(off[0]), F.Copy), [win, off], [o] + ([tok("ordA")] if o[1][:2] == "d3" else []), 0.065 + 1.56 * o[3] * CYC, None, "g")
        else:
            op("V", lambda: v.tensor_tensor(out=o[0], in0=win[0].indirect(off[0]), in1=q[0], op=f), [win, off, q], [o] + ([tok("ordV")] if o[1][:2] == "d3" else []), 0.05 + 1.56 * o[3] * CYC, None, "g")

    def scat(win, off, i, after=None):
        op("V", lambda: v.tensor_copy(win[0].indirect(off[0]), i[0]), [off, i], [win] + ([(None, after, int(after != "either"), 0)] if after else []), 0.05 + 3.8 * i[3] * CYC, None, "s")

    def gcp(o, i, also=[]):
        op("G", lambda: g.affine_select(o[0], i[0], [[0, i[3]]], A.is_gt, 0.0, 1, 0), [i], [o] + also, 0.2 + 2 * i[3] * CYC)

    def iota(o, pat, base, cm=0):
        op("G", lambda: g.iota(o[0], pat, base, cm, allow_small_or_imprecise_dtypes=True), [], [o], 0.13 + 2 * o[3] * CYC)

    def P(o, terms, start=True, stop=True, free=False):
        def run():
            for j, t in enumerate(terms):
                i = pe.matmul((t[2] if len(t) > 2 else o)[0], t[0][0], t[1][0], start and j == 0, stop and j == len(terms) - 1)
            return i
        d = sum(max(64, t[1][3]) * (1 if two(t[1]) else 4) for t in terms) * PCYC
        op("P", run, [x for t in terms for x in t[:2]] + ([tok("open" + o[1])] if free else []), [o] + ([] if free else [tok("open" + o[1])]), d)

    nsem = [0]

    def DMA(q, prs, rd, wr, dur):
        name = "m%d" % nsem[0]
        nsem[0] += 1

        def run():
            for o, i in prs:
                (g.sync if q == "S" else ac).dma_start(o, i).then_inc(T.sem[name], 16)
        op(q, run, rd, wr, dur, (name, 16 * len(prs)))

    def sums(L, b, b0, w):
        return [(R(L, (15 - r, 143 - r)), R(b, (b0 + r, b0 + 16 * w, 16))) for r in range(16)]

    ID, NID, NEG, BIG, BLK, TRS, IDF, BLKF = [R(k) for k in ("ID", "NID", "NEG", "BIG", "BLK", "TRS", "IDF", "BLKF")]
    XC, POS = R("X", (0, 4096)), R("POS")

    DMA("S", [(T.QS[:, :], T.qs[:, :]), (T.WT[:, :], T.wt[:, :]), (T.KI[:, :], T.kk[:, :])], [], [R("QS"), R("WT"), R("KI")], 2.5)
    DMA("AD", [(XC[0], T.x0[:, :])], [], [XC, tok("X0D")], 4.8)
    iota(R("PI", (0, 1)), [[0, 1]], 0, 1)
    iota(R("CI"), [[1, 144]], 0)
    iota(R("CR"), [[0, 15], [1, 16]], 0)
    ts(R("PI", (1, 2)), R("PI", (0, 1)), 112, A.bitwise_and)
    ts(R("PI", (2, 3)), R("PI", (0, 1)), 15, A.bitwise_and)
    cp(R("PF", (0, 3)), R("PI", (0, 3)))
    pcol, gcol, rcol, g15, thr = [R("PF", (i, i + 1)) for i in range(5)]
    ts(g15, gcol, 15.0, A.add)
    cp(R("PF", (5, 6)), R("WT"))
    ts(R("WL"), R("CI"), g15, A.is_equal, R("PF", (5, 6)), A.mult)
    ts(R("OL"), R("CI"), g15, A.is_equal, 1024.0, A.mult)
    ci = R("CI", (0, 128))
    for k, c in ((NID, -1.0), (ID, 1.0), (IDF, 1.0), (NEG, -B24), (BIG, B22), (POS, B24)):
        ts(k, ci, pcol, A.is_equal, c, A.mult)
    ms(R("C2K"), 2048.0)
    ts(BLKF, ci, gcol, A.is_ge)
    ts(BLK, ci, g15, A.is_le)
    tt(BLK, BLK, BLKF, A.mult)
    cp(BLKF, BLK)
    ts(TRS, ci, pcol, A.is_gt)
    tt(TRS, TRS, BLK, A.mult)
    ts(R("MASK"), R("CR"), rcol, A.is_equal)
    ts(R("RST"), R("CR"), 0.0, A.is_gt)
    pen = R("PEN", (96, 144))
    ms(R("PEN", (0, 96)), 0.0)
    ts(pen, R("CR", (0, 48)), rcol, A.is_gt, -64.0, A.mult)
    ts(R("JK", 0, (0, 48)), R("MASK", (0, 48)), -1.5, A.mult)
    tt(pen, pen, R("JK", 0, (0, 48)), A.add)
    P(R("B4", (0, 1)), [(BLK, R("WT"))])
    rs, rb = R("PF", (6, 7)), R("PF", (7, 8))
    if CFG["FL"]:
        ts(thr, R("B4", (0, 1)), 200.0, A.mult)
        op("V", lambda: v.reciprocal(rs[0], thr[0]), [thr], [rs], 0.2)
        ts(rb, rs, 2048.0, A.mult, -1.5, A.add)
    else:
        ts(rb, R("B4", (0, 1)), 300.0, A.mult, -2048.0, A.add)

    def empty(o, U):
        if CFG["FL"]:
            act(o, U, F.Relu, scale=rs, bias=rb)
        else:
            ts(o, U, rb, A.is_gt)
    KK, KC = R("KF", 0), R("KF", 1)
    ts(KK, R("KI"), 1920.5, A.is_gt, -4096.0, A.mult)
    tt(KK, KK, R("KI"), A.add)
    ts(KK, KK, 128.0, A.add)
    ts(R("PI", (4, 8)), R("KI"), 1, A.bitwise_and)
    ts(KC, R("PI", (4, 8)), 2048.0, A.mult, 3 * B22 - 131072.0, A.add)
    iota(R("DUMP"), [[16, 24]], DUMPX)
    ts(R("DUMP"), R("DUMP"), rcol, A.add)
    iota(R("RT"), [[16, 8]], 0)
    ts(R("RT"), R("RT"), rcol, A.add)
    ts(R("SD"), R("RT"), 128.0 - B24, A.add)
    ms(R("GPA"), 0.0)
    if CFG["PAD"]:
        ms(R("r3A", (0, 320)), 0.0)
    if any("Y" in CFG[k] for k in ("L3D", "L3A", "L3D0", "L3A0")):
        ts(R("OL2"), R("CI"), g15, A.is_equal, 2048.0, A.mult)
        ts(R("OLN"), R("CI"), g15, A.is_equal, -1024.0, A.mult)
    ms(R("SND"), 512.0)
    ms(R("X", (4096, XW)), 0.0)
    for a, b, c in ((0, 4, 4), (4, 20, 16), (21, 85, 64)):
        iota(R("cd", (a, b)), [[STR, b - a], [0, NM]], c * STR)
    ms(R("cd", 20), 0.0)
    iota(R("hi"), [[0, 3], [1, NM]], 0)
    for a, b in ((0, 32), (64, 128)):
        ms(R("PLD", (a, b)), 0)
        iota(R("PLA", (a, b)), [[0, (b - a) * STR]], 0)
    for h in "DA":
        iota(R("PT" + h, (32 * STR, 64 * STR)), [[0, 32 * STR]], 0)

    up = {"U2": 0, "t": 80, "up1": 400, "U1": 480, "pre": 500, "U0": 506}

    def chain(h, n, m, U, p, l, pl=None):
        w, t0 = m * n, up["t"]
        r_, v_, s_ = [R(x + h, (0, w)) for x in ("cR", "cv", "cs")]
        z = R("cz" + h, (0, 4 * m), (0, n))
        ts(r_, U, CM, A.add, CM, A.subtract)
        tt(v_, U, r_, A.subtract)
        if w > CFG["SQ"]:
            act(s_, v_, F.Square)
        else:
            tt(s_, v_, v_, A.mult)
        if w <= CFG["TV"]:
            ts(s_, s_, 15.0, A.subtract, 2.0 ** -5, A.mult)
            for a in range(4):
                ts(R("ct" + h, 0, (a, 4 * m, 4), (0, n)), v_, R("KF", 0, (a, a + 1)), A.mult, R("KF", 1, (a, a + 1)), A.add)
            for a in range(4):
                tt(R("cz" + h, (a, 4 * m, 4), (0, n)), R("ct" + h, 0, (a, 4 * m, 4), (0, n)), s_, A.add)
        elif w <= CFG["ONE"]:
            for a in range(4):
                act(R("ct" + h, 0, (a, 4 * m, 4), (0, n)), v_, F.Identity, scale=R("KF", 0, (a, a + 1)), bias=R("KF", 1, (a, a + 1)))
            for a in range(4):
                act(R("ct" + h, 1, (a, 4 * m, 4), (0, n)), s_, F.Identity, scale=2.0 ** -5, bias=-0.46875)
            tt(z, R("ct" + h, 0, (0, 4 * m), (0, n)), R("ct" + h, 1, (0, 4 * m), (0, n)), A.add)
        else:
            for a in range(4):
                act(R("U" + h, (t0 + a * w, t0 + a * w + w)), v_, F.Identity, scale=R("KF", 0, (a, a + 1)), bias=R("KF", 1, (a, a + 1)))
            if w > CFG["S2"]:
                act(s_, s_, F.Identity, scale=2.0 ** -5, bias=-0.46875)
            else:
                ts(s_, s_, 15.0, A.subtract, 2.0 ** -5, A.mult)
            for a in range(4):
                tt(R("cz" + h, (a, 4 * m, 4), (0, n)), R("U" + h, (t0 + a * w, t0 + a * w + w)), s_, A.add)
        if m != 16:
            if CFG["ANDU"] and not pl:
                ts(l, z, 4095, A.bitwise_and)
            ts(p, z, 4095, A.bitwise_and)
            if pl or not CFG["ANDU"]:
                cp(l, pl or p)
            return
        cut = CFG["CUT" + h]
        for a, b in zip(cut, cut[1:]):
            pp, ll = R("PL" + h, (64 + a, 64 + b), (0, n)), R("l3" + h, (a * n, b * n))
            if CFG["ANDU"]:
                ts(ll, R("cz" + h, (a, b), (0, n)), 4095, A.bitwise_and)
            ts(pp, R("cz" + h, (a, b), (0, n)), 4095, A.bitwise_and)
            if not CFG["ANDU"]:
                (gcp if CFG["LG" + h] and a else cp)(ll, pp)

    zb, jb, where = [0], [0], {}

    def search(h, s, o, n):
        Un, Kn, PL = "U" + h, "K" + h, "PL" + h
        tag = h + ("0" if s == 0 else "")
        ns = (0, n)
        phase[0] = "head" + h
        if where.get(h) != o:
            where[h] = o
            for c, base in ((1, QC), (0, SPARE)):
                ts(R(PL, c, (0, min(NM, 8 - o))), R("RT", (o, min(o + NM, 8))), float(base), A.add)

        def QX(a, b):
            if h == "A":
                return R("QXA", (a, b))
            return R("QX0", (a, b)) if s == 0 else R("QXD", s - 1, (a, b))

        def dist(dn, bn, b0, W, l, e):
            d = R(dn, (b0, b0 + W))
            if e == "V":
                gat(d, XC, l, QX(0, W))
                act(R(bn, (b0, b0 + W)), d, F.Abs)
                return
            if e == "Y":
                gat(d, XC, l, QX(0, W))
                ts(R("r3" + h, (b0, b0 + W)), d, 0.0, A.max)
                return
            gat(d, XC, l)
            pc = W // -(-W // 512)
            for x in range(0, W, pc):
                zb[0] ^= 1
                Z = R(("B4", "B5")[zb[0]] if dn == "d12A" else "Z%d" % zb[0], (0, pc))
                P(Z, [(ID, R(dn, (b0 + x, b0 + x + pc))), (NID, QX(x, x + pc))])
                act(R(bn, (b0 + x, b0 + x + pc)), Z, F.Abs)
        p1, p2 = R(PL, (4, 8), ns), R(PL, (16, 32), ns)
        nd = min(n, 5 - o)
        na = n - nd
        if nd:
            gcp(R(PL, (4, 8), (0, nd)), R("p1D", (4 * s, 4 * s + 4), (o, o + nd)))
        if h == "A":
            q, l1, uq = QX(0, 16 * n), R("l1A", (0, 4 * n)), lambda m: R("UQA", (0, m), ns)
            if nd:
                for c in range(2):
                    gcp(QX(16 * n * c, 16 * (n * c + nd)), R("QS", (80 * s + 16 * o, 80 * s + 80)))
                gcp(R("UQA", 0, (0, nd)), R("UQD", 0, (5 * s + o, 5 * s + 5)))
            if na:
                for c in range(2):
                    gcp(QX(16 * (n * c + nd), 16 * n * (c + 1)), R("ARR", s - 1))
                U0 = R(Un, (up["U0"], up["U0"] + na))
                P(U0, [(NID, R("C2K", (0, na)))], True, False)
                P(U0, [(R("WL", (15 - r, 143 - r)), R("ARR", s - 1, (r, C, 16))) for r in range(16)], False, True)
                act(R("UQA", 0, (nd, n)), U0, F.Copy)
                chain(h, na, 1, U0, R(PL, (4, 8), (nd, n)), l1, p1 if nd else None)
                empty(R("htA", (4 * n, 4 * n + na)), U0)
            else:
                cp(l1, p1)
            for w in (32 * n, 64 * n, 128 * n):
                gcp(QX(w, 2 * w), QX(0, w))
            for w in (1, 2, 4, 8):
                gcp(R("UQA", (w, 2 * w), ns), R("UQA", (0, w), ns))
        else:
            q = R("QS", (s * 80, s * 80 + 16 * n))
            l1, uq = R("l1D", (20 * s, 20 * s + 4 * n)), lambda m: R("UQD", (0, m), (5 * s, 5 * s + n))
        gcp(R("X", (QC + 16 * o, QC + 16 * (o + n))), q, [tok("own")])
        gcp(R("RG" + h, (48 * n, 64 * n)), q)
        for a in range(4):
            gcp(R("r1" + h, (a, 16, 4), ns), p1)
        up1, up2 = R(Un, (up["up1"], up["up1"] + 16 * n)), R(Kn, (432, 432 + 16 * n))
        e21, v1, v2, v1r = R("e21" + h, (0, 16 * n)), R("v1" + h, (0, 4 * n)), R("v2" + h, (0, 16 * n)), R("v1r" + h, sl(None), ns)
        U1 = R(Un, (up["U1"], up["U1"] + 4 * n))
        first = []
        for a, b, e in _pieces(CFG["L1" + h]):
            lo = 20 * s if h == "D" else 0
            dist("d12" + h, "b12" + h, 16 * n * a, 16 * n * (b - a), R("l1" + h, (lo + a * n, lo + b * n)), e)
            part = R(Un, (up["U1"] + a * n, up["U1"] + b * n))
            first.append((IDF, uq(b - a), part) if e == "V" else (NID, R("C2K", (0, (b - a) * n)), part))
        P(U1, ([(BIG, R("PEN", (0, 4 * n)))] if len(first) > 1 else []) + first, True, False)
        P(U1, sums("WL", "d12" + h, 0, 4 * n), False, True)
        chain(h, n, 4, U1, p2, R("l2" + h, (0, 16 * n)))
        empty(v1, U1)
        for a in range(4):
            gcp(R("v1r" + h, (a, 16, 4), ns), v1)
        u2, first = up["U2"], []
        for a, b, e in _pieces(CFG["L2" + tag]):
            dist("d12" + h, "b12" + h, 64 * n + 16 * n * a, 16 * n * (b - a), R("l2" + h, (a * n, b * n)), e)
            part = R(Un, (u2 + a * n, u2 + b * n))
            first.append((IDF, uq(b - a), part) if e == "V" else (NID, R("C2K", (0, (b - a) * n)), part))
        if CFG["UP"]:
            act(up1, R("r1" + h, sl(None), ns), F.Copy)
            gcp(R("r2" + h, (0, 16 * n)), p2)
            act(up2, R("r2" + h, (0, 16 * n)), F.Copy)
        else:
            cp(up1, R("r1" + h, sl(None), ns))
            cp(up2, p2)
        tt(e21, p2, up1, A.is_equal)
        U2 = R(Un, (u2, u2 + 16 * n))
        P(U2, [(BIG, e21), (BIG, v1r)] + first, True, False)
        P(U2, sums("WL", "d12" + h, 64 * n, 16 * n), False, True)
        chain(h, n, 16, U2, None, None)
        phase[0] = "keys" + h
        for a, b in ((0, 32), (64, 128)):
            i, d = R(PL, (a, b)), R("PT" + h, (a * STR, b * STR))
            DMA("S", [(d[0], i[0])], [i], [d], 2.5)
        empty(v2, U2)
        for a in range(4):
            gcp(R("v2r" + h, (a, 64, 4), ns), v2)
        for a in range(4):
            blk = R(PL, (64 + a, 128, 4), ns)
            tt(R("e32" + h, (a, 64, 4), ns), blk, up2, A.is_equal)
            tt(R("e31" + h, (a, 64, 4), ns), blk, up1, A.is_equal)
        k2 = R(Kn, (4 * n, 20 * n))
        P(R(Kn, (0, 20 * n)), [(ID, R("cd", (0, 20), ns)), (NEG, e21, k2), (NEG, v1r, k2)] + sums("OL", "b12" + h, 0, 20 * n))
        P(R(Kn, (20 * n, 85 * n)), [(ID, R("cd", (20, 85), ns))], True, False)
        if CFG["FL"]:
            act(R("ht" + h, (0, 4 * n)), R(Kn, (0, 4 * n)), F.Relu, scale=-2.0 ** -9, bias=2.0)
        else:
            ts(R("ht" + h, (0, 4 * n)), R(Kn, (0, 4 * n)), 1024.0, A.is_lt)
        P(R(Kn, (20 * n, 21 * n)), [(POS, R("ht" + h, (a * n, a * n + n))) for a in range(4)] +
          ([(POS, R("htA", (4 * n, 4 * n + na)), R(Kn, (20 * n + nd, 21 * n)))] if na else []), False, False, True)
        for e in ("e32", "e31", "v2r"):
            P(R(Kn, (21 * n, 85 * n))[:2] + (0, 0), [(NEG, R(e + h, sl(None), ns))], False, False, True)
        for _ in range(CFG["PAD"]):
            P(R(Kn, (21 * n, 85 * n))[:2] + (0, 0), [(ID, R("r3A", (0, 64 * n)))] * 4, False, False, True)
        for a, b, e in _pieces(CFG["L3" + tag]):
            dist("d3" + h, "d3" + h, 16 * n * a, 16 * n * (b - a), R("l3" + h, (a * n, b * n)), e)
        c0 = 0
        who = {a: e for a, b, e in _pieces(CFG["L3" + tag])}
        for m in CFG["KEY" + tag]:
            c1 = c0 + m
            if who[c0] == "Y":
                t = sums("OLN", "d3" + h, 16 * n * c0, m * n) + sums("OL2", "r3" + h, 16 * n * c0, m * n)
            else:
                t = sums("OL", "d3" + h, 16 * n * c0, m * n)
            P(R(Kn, ((21 + c0) * n, (21 + c1) * n)), t, False, c1 == 64, c1 < 64)
            c0 = c1

    def tail(h, s, o, n, last):
        w, ns = 48 * n, (0, n)
        phase[0] = "tail" + h
        MI, sc, cc, gm, o16 = R("MI" + h, ns), "sc" + h, "cc" + h, R("gm" + h, (0, w)), R("o16" + h, (0, 3 * n))
        for i in range(n):
            red(R("MI" + h, (i, i + 1)), R("K" + h, (i, 85 * n, n)))
        for k in range(3):
            ts(R(cc, k, ns), MI, 2 * k, A.arith_shift_right, ((128 >> 2 * k) - 1) * STR, A.bitwise_and)
        if last or n < NM:
            for i in range(n):
                ts(R("o16" + h, (i, 3 * n, n)), R(cc, sl(None), i), float(i), A.add)
        else:
            tt(R(cc, sl(None), ns), R(cc, sl(None), ns), R("hi", sl(None), ns), A.add)
            cp(o16, R(cc, sl(None), ns))
        gat(gm, R("PT" + h), o16, R("MASK", (0, w)), A.mult)
        sp = R("B4" if h == "D" else "KA", (0, w))
        P(sp, [(BLKF, gm)])
        cp(R("SP", sl(None), (16 * o, 16 * (o + n))), sp)
        a, b = R(sc, (0, w)), R("RST", (0, w))
        op("V", lambda: v.tensor_tensor_scan(a[0], b[0], gm[0], 0.0, A.mult, A.add), [b, gm], [a], w * CYC)
        rg, win, rl = R("RG" + h, (0, w)), R("X", (0, DUMPX)), R("rl" + h, (0, 3 * n))
        cp(rl, R(sc, (15, w, 16)))
        if o:
            op("A", lambda: ac.activation(rg[0], win[0].indirect(rl[0]), F.Copy), [tok("own"), tok("last"), rl, (None, "either", 0, 0)], [rg], 0.065 + 1.56 * w * CYC, None, "g")
        else:
            gat(rg, win, rl)
        ts(R("ne" + h, ns), MI, THR, A.is_lt, 0.5, A.subtract)
        for i in range(n):
            gi = o + i
            Zn, wo = CFG["FOLD" + h][i], 48 * min(gi, 2)
            Z = R(Zn, (352 - wo, 400))
            P(Z, [(BIG, R("PEN", (96 - wo, 144)))], True, False)
            for b0, b1 in ((0, o), (o, gi + 1)) if o and i < CFG["SPLIT"] else ((0, gi + 1),):
                for k in range(3):
                    x = 16 * (k * n + i) + 15
                    ts(R("EQ" + h, i, k, sl(None), (16 * b0, 16 * b1)), R("SP", sl(None), (16 * b0, 16 * b1)), R(sc, (x, x + 1)), A.is_equal)
                    t = [(BIG, R("EQ" + h, i, k, sl(None), (16 * j, 16 * min(j + 2, b1, gi))), R(Zn, (352 - 48 * (min(j + 2, b1, gi) - j), 352)))
                         for j in range(b0, min(b1, gi), 2)]
                    if b1 > gi:
                        t.append((BIG, R("EQ" + h, i, k, sl(None), (16 * gi, 16 * gi + 16)), R(Zn, (352, 400))))
                    P(Z, t, False, b1 > gi and k == 2)
            if CFG["RED" + h][i] == "V" and gi:
                red(R("res" + h, (i, i + 1)), Z)
            else:
                jb[0] = (jb[0] + 1) % 4
                act(R("JK", jb[0], (0, wo + 48)), Z, F.Relu, accum_out=R("res" + h, (i, i + 1)))
        res = R("res" + h, ns)
        if s < S - 1:
            gone, p4 = R("GP" + h, (8, 8 + n)), R("U" + h, (up["pre"], up["pre"] + n))
            if h == "D" and s < 2:
                ms(R("GPD"), 0.0)
            tt(gone, res, R("ne" + h, ns), A.is_lt)
            if o:
                P(p4, [(BLK, R("GPD", (x, x + n))) for x in range(9 - n, 8 + o)], True, False)
            P(p4, [(TRS, gone), (NEG, gone)] + [(BLK, R("GP" + h, (8 - x, 8 + n - x))) for x in range(1, n)], not o, True)
            if last:
                for i in range(n):
                    x = up["pre"] + i
                    ts(R("s16" + h, (i, i + 1)), R("U" + h, (x, x + 1)), R("SD", (o + i, o + i + 1)), A.min, B24, A.add)
            else:
                tt(R("ds" + h, ns), p4, R("SD", (o, o + n)), A.min)
                ts(R("s16" + h, ns), R("ds" + h, ns), B24, A.add)
            scat(R("SND"), R("s16" + h, ns), R("RG" + h, (0, 16 * n)), "last" if last and CFG["SF"] else None)
        if last and CFG["W1"]:
            for x in range(3 * n):
                ts(R("w16" + h, (x, x + 1)), R(sc, (16 * x + 15, 16 * x + 16)), R("res" + h, (x % n, x % n + 1)), A.add, R("DUMP", (3 * o + x, 3 * o + x + 1)), A.min)
            return
        for k in range(3):
            tt(R("wm" + h, k, ns), R(sc, (16 * k * n + 15, 16 * (k + 1) * n, 16)), res, A.add)
        wm = R("wm" + h, sl(None), ns)
        tt(wm, wm, R("DUMP", (3 * o, 3 * (o + n))), A.min)
        cp(R("w16" + h, (0, 3 * n)), wm)

    n0, nd = CFG["ND0"], CFG["ND"]
    U0 = R("UD", (0, 30))
    P(U0, [(NID, R("C2K", (0, 30)))] + sums("WL", "QS", 0, 30))
    act(R("UQD", 0), U0, F.Copy)
    chain("D", 5, 6, U0, R("p1D"), R("l1D", (0, 4 * n0)), R("p1D", (0, 4), (0, n0)))
    for s in range(1, S):
        cp(R("l1D", (20 * s, 20 * s + 4 * nd)), R("p1D", (4 * s, 4 * s + 4), (0, nd)))
    for w in (1, 2, 4, 8):
        gcp(R("UQD", (w, 2 * w)), R("UQD", (0, w)))
    cp(R("QX0", (0, 16 * n0)), R("QS", (0, 16 * n0)))
    for w in (16 * n0, 32 * n0, 64 * n0, 128 * n0):
        cp(R("QX0", (w, 2 * w)), R("QX0", (0, w)))
    DMA("S", [(T.QXD[:, s - 1, 0:16 * nd], T.QS[:, 80 * s:80 * s + 16 * nd]) for s in range(1, S)], [R("QS"), tok("X0D")], [R("QXD", sl(None), (0, 16 * nd))], 2.5)
    for w in (16 * nd, 32 * nd, 64 * nd, 128 * nd):
        DMA("S", [(T.QXD[:, :, w:2 * w], T.QXD[:, :, 0:w])], [R("QXD", sl(None), (0, w))], [R("QXD", sl(None), (w, 2 * w))], 2.5)
    nxt = T.cores[(rank + 1) % len(T.cores)]
    rid, pid = topo.addr(nxt)[:2]
    msk, neng = topo.mask(core, nxt), len(topo.engines(core, nxt))
    snd = R("SND", (0, C))
    for s in range(S):
        halves = [("D", 0, nd), ("A", nd, 8 - nd)] if s else [("D", 0, n0), ("A", n0, 5 - n0)][:1 + (n0 < 5)]
        seen.clear()
        if 0 < s < S - 1:
            op("G", lambda: g.iota(snd[0], [[0, C]], 512, 0, allow_small_or_imprecise_dtypes=True), [tok("snt%d" % s)], [snd], 0.25)
        for h, o, n in halves:
            search(h, s, o, n)
        for h, o, n in halves:
            last = h == halves[-1][0]
            tail(h, s, o, n, last)
            if last and s < S - 1:
                op("G", (lambda s=s: g.remote_dma(T.ARR[:, s, :], snd[0], T.sem["arr%d" % (s + 1)], T.sem["snt%d" % (s + 1)], pid, rid, msk)),
                   [snd], [], 0.5, ("none", 0))
                op("N", None, [snd], [R("ARR", s)], 3.5, ("arr%d" % (s + 1), neng))
                op("N", None, [snd], [tok("snt%d" % (s + 1))], 2.5, ("snt%d" % (s + 1), neng))
            scat(R("X"), R("w16" + h, (0, 3 * n)), R("RG" + h, (16 * n, 64 * n)), "last" if last else "either")
    DMA("S", [(T.y[:, 0:2048], T.X[:, 0:2048])], [R("X", (0, 2048))], [tok("y1")], 4.0)
    DMA("AD", [(T.y[:, 2048:4096], T.X[:, 2048:4096])], [R("X", (2048, 4096))], [tok("y2")], 4.0)

    eng = {"V": v, "A": ac, "P": pe, "G": g, "S": g.sync, "AD": ac}
    N = len(ops)
    if "o" not in ORDER:
        ORDER["o"], ORDER["d"], ORDER["fin"] = _schedule(ops, kind)
        ORDER["ops"] = ops
    deps = ORDER["d"]
    cnt = {"V": 0, "A": 0, "P": 0, "G": 0}
    val, snap = [None] * N, [{} for _ in range(N)]
    know = {q: {} for q in "VAPGS"}
    for i in ORDER["o"]:
        q, fn, rd, wr, du, own, cat = ops[i]
        p = PHYS[q]
        if p == "N":
            val[i] = own
            continue
        kn, want = know[p], {}
        for j, need in deps[i].items():
            sem, c = val[j]
            if need and kn.get(sem, 0) < c:
                want[sem] = max(want.get(sem, (0, 0)), (c, j))
        for sem in sorted(want, key=lambda k: -want[k][1]):
            c, j = want[sem]
            if kn.get(sem, 0) < c:
                eng[q].wait_ge(T.sem[sem], c)
                for k2, c2 in snap[j].items():
                    kn[k2] = max(kn.get(k2, 0), c2)
                kn[sem] = c
        r = fn()
        if own is None:
            cnt[p] += 1
            r.then_inc(T.sem["c" + p], 1)
            val[i] = ("c" + p, cnt[p])
        else:
            val[i] = own
        snap[i] = dict(kn)
    for p in "VAPG":
        g.wait_ge(T.sem["c" + p], cnt[p])
    for i in range(N):
        if ops[i][0] in ("S", "AD"):
            g.wait_ge(T.sem[val[i][0]], val[i][1])
    for s in range(1, S):
        g.wait_ge(T.sem["snt%d" % s], neng)
        g.wait_ge(T.sem["arr%d" % s], neng)
